import numpy as np, ml_dtypes
CORES = [5,29,101,125,133,157,229,253]
N = 8
BF = ml_dtypes.bfloat16
def gentries(a):
    return np.ascontiguousarray(a.reshape(8, 16, -1).transpose(0, 2, 1)).reshape(8, -1)
def gtable(e):
    e = np.asarray(e); return np.ascontiguousarray(e.reshape(8, -1, 16).transpose(0, 2, 1)).reshape(128, -1).astype(np.int32)
VA, G, OB, W, CAP, S = 640, 384, 1280, 2560, 240, 176
E0, M, RO = 3, 14, 5
WA, NIL = VA + G, W - 1
H = NIL - OB
KC = 6
def within(rng, ke, k):
    o = np.argsort(ke, kind="stable"); cnt = np.bincount(ke, minlength=KC); lo = np.add.accumulate(cnt) - cnt
    i = lo[k] + (rng.random(k.shape) * np.maximum(cnt[k], 1)).astype(np.int64)
    return o[np.minimum(i, ke.size - 1)]
def feat(rng, cen, k, a):
    v = np.swapaxes(cen[np.arange(8)[None, :, None], k], 2, 3)
    return v + rng.integers(-a, a + 1, v.shape)
def parts(rng, bd=None):
    if bd is None: bd = np.argsort(rng.random((N, 8, VA)), axis=-1)[..., :G]
    cen = rng.integers(-90, 91, (8, KC, 16)); ka = rng.integers(0, KC, (N, 8, VA)); kb = rng.integers(0, KC, (N, 8, OB))
    kx = np.concatenate([ka, np.take_along_axis(np.roll(ka, 1, axis=0), np.roll(bd, 1, axis=0), 2)], axis=2)
    eo = np.argsort(kx[:, :, None, :] + 1.5 * rng.random((N, 8, 16, WA)), axis=-1); ao = np.argsort(ka[:, :, None, :] + 1.5 * rng.random((N, 8, 16, VA)), axis=-1)
    nba = np.empty((N, 8, 16, VA), np.int64); np.put_along_axis(nba, ao, eo[..., np.arange(VA) * WA // VA], -1)
    ky = np.concatenate([kb, np.roll(kb, -1, axis=0)[..., :H]], axis=2); nbb = np.empty((N, 8, 16, OB), np.int64); f0 = np.empty((N, 8, 16, S), np.int64)
    dens = rng.choice(np.array([0.3, 0.5, 0.8]), (N, 8))
    for r in range(N):
        for g in range(8):
            k = np.where(rng.random((16, OB)) < 0.75, kb[r, g], rng.integers(0, KC, (16, OB)))
            nbb[r, g] = np.where(rng.random((16, OB)) < 0.04, NIL, within(rng, ky[r, g], k))
            keep = (rng.random((16, S)) < dens[r, g]) & (rng.random((1, S)) > 0.1)
            f0[r, g] = np.where(keep, within(rng, ky[r, g], np.broadcast_to(ka[r, g, :S], (16, S))), NIL)
    return dict(cen=cen, ka=ka, kb=kb, bd=bd, nba=nba, nbb=nbb, f0=f0, xa=feat(rng, cen, ka, 3), xb=feat(rng, cen, kb, 3))
def pack(d):
    t = lambda v, w: np.ascontiguousarray(np.reshape(v, (N, 128, w)))
    return {"xa": t(d["xa"], VA).astype(np.float32).astype(BF), "xb": t(d["xb"], OB).astype(np.float32).astype(BF), "nba": t(d["nba"], VA).astype(np.int32),
            "nbb": t(d["nbb"], OB).astype(np.int32), "f0": t(d["f0"], S).astype(np.int32), "bd": np.stack([gtable(a) for a in d["bd"]])}
def put(row, c, v):
    o = np.setdiff1d(np.arange(row.size), c); hit = o[np.isin(row[o], v)]
    row[hit] = np.setdiff1d(row[c], v)[:hit.size]; row[c] = v
def short(rng, d, r, g):
    z1, z2, x = S, S + 1, VA - 1; P = np.array([S // 4, S // 2, 3 * S // 4, VA - 4, VA - 3, VA - 2])
    T = rng.permutation(np.setdiff1d(np.arange(S), P[:3])); D1, D2 = int(T[0]), int(T[1]); T = T[2:]
    f = d["f0"][r, g]; f[:] = rng.integers(0, NIL, f.shape); f[:, P[:3]] = NIL; f[:15, D1] = NIL; f[:15, D2] = NIL
    m = np.concatenate([P[:3], np.arange(S + 2, VA)])
    for p in range(16):
        c, v = [z1, z2], [D1, D2]
        if p == 0: c, v = [z1, z2, x], [x, z1, int(T[0])]
        elif p == 1: v = [z2, D2]
        elif p == 2: c, v = [z1, z2, x], [D1, D2, z1]
        elif p < 9: c, v = [z1, z2, int(P[p - 3])], [D1, D2, z2]
        elif p < 15:
            i = m[(p - 9) * T.size:(p - 8) * T.size]; c, v = np.concatenate([c, i]), np.concatenate([v, T[:i.size]])
        else: v = [z1, z2]
        put(d["nba"][r, g, p], np.array(c, np.int64), np.array(v, np.int64))
def lone(rng, d, r, g, z0, L):
    c, u, w = OB - 1, VA - 1, S
    f = d["f0"][r, g]; nb = d["nba"][r, g]; v = rng.integers(0, NIL - 1, S)
    f[:] = NIL; f[rng.integers(0, 16, S), np.arange(S)] = v + (v >= c); f[:, 64 + rng.permutation(S - 64)[:z0]] = NIL
    f[:, 0] = NIL; f[0, 0] = NIL - 1; f[1:3, 1] = c
    cells = [0, u, w] if L == 0 else [u, u - 1] + [S + i for i in range(L)]
    d["xa"][r, g][:, cells] = 40; d["xb"][r, g][:, c] = 40; d["nbb"][r, g][:, c] = c
    for p in range(16):
        if L == 0:
            to = {u: p}
            if p == 1: to[w] = u
            if p == 2: to[0] = 1
            if p == 3: to[0] = w
        else:
            to = {u: 1 if p == 1 else S, u - 1: S if p == 1 else (1 if p == 2 else p)}
            for i in range(1, L + 1): to[S + i - 1] = u if p == 4 + i else (S + i if p == 3 and i < L else 16 * i + p)
        k = sorted(to); put(nb[p], np.array(k, np.int64), np.array([to[i] for i in k], np.int64))
def quiet(rng, d, r):
    for g in range(8):
        o = rng.permutation(min(S, CAP)); x, y = int(o[0]), int(o[1]); z = int(rng.integers(2 * CAP + 1, VA)); c = int(rng.integers(0, OB))
        d["f0"][r, g] = NIL; d["f0"][r, g][:, y] = c
        for p in range(16):
            d["nba"][r, g, p] = rng.permutation(VA)
            if p == 0: k, v = [x, y], [y, x]
            else: k, v = [x, z, y], [x, y, z]
            put(d["nba"][r, g, p], np.array(k, np.int64), np.array(v, np.int64))
        b = d["xb"][r, g][:, c]; d["xa"][r, g][:, x] = b + (E0 if g < 7 else E0 + 1); d["xa"][r, g][:, z] = b - (E0 + 1)
def setup_inputs(rng):
    return pack(parts(rng))
def setup_inputs_room(rng):
    d = parts(rng); d["xa"] = feat(rng, d["cen"], d["ka"], 1); d["xb"] = feat(rng, d["cen"], d["kb"], 1); z0 = (S - VA) % CAP
    d["xa"][:, ::2, M - 1:] = 127; d["xb"][:, ::2, M - 1:] = -127; d["xa"][:, 1::2, M:] = 127; d["xb"][:, 1::2, M:] = -127
    d["xa"][:, 1::4, :M] = rng.integers(-1, 2, (N, 2, M, VA)); d["xb"][:, 1::4, :M] = rng.integers(-1, 2, (N, 2, M, OB))
    for r in range(N):
        for g in (0, 4):
            z = z0 + (0, 1, -1)[(r + g // 2) % 3]; o = rng.permutation(S)
            d["f0"][r, g][:, o[:z]] = NIL; d["f0"][r, g, rng.integers(0, 16, S - z), o[z:]] = rng.integers(0, NIL, S - z)
        lone(rng, d, r, 2, z0, 0); lone(rng, d, r, 6, z0, RO - (VA - S + z0) // CAP)
        for g in (1, 5): short(rng, d, r, g)
    return pack(d)
def setup_inputs_ties(rng):
    d = parts(rng); d["xb"] = feat(rng, d["cen"], d["kb"], 0); v = feat(rng, d["cen"], d["ka"], 0)
    d["xa"] = v + rng.choice(np.array([0, E0, E0 + 1, E0 + 2]), v.shape, p=[0.3, 0.55, 0.12, 0.03]) * rng.choice(np.array([-1, 1]), v.shape)
    d["f0"][:, ::2] = d["f0"][:, ::2, :1].copy(); d["nbb"][:, 1::2] = d["nbb"][:, 1::2, 5:6].copy(); d["nbb"][:, 0, 15] = np.arange(OB)
    quiet(rng, d, 0)
    return pack(d)
def setup_inputs_ends(rng):
    o = 1 + np.argsort(rng.random((N, 8, VA - 2)), axis=-1)[..., :G - 2]; z = np.zeros((N, 8, 1), np.int64)
    d = parts(rng, np.concatenate([z, o, z + VA - 1], axis=2)); ends = np.array([0, H - 1, H, OB - 1, OB, W - 2, NIL])
    d["cen"][::2] = d["cen"][::2, :1].copy(); d["cen"][4] = 125; d["cen"][6] = -125
    d["xa"] = feat(rng, d["cen"], d["ka"], 2); d["xb"] = feat(rng, d["cen"], d["kb"], 2)
    d["f0"] = np.where(rng.random(d["f0"].shape) < 0.5, rng.choice(ends, d["f0"].shape), d["f0"])
    e = d["nbb"][:, ::2]; d["nbb"][:, ::2] = np.where(rng.random(e.shape) < 0.5, rng.choice(ends, e.shape), e)
    d["nbb"][:, 5] = NIL; d["f0"][0, 7] = NIL; d["nba"][:, 2, 0] = np.arange(VA); d["nba"][:, 2, 1] = WA - 1 - np.arange(VA)
    return pack(d)
def setup_inputs_cross(rng):
    h = min(S, G) // 2; a = np.argsort(rng.random((N, 8, S)), axis=-1)[..., :h]; b = S + np.argsort(rng.random((N, 8, VA - S)), axis=-1)[..., :G - h]
    bd = np.concatenate([a, b], axis=2); bd = np.take_along_axis(bd, np.argsort(rng.random(bd.shape), axis=-1), 2); d = parts(rng, bd)
    noise = np.full((1, 8, 1, 1), 3); noise[:, :2] = 1; d["xa"] = feat(rng, d["cen"], d["ka"], noise); d["xb"] = feat(rng, d["cen"], d["kb"], noise)
    for r in range(N):
        for g in range(8):
            far = OB + within(rng, d["kb"][(r + 1) % N, g, :H], np.broadcast_to(d["ka"][r, g, :S], (16, S))); f = d["f0"][r, g]
            d["f0"][r, g] = np.where((f != NIL) & (rng.random(f.shape) < 0.8), far, f)
    d["f0"][1::2, :4] = NIL; lo = np.arange(VA) < CAP
    for r in range(1, N, 2):
        for g in (0, 1):
            for p in range(16):
                row = d["nba"][r, g, p]; gh = row >= VA
                i = np.flatnonzero(gh & (lo == (g == 0))); j = np.flatnonzero(~gh & (lo == (g == 1))); k = min(i.size, j.size); i = i[:k]; j = j[:k]
                vi = row[i].copy(); row[i] = row[j]; row[j] = vi
    return pack(d)
def setup_inputs_spread(rng):
    d = parts(rng); cen = rng.integers(-127, 128, (8, KC, 16))
    for x, k, n in (("xa", d["ka"], VA), ("xb", d["kb"], OB)):
        v = np.clip(feat(rng, cen, k, rng.choice(np.array([0, 1, 2, 2, 3, 3, 5, 12]), (N, 8, 1, n))), -127, 127)
        v = np.where(rng.random((N, 8, 1, n)) < 0.125, rng.integers(-127, 128, v.shape), v)
        d[x] = v * (rng.random((N, 8, 1, n)) > 0.0625)
    d["nba"][:, :, 4:8] = np.argsort(rng.random((N, 8, 4, WA)), axis=-1)[..., :VA]
    d["nbb"] = np.where(rng.random(d["nbb"].shape) < 0.3, rng.integers(0, W, d["nbb"].shape), d["nbb"])
    return pack(d)
def check_inputs(d):
    bad = []
    for k, hi in (("nba", WA - 1), ("nbb", NIL), ("f0", NIL), ("bd", VA - 1)):
        if np.min(d[k]) < 0 or np.max(d[k]) > hi: bad.append("range of " + k)
    for k in ("xa", "xb"):
        v = d[k].astype(np.float32)
        if not np.all((v >= -127) & (v <= 127) & (np.rint(v) == v)): bad.append("whole numbers of " + k)
    s = np.sort(d["nba"], axis=2)
    if np.any(s[..., 1:] == s[..., :-1]): bad.append("repeated in a row of nba")
    s = np.sort(np.stack([gentries(a) for a in d["bd"]]), axis=2)
    if np.any(s[..., 1:] == s[..., :-1]): bad.append("repeated in bd")
    return bad
def reference(xa, xb, nba, nbb, f0, bd):
    A = xa.astype(np.float32).astype(np.int32).reshape(N, 8, 16, VA); own = xb.astype(np.float32).astype(np.int32).reshape(N, 8, 16, OB)
    na = nba.astype(np.int64).reshape(N, 8, 16, VA); no = nbb.astype(np.int64).reshape(N, 8, 16, OB); bl = np.stack([gentries(a) for a in bd]).astype(np.int64)
    B = np.zeros((N, 8, 16, W), np.int32); NB = np.full((N, 8, 16, W), NIL, np.int64)
    for r in range(N):
        q = (r + 1) % N; n = no[q, :, :, :H]
        B[r, :, :, :OB] = own[r]; B[r, :, :, OB:NIL] = own[q, :, :, :H]
        NB[r, :, :, :OB] = no[r]; NB[r, :, :, OB:NIL] = np.where(n < H, OB + n, NIL)
    F = np.full((N, 8, 16, VA), NIL, np.int64); F[..., :S] = f0.reshape(N, 8, 16, S)
    flag = np.ones((N, 8, VA), bool); e = [E0] * N; rows = np.arange(16)[:, None]
    for wave in range(RO):
        ext = []
        for r in range(N):
            q = (r - 1) % N; n = np.take_along_axis(F[q], bl[q][:, None, :], 2)
            ext.append(np.concatenate([F[r], np.where((n >= OB) & (n < NIL), n - OB, NIL)], axis=2))
        for r in range(N):
            good = 0
            for g in range(8):
                a = np.flatnonzero(flag[r, g] & np.all(F[r, g] == NIL, axis=0))[:CAP]
                x = A[r, g][:, a]; c = ext[r][g][rows, na[r, g][:, a]]; col = np.arange(a.size)
                new = np.full(c.shape, NIL, np.int64)
                for t in range(3):
                    near = (np.abs(B[r, g][:, c] - x[:, None, :]) <= e[r]).astype(np.int32)
                    v = (c != NIL) & (np.add.reduce(near, axis=0) >= M); new = np.where(v, c, new); some = np.any(v, axis=0)
                    if t == 0:
                        ok = some; b = np.where(ok, c[np.argmax(v, axis=0), col], NIL)
                    else:
                        b = np.where(some, c[15 - np.argmax(v[::-1], axis=0), col], b)
                    c = NB[r, g][:, b]
                s = a[ok]; b = b[ok]; F[r, g][:, s] = new[:, ok]
                A[r, g][:, s] = x[:, ok] + np.clip(B[r, g][:, b] - x[:, ok], -2, 2)
                flag[r, g, a] = False
                w = na[r, g][:, s].reshape(-1); flag[r, g, w[w < VA]] = True
                good += int(s.size)
            e[r] = E0 + (good & 1)
    return {"yf": F.reshape(N, 128, VA).astype(np.float32), "ya": A.reshape(N, 128, VA).astype(np.float32).astype(BF)}

@@ -1,0 +1,534 @@
+from concourse.mybir import AluOpType as O, ActivationFunctionType as F
+
+VA, GH, OB, CAP, S0, RO = 640, 384, 1280, 240, 176, 5
+OFF, NULLC, ZC = 9, 2568, 1288
+EXT = OFF + OB
+WB = 2576
+WE = 1264
+NB_HALF = 640
+CH = ((0, 96), (96, 64), (160, 80))
+S_ACT = (1,)
+
+SCRATCH = {}
+_L = {
+    "bfloat16": "ZB:2576 XA:1264 EM:1264 FLB:640 MB:176 ONB:128 BD:128 BDT:128 ID:128 SLM:128 SUM:128 LU:128 FU:128 IDH:128 IDB:128 "
+                "SLN:128 TRIX:128 BDN:128 BDM:128 GS:2048 EB:2048 HB:512 DJ:240 EL:40 XD:240 XC:240 XN:240 RX:640 "
+                "XR0:3840 XR1:3840 XF0:240 XF1:240 NO0:240 NO1:240 D:3840 SQ:3840 NR:3840 SG:240 NN:240",
+    "float16": "LWH:240 BDH:128 SELH:8 Y:384 EH:2048 HS:512 TT:256 TTT:256 NFH0:240 NFH1:240 ST:3840 SP:240",
+    "float32": "NB:2576 FX:1264 FL:1264 LW:1280 MF:176 FA:176 EF:2048 O16:128 COL:8 JR:240 MQ:128 MASK:128 BF:48 BM:48 BS:16 "
+               "DUMROW:240 IOTAF:640 DUMA0:40 DUMPA:40 C20:240 ZROW:240 ONE40:40 CUM:40 PO1:40 PO2:40 THR:8 NFAIL:16 "
+               "YM:640 Y1:640 YO:640 SF:3840 Z:240 OK:240 NW:240 NX:240",
+    "int32": "NBB:1280 NBA:1264 F0I:176 BDI:24 ICOL:4 KI:240 NI:240",
+    "uint16": "NBX:1280 LN:1280 BDU:24 POU:40 FT:256 BW2:16 RN:640 GHS:1920 RG:1920 LG:1920 NFU0:240 NFU1:240 AW0:16 AW1:16 "
+              "LU0:240 LU1:240 OFS:240 OBW:48",
+}
+for _d in _L:
+    for _x in _L[_d].split():
+        SCRATCH[_x.split(":")[0]] = ("sbuf", [128, int(_x.split(":")[1])], _d)
+for _i in range(7):
+    SCRATCH["ps%d" % _i] = ("psum", [128, 512], "float32")
+
+LOADS = ["xb", "f0", "bd", "nba", "xa", "nbb"]
+SEMAPHORES = ["sV", "sA", "sP", "sG", "ls", "oy", "ox", "rx", "rn", "ax0", "ax1", "an0", "an1"] + \
+    ["l" + n for n in LOADS] + ["rg%d" % w for w in range(RO)] + ["ag%d" % w for w in range(RO)]
+
+
+def relays(topo, src, dst):
+    c = [x for x in topo.cores_of(src) if x != src and topo.may_write(x, dst)]
+    return sorted(c, key=lambda x: (topo.die(x) != topo.die(src), x))
+
+
+def messages(topo, cores):
+    n, out = len(cores), []
+    for r in range(n):
+        src, prev, nxt = cores[r], cores[(r - 1) % n], cores[(r + 1) % n]
+        rb = relays(topo, src, prev)
+        w = (NB_HALF, OB - 1 - NB_HALF)
+        for i in range(2):
+            a, b = i * NB_HALF, i * NB_HALF + w[i]
+            out.append((src, rb[i], prev, "RX", (0, w[i]), "rx", "ZB", (EXT + a, EXT + b), "ax%d" % i, "ZB", (OFF + a, OFF + b)))
+        for i in range(2):
+            a, b = i * NB_HALF, i * NB_HALF + w[i]
+            out.append((src, rb[2 + i], prev, "RN", (0, w[i]), "rn", "LN", (a, b), "an%d" % i, "NBX", (a, b)))
+        rg = relays(topo, src, nxt)
+        for k in range(RO):
+            s = (k * GH, (k + 1) * GH)
+            out.append((src, rg[0], nxt, "RG", s, "rg%d" % k, "LG", s, "ag%d" % k, "GHS", s))
+    return out
+
+
+def send(g, topo, src, dst, dbuf, dcol, sbuf, scol, T, rsem):
+    rid, pid = topo.addr(dst, src)
+    g.remote_dma(T[dbuf][:, dcol[0]:dcol[1]], T[sbuf][:, scol[0]:scol[1]], T.sem[rsem], T.sem["ls"], pid, rid, topo.mask(src, dst))
+    return len(topo.engines(src, dst))
+
+
+def relay_program(g, core, T, topo, msgs):
+    total = 0
+    for m in msgs:
+        if m[1] == core:
+            g.wait_ge(T.sem[m[5]], len(topo.engines(m[0], core)))
+            total += send(g, topo, core, m[2], m[6], m[7], m[3], m[4], T, m[8])
+    if total:
+        g.wait_ge(T.sem["ls"], total)
+
+
+CY = 0.00083 * 1.25
+GA, SCA = 1.5, 3.6
+
+
+def build(g, core, T, topo, msgs):
+    tasks, lastw, readers = [], {}, {}
+    V, A, P, SY = g.vector, g.scalar, g.tensor, g.sync
+    COL = {x: T.COL[:, i:i + 1] for i, x in enumerate(("PF", "BIASL", "BIASF", "M0", "M1", "C0", "C2", "C02"))}
+    ICOL = {x: T.ICOL[:, i:i + 1] for i, x in enumerate(("PI", "PJ", "EI", "EJ"))}
+
+    def tk(q, dur, rd, wr, fn, sem=None, val=0):
+        deps = {}
+        i = len(tasks)
+        for b in rd:
+            if b in lastw:
+                deps[lastw[b]] = True
+        for b in wr:
+            if b in lastw:
+                deps[lastw[b]] = True
+            for x in readers.get(b, []):
+                deps.setdefault(x, False)
+        for b in rd:
+            if b not in wr:
+                readers.setdefault(b, []).append(i)
+        for b in wr:
+            lastw[b] = i
+            readers[b] = []
+        tag = "".join(x for x in wr[0] if x.isalpha()) + (q or "")
+        tasks.append(dict(q=q, dur=dur, deps=deps, fn=fn, sem=sem, val=val, tag=tag))
+
+    def cost(n, c):
+        return 0.06 + max(64, n * c) * CY
+
+    def vts(out, in0, s1, s2, o0, o1, rd, wr, n, c=1.0):
+        if o1 is None:
+            tk("V", cost(n, c), rd, wr, lambda: V.tensor_scalar(out, in0, s1, None, op0=o0))
+        else:
+            tk("V", cost(n, c), rd, wr, lambda: V.tensor_scalar(out, in0, s1, s2, op0=o0, op1=o1))
+
+    def vtt(out, a, b, op, rd, wr, n, c=2.0):
+        tk("V", cost(n, c), rd, wr, lambda: V.tensor_tensor(out, a, b, op))
+
+    def vcp(out, in_, rd, wr, n, c=1.0):
+        tk("V", cost(n, c), rd, wr, lambda: V.tensor_copy(out, in_))
+
+    def vms(ap, x, wr, n, c=1.0):
+        tk("V", cost(n, c), [], wr, lambda: V.memset(ap, x))
+
+    def act(out, in_, fn, rd, wr, n, c=1.0, **kw):
+        tk("A", 0.07 + n * c * CY, rd, wr, lambda: A.activation(out, in_, fn, **kw))
+
+    def mm(lst, rd, wr, cyc):
+        def fn():
+            x = None
+            for o, l, r, a, b in lst:
+                x = P.matmul(o, l, r, a, b)
+            return x
+        tk("P", 0.05 + cyc * 0.00075, rd, wr, fn)
+
+    def iota(out, pat, base, wr, n, rd=()):
+        tk("G", 0.13 + 2 * n * CY, list(rd), wr, lambda: g.iota(out, pat, base, 0, allow_small_or_imprecise_dtypes=True))
+
+    def asel(out, in_, pat, op, base, cm, rd, wr, n):
+        tk("G", 0.17 + 2 * n * CY, rd, wr, lambda: g.affine_select(out, in_, pat, op, 0.0, base, cm))
+
+    def ch(name, k, w=1):
+        return T[name][:, w * CH[k][0]:w * (CH[k][0] + CH[k][1])]
+
+    def by(name, k, q):
+        return T[name][:, 16 * CH[k][0] + q:16 * (CH[k][0] + CH[k][1]):16]
+
+    def load(q, name, out, wr, rd):
+        e = SY if q == "S" else A
+        tk(q, 0.1, rd, wr, lambda: e.dma_start(out, T[name][:]), sem="l" + name, val=16)
+
+    vms(T.ZB[:, 0:OFF], 1000.0, ["ZBf"], OFF)
+    vms(T.ZB[:, NULLC:WB], 1000.0, ["ZBg"], 8)
+    load("S", "f0", T.F0I[:], ["F0I"], [])
+    load("A", "xb", T.ZB[:, OFF:EXT], ["ZBo"], ["ZBf"])
+    load("S", "bd", T.BDI[:], ["BDI"], [])
+    load("S", "nba", T.NBA[:, 0:VA], ["NBA"], [])
+    load("A", "xa", T.XA[:, 0:VA], ["XA"], [])
+    load("S", "nbb", T.NBB[:], ["NBB"], [])
+
+    mine = [m for m in msgs if m[0] == core]
+    inb = {m[8]: m for m in msgs if m[2] == core}
+    sent = [0]
+
+    def remote(m, rd):
+        def fn():
+            sent[0] += send(g, topo, core, m[1], m[3], m[4], m[9], m[10], T, m[5])
+        tk("G", 0.6, rd, ["snt" + m[8]], fn, sem="none")
+
+    def arrive(sem, wr, delay):
+        m = inb[sem]
+        tk(None, delay, ["snt" + sem], wr, None, sem=sem, val=len(topo.engines(m[1], core)))
+
+    for m in mine[0:2]:
+        remote(m, ["ZBo"])
+
+    vms(T.ONB[:], 1.0, ["ONB"], 128, .5)
+    asel(T.BDT[:], T.ONB[:], [[-16, 8], [0, 16]], O.is_ge, 0, 1, ["ONB"], ["BDT"], 128)
+    asel(T.BD[:], T.BDT[:], [[16, 8], [0, 16]], O.is_ge, 15, -1, ["BDT"], ["BD"], 128)
+    asel(T.ID[:], T.ONB[:], [[-1, 128]], O.is_equal, 0, 1, ["ONB"], ["ID"], 128)
+    tk("G", 0.15, [], ["PI"], lambda: g.iota(ICOL["PI"], [[0, 1]], 0, 1))
+    iota(T.IOTAF[:], [[1, VA]], 0, ["IOTAF"], VA, ["BD"])
+    iota(T.DUMROW[:], [[1, CAP]], 1024, ["DUMROW"], CAP)
+    iota(T.DUMA0[:], [[16, 40]], VA, ["DUMA0"], 40)
+    iota(T.MQ[:], [[0, 8], [1, 16]], 0, ["MQ"], 128)
+    asel(T.SLM[:], T.BD[:], [[-1, 128]], O.is_gt, 0, 1, ["BD"], ["SLM"], 128)
+    asel(T.SUM[:], T.BD[:], [[1, 128]], O.is_gt, 0, -1, ["BD"], ["SUM"], 128)
+    iota(T.JR[:], [[1, CAP]], 0, ["JR"], CAP)
+    for ap, x, n, b in ((T.GS[:, 0:1024], 0, 1024, "GS"), (T.GS[:, 1024:2048], 0, 1024, "GSz"), (T.XA[:, VA:WE], 0, WE - VA, "XAd"), (T.ZROW[:], 0, CAP, "ZROW"),
+                        (T.FL[:], 1, WE, "FL"), (T.C20[:], 20, CAP, "C20"), (T.HB[:], 0, 512, "HB")):
+        iota(ap, [[0, n]], x, [b], n)
+    tk("G", 0.13 + 2 * (WE - VA) * CY, [], ["NBAd"], lambda: g.iota(T.NBA[:, VA:WE], [[0, WE - VA]], 1024, 0))
+
+    vms(T.FX[:, S0:VA], 0.0, ["FX"], VA - S0)
+    vms(T.FX[:, VA + GH:WE], 0.0, ["FX"], CAP)
+    vts(T.MF[:], T.F0I[:], 2559, None, O.is_lt, None, ["F0I"], ["MF"], S0)
+    vts(T.FA[:], T.F0I[:], OFF, None, O.add, None, ["F0I"], ["FA"], S0)
+    vtt(T.FX[:, 0:S0], T.FA[:], T.MF[:], O.mult, ["FA", "MF"], ["FX"], S0)
+    vcp(T.BDU[:], T.BDI[:], ["BDI"], ["BDU"], 24)
+    vcp(T.MB[:], T.MF[:], ["MF"], ["MB"], S0)
+    vms(T.EM[:], 1.0, ["EM"], WE, .5)
+    vms(T.EB[:], 0.0, ["EB"], 2048, .5)
+    EBT, GST, HBT = ["EB"], ["GS"], ["HB"]
+    for q in range(16):
+        act(T.EB[:, 128 * q + q:128 * q + 128:16], T.ID[:, q:128:16], F.Copy, ["ID", "EB"], ["EB%d" % q], 8)
+        EBT.append("EB%d" % q)
+    if S_ACT:
+        act(T.EF[:], T.EB[:], F.Copy, EBT, ["EF"], 2048)
+    vcp(T.EH[:], T.EB[:], EBT, ["EH"], 2048, .5)
+    for q in range(16):
+        act(T.GS[:, 128 * q + q:128 * q + 128:16], T.BD[:, q:128:16], F.Copy, ["BD", "GS", "GSz"], ["GS%d" % q], 8, scale=32768.0)
+        GST.append("GS%d" % q)
+    vts(ICOL["PJ"], ICOL["PI"], 15, None, O.bitwise_and, None, ["PI"], ["PJ"], 1)
+    vcp(COL["PF"], ICOL["PJ"], ["PJ"], ["PF"], 1)
+    vts(T.DUMPA[:], T.DUMA0[:], COL["PF"], None, O.add, None, ["DUMA0", "PF"], ["DUMPA"], 40)
+    vts(COL["BIASL"], COL["PF"], -14.5, None, O.add, None, ["PF"], ["BIASL"], 1)
+    vts(COL["BIASF"], COL["PF"], -1.0, 0.5, O.mult, O.add, ["PF"], ["BIASF"], 1)
+    vts(COL["M0"], COL["PF"], 0.0, -float(ZC), O.is_equal, O.mult, ["PF"], ["M0"], 1)
+    vts(T.BDM[:], T.BD[:], COL["M0"], None, O.mult, None, ["BD", "M0"], ["BDM"], 128)
+    vcp(T.BDH[:], T.BD[:], ["BD"], ["BDH"], 128, .5)
+    vcp(T.SELH[:], T.BD[:, 0:128:16], ["BD"], ["SELH"], 8)
+    vts(T.MASK[:], T.MQ[:], COL["PF"], None, O.is_equal, None, ["MQ", "PF"], ["MASK"], 128)
+    vts(COL["M1"], COL["PF"], 1.0, None, O.is_equal, None, ["PF"], ["M1"], 1)
+    vts(COL["C0"], COL["PF"], 0.0, 1024.0, O.is_equal, O.mult, ["PF"], ["C0"], 1)
+    vts(COL["C2"], COL["PF"], 2.0, -32768.0, O.is_equal, O.mult, ["PF"], ["C2"], 1)
+    vtt(COL["C02"], COL["C0"], COL["C2"], O.add, ["C0", "C2"], ["C02"], 1)
+    vts(T.DJ[:], T.JR[:], COL["M1"], COL["C02"], O.mult, O.add, ["JR", "M1", "C02"], ["DJ"], CAP)
+    vts(T.IDH[:], T.ID[:], 0.5, None, O.mult, None, ["ID"], ["IDH"], 128, .5)
+    vtt(T.LU[:], T.IDH[:], T.SLM[:], O.subtract, ["IDH", "SLM"], ["LU"], 128)
+    vtt(T.FU[:], T.IDH[:], T.SUM[:], O.subtract, ["IDH", "SUM"], ["FU"], 128)
+    vts(T.IDB[:], T.ID[:], 2048.0, None, O.mult, None, ["ID"], ["IDB"], 128, .5)
+    vts(T.SLN[:], T.SLM[:], -1.0, None, O.mult, None, ["SLM"], ["SLN"], 128, .5)
+    vtt(T.TRIX[:], T.SLN[:], T.IDB[:], O.subtract, ["SLN", "IDB"], ["TRIX"], 128)
+    vts(T.BDN[:], T.BD[:], -2048.0, None, O.mult, None, ["BD"], ["BDN"], 128, .5)
+    for h in range(2):
+        for e in range(2):
+            for a in range(4):
+                c = 128 * (2 * h + e) + 32 * a + 16 * e
+                HBT.append("HB%d" % c)
+                act(T.HB[:, c:c + 16], T.ID[:, 32 * a + 16 * h:32 * a + 16 * h + 16], F.Copy, ["ID", "HB"], [HBT[-1]], 16)
+    vcp(T.HS[:], T.HB[:], HBT, ["HS"], 512, .5)
+    vms(T.O16[:], 1.0 / 16.0, ["O16"], 128)
+    vms(T.ONE40[:], 1.0, ["ONE40"], 40)
+    vms(T.THR[:, 0:1], 9.0, ["THR0"], 1)
+    vms(T.OBW[:], 0, ["OBW%d%d" % (x, k) for x in range(3) for k in range(3)], 48)
+    vms(T.NB[:, 0:OFF], float(NULLC), ["NBf"], OFF)
+    vms(T.NB[:, NULLC:WB], float(NULLC), ["NBg"], 8)
+    vts(T.TT[:, 240:256], T.ONB[:, 0:16], 1024.0, None, O.mult, None, ["ONB"], ["TTp"], 16)
+
+    def ghosts_out(w):
+        vts(T.GHS[:, w * GH:(w + 1) * GH], T.FX[:, 0:VA].indirect(T.BDU[:, 0:24]), float(OB + 8), -float(OB), O.max, O.add,
+            ["FX", "BDU"], ["GHS%d" % w], GH, GA)
+        remote(mine[4 + w], ["GHS%d" % w])
+
+    def ghosts_in(w):
+        arrive("ag%d" % w, ["LG%d" % w], 4.0)
+        vcp(T.FX[:, VA:VA + GH], T.LG[:, w * GH:(w + 1) * GH], ["LG%d" % w], ["FX"], GH)
+
+    ghosts_out(0)
+    vts(T.NBX[:], T.NBB[:], EXT, NULLC, O.add, O.min, ["NBB"], ["NBX"], OB)
+    for m in mine[2:4]:
+        remote(m, ["NBX"])
+    vts(T.NB[:, OFF:EXT], T.NBB[:], OFF, None, O.add, None, ["NBB"], ["NBo"], OB)
+    for i in range(2):
+        arrive("ax%d" % i, ["ZBe%d" % i], 8.0)
+    for i in range(2):
+        arrive("an%d" % i, ["LN%d" % i], 10.0)
+    ZBT = ["ZBf", "ZBg", "ZBo", "ZBe0", "ZBe1"]
+    NBT = ["NBf", "NBg", "NBo", "NBe0", "NBe1"]
+    B = [T["ps%d" % i] for i in range(7)]
+
+    def front(w):
+        p = str(w % 2)
+        el = B[6][:, 0:40]
+        if w == 0:
+            mm([(B[6][:, 40:40 + S0], T.BD[:], T.MB[:], True, True)], ["BD", "MB"], ["ps6"], S0)
+            vts(T.EM[:, 0:S0], B[6][:, 40:40 + S0], 0.0, None, O.is_equal, None, ["ps6"], ["EM", "ps6"], S0)
+        mm([(el, T.EB[:, 128 * q:128 * q + 128], T.EM[:, q:VA:16], q == 0, w == 0 and q == 15) for q in range(16)], ["EM"] + EBT, ["ps6"], 1024)
+        if w:
+            act(T.FLB[:], T.FL[:, 0:VA], F.Copy, ["FL"], ["FLB"], VA)
+            mm([(el, T.EB[:, 128 * q:128 * q + 128], T.FLB[:, q:VA:16], False, q == 15) for q in range(16)], ["FLB"] + EBT, ["ps6"], 1024)
+        vts(T.EL[:], el, 1.5 if w else 0.5, None, O.is_ge, None, ["ps6"], ["EL", "ps6"], 40)
+        mm([(B[6][:, 40:80], T.BD[:], T.EL[:], True, True), (B[6][:, 80:120], T.TRIX[:], T.EL[:], True, True)], ["BD", "TRIX", "EL"], ["ps6"], 128)
+        tk("V", cost(40, 1), ["ONE40"], ["CUM", "ps6"], lambda: V.tensor_tensor_scan(T.CUM[:], T.ONE40[:], B[6][:, 40:80], 2047.0, O.mult, O.add))
+        vtt(T.PO1[:], T.CUM[:], B[6][:, 80:120], O.add, ["CUM"], ["PO1", "ps6"], 40, 1)
+        vtt(T.PO2[:], T.PO1[:], T.DUMPA[:], O.min, ["PO1", "DUMPA"], ["PO2"], 40)
+        vcp(T.POU[:], T.PO2[:], ["PO2"], ["POU"], 40)
+        act(T.LW[:, 0:CAP], T.DUMROW[:], F.Copy, ["DUMROW"], ["LW"], CAP)
+        tk("V", cost(VA, SCA), ["POU", "IOTAF"], ["LW"], lambda: V.tensor_copy(T.LW[:, 0:1280].indirect(T.POU[:, 0:40]), T.IOTAF[:]))
+        vcp(T.LWH[:], T.LW[:, 0:CAP], ["LW"], ["LWH"], CAP)
+        mm([(B[6][:, 120:135], T.EH[:, 128 * q:128 * q + 128], T.LWH[:, q:CAP:16], q == 0, q == 15) for q in range(16)], ["LWH", "EH"], ["ps6"], 1024)
+        vcp(T["LU" + p][:], T.LW[:, 0:CAP], ["LW"], ["LU" + p], CAP)
+        vcp(T["AW" + p][:, 0:15], B[6][:, 120:135], [], ["AW" + p, "ps6"], 15)
+        vcp(T["NFU" + p][:], T.NBA[:, 0:WE].indirect(T["AW" + p][:, 0:15]), ["NBA", "NBAd", "AW" + p], ["NFU" + p], CAP, GA)
+        vcp(T["NFH" + p][:], T["NFU" + p][:], ["NFU" + p], ["NFH" + p], CAP, .5)
+        act(T["XF" + p][:], T.XA[:, 0:WE].indirect(T["AW" + p][:, 0:15]), F.Copy, ["XA", "XAd", "AW" + p], ["XF" + p], CAP, GA)
+        for k in range(3):
+            act(ch("XR" + p, k, 16), T.XA[:, 0:WE].indirect(ch("LU" + p, k)), F.Copy, ["XA", "XAd", "LU" + p], ["XR%s%d" % (p, k)], 16 * CH[k][1], GA)
+        if w < RO - 1:
+            act(T.FL[:, 0:WE].indirect(T["AW" + p][:, 0:15]), T.ZROW[:], F.Tanh, ["ZROW", "AW" + p], ["FL"], CAP, SCA)
+
+    front(0)
+    for i in range(2):
+        a, b = (0, NB_HALF) if i == 0 else (NB_HALF, OB - 1)
+        vcp(T.NB[:, EXT + a:EXT + b], T.LN[:, a:b], ["LN%d" % i], ["NBe%d" % i], b - a)
+
+    def test(w, k, step):
+        p, s, pa, pb = str(w % 2), str(k), "ps%d" % k, "ps%d" % (3 + k)
+        c0, n = CH[k]
+        PA, PB = B[k], B[3 + k]
+        cnt, pick, none = PA[:, 0:n], PB[:, 192:192 + n], PB[:, 288:288 + n]
+        tk("V", cost(16 * n, GA), ZBT + ["OFS" + s, "XR" + p + s], ["D" + s],
+           lambda: V.tensor_tensor(ch("D", k, 16), T.ZB[:, 0:WB].indirect(ch("OFS", k)), ch("XR" + p, k, 16), O.subtract))
+        act(ch("SQ", k, 16), ch("D", k, 16), F.Square, ["D" + s], ["SQ" + s], 16 * n)
+        vts(ch("NR", k, 16), ch("SQ", k, 16), T.THR[:, w:w + 1], 0.84375, O.is_le, O.subtract, ["SQ" + s, "THR%d" % w], ["NR" + s], 16 * n, .5)
+        mm([(cnt, T.GS[:, 128 * q:128 * q + 128], by("NR", k, q), q == 0, q == 15) for q in range(16)], ["NR" + s] + GST, [pa], 16 * n)
+        act(ch("SG", k), cnt, F.Sign, [], ["SG" + s, pa], n)
+        U = "LU" if step else "FU"
+        mm([(pick, T[U][:], ch("SG", k), True, True), (none, T.BD[:], ch("SG", k), True, True)], [U, "BD", "SG" + s], [pb], 2 * n)
+        act(pick, pick, F.Relu, ["BIASL", "BIASF"], [pb], n, bias=COL["BIASL" if step else "BIASF"])
+        nn = ch("NO" + p, k) if step == 0 else ch("NN", k)
+        nt = "NO" + p + s if step == 0 else "NN" + s
+        kw = dict(accum_out=T.NFAIL[:, 4 * (w % 2) + k:4 * (w % 2) + k + 1]) if step == 0 else {}
+        act(nn, none, F.Relu, [], [nt, pb] + (["NFAIL%d%d" % (w % 2, k)] if step == 0 else []), n, scale=-0.5, bias=-7.0, **kw)
+        vtt(ch("SP", k), pick, ch("Z", k), O.mult, ["Z" + s], ["SP" + s, pb], n, 1)
+        m, turned, ob = n // 16, PB[0:n, 384:512], PB[:, 96:96 + n // 16]
+        Y = T.Y[0:n, 128 * k:128 * k + 128]
+        mm([(turned, nn, T.BDM[:], True, False), (turned, ch("SP", k), T.BDH[:], False, True)], ["BDM", "BDH", nt, "SP" + s], [pb], 256)
+        vtt(Y, turned, T.MASK[0:n, :], O.mult, ["MASK"], ["Y" + s, pb], 128, 1)
+        mm([(ob, Y, T.SELH[0:n, 0:m], True, True)], ["Y" + s, "SELH"], [pb], 64)
+        vts(T.OBW[:, 16 * step + c0 // 16:16 * step + c0 // 16 + m], ob, float(ZC), None, O.add, None, [], ["OBW%d%s" % (step, s), pb], m)
+        cand, ct = (ch("Z", k), "Z") if step == 0 else (ch("OK", k), "OK")
+        vtt(cnt, cnt, cand, O.min, [ct + s], [pa], n, 1)
+        if step == 0:
+            vts(ch("NW", k), cnt, -float(ZC), float(ZC), O.max, O.add, [], ["NW" + s, pa], n)
+        elif step == 1:
+            vtt(ch("NX", k), ch("NW", k), cnt, O.max, ["NW" + s], ["NX" + s, pa], n, 1)
+        else:
+            vtt(ch("KI", k), ch("NX", k), cnt, O.max, ["NX" + s], ["KI" + s, pa], n, 1)
+            vts(ch("NI", k), ch("KI", k), 4095, None, O.bitwise_and, None, ["KI" + s], ["NI" + s], n)
+
+    def mark(w, k):
+        p, s = str(w % 2), str(k)
+        c0, n = CH[k]
+        nb = (n + 31) // 32
+        mm([(B[6][:, c0:c0 + n], T.BD[:], ch("DJ", k), True, False), (B[6][:, c0:c0 + n], T.BDN[:], ch("SG", k), False, True)],
+           ["BD", "DJ", "BDN", "SG" + s], ["ps6"], 2 * n)
+        vtt(ch("TT", k), ch("NFH" + p, k), B[6][:, c0:c0 + n], O.max, ["NFH" + p], ["TT" + s, "ps6"], n, 1)
+        tk("V", cost(32 * nb, .5), ["TT" + s, "TTp"], ["TTT" + s], lambda: V.transpose(T.TTT[:, c0:c0 + 32 * nb], T.TT[:, c0:c0 + 32 * nb]))
+        lst, z = [], 240 + c0
+        for b in range(nb):
+            for h in range(2):
+                for e in range(2):
+                    i, a = 2 * h + e, c0 + 32 * b + 16 * e
+                    lst.append((B[6][:, z + h * nb + b:z + 32 * nb:2 * nb], T.HS[:, 128 * i:128 * i + 128], T.TTT[:, a:a + 16], e == 0, e == 1))
+        mm(lst, ["TTT" + s, "HS"], ["ps6"], 64 * len(lst))
+        vcp(T.FT[:, c0:c0 + 32 * nb], B[6][:, z:z + 32 * nb], [], ["FT" + s, "ps6"], 32 * nb)
+        for q in range(16):
+            a = c0 + 2 * nb * q
+            act(T.FL[:, 0:WE].indirect(T.FT[:, a:a + n // 16]), T.C20[:, 0:n], F.Tanh, ["C20", "FT" + s], ["FL"], n, SCA)
+
+    def wave(w):
+        p = str(w % 2)
+        last = w == RO - 1
+        AW15 = T["AW" + p][:, 0:15]
+        ghosts_in(w)
+        for k in range(3):
+            s = str(k)
+            c0, n = CH[k]
+            PA = B[k]
+            off = ch("NFU" + p, k)
+            if k in S_ACT:
+                act(ch("SF", k, 16), T.FX[:, 0:WE].indirect(off), F.Copy, ["FX", "NFU" + p], ["SF" + s], 16 * n, GA, bias=-float(ZC))
+                src, E, cyc = "SF", "EF", 64 * n
+            else:
+                vts(ch("ST", k, 16), T.FX[:, 0:WE].indirect(off), -float(ZC), None, O.add, None, ["FX", "NFU" + p], ["ST" + s], 16 * n, GA)
+                src, E, cyc = "ST", "EH", 16 * n
+            mm([(PA[:, 96:96 + n], T[E][:, 128 * q:128 * q + 128], by(src, k, q), q == 0, q == 15) for q in range(16)], [src + s, E], ["ps%d" % k], cyc)
+            vts(ch("OFS", k), PA[:, 96:96 + n], float(ZC), None, O.add, None, [], ["OFS" + s, "ps%d" % k], n)
+            act(ch("Z", k), PA[:, 96:96 + n], F.Copy, [], ["Z" + s, "ps%d" % k], n)
+            test(w, k, 0)
+            if not last:
+                mark(w, k)
+        if not last:
+            tk("V", cost(CAP, SCA), ["NO%s%d" % (p, k) for k in range(3)] + ["AW" + p], ["EM"],
+               lambda: V.tensor_copy(T.EM[:, 0:WE].indirect(AW15), T["NO" + p][:]))
+            nf = 4 * (w % 2)
+            mm([(B[6][:, 500:501], T.O16[:], T.NFAIL[:, nf + k:nf + k + 1], k == 0, k == 2) for k in range(3)],
+               ["O16"] + ["NFAIL%d%d" % (w % 2, k) for k in range(3)], ["ps6"], 768)
+            vcp(ICOL["EI"], B[6][:, 500:501], [], ["EI", "ps6"], 1)
+            vts(ICOL["EJ"], ICOL["EI"], 1, None, O.bitwise_and, None, ["EI"], ["EJ"], 1)
+            vts(T.THR[:, w + 1:w + 2], ICOL["EJ"], 7.0, 9.0, O.mult, O.add, ["EJ"], ["THR%d" % (w + 1)], 1)
+        for step in (1, 2):
+            up = 4096.0 * step
+            for k in range(3):
+                s, n = str(k), CH[k][1]
+                c = 16 * (step - 1) + CH[k][0] // 16
+                nbr, ot = T.NB[:, 0:WB].indirect(T.OBW[:, c:c + n // 16]), "OBW%d%s" % (step - 1, s)
+                vcp(ch("OFS", k), nbr, NBT + [ot], ["OFS" + s], n, GA)
+                act(ch("Z", k), nbr, F.Copy, NBT + [ot], ["Z" + s], n, GA, bias=-float(ZC))
+                act(ch("OK", k), ch("Z", k), F.Copy, ["Z" + s], ["OK" + s], n, bias=up + ZC)
+                test(w, k, step)
+        for k in range(3):
+            c0, n = CH[k]
+            tk("V", cost(n, SCA), ["NI%d" % k, "AW" + p], ["FX"],
+               lambda k=k, c0=c0, n=n: V.tensor_copy(T.FX[:, 0:WE].indirect(T["AW" + p][:, c0 // 16:(c0 + n) // 16]), ch("NI", k)))
+        if not last:
+            ghosts_out(w + 1)
+            front(w + 1)
+        XFP = T["XF" + p][:]
+        obt = ["OBW%d%d" % (x, k) for x in range(3) for k in range(3)]
+        f = [T.BF[:, 16 * x:16 * x + 15] for x in range(3)]
+        vcp(T.BF[:, 0:47], T.OBW[:, 0:47], obt, ["BF"], 47)
+        vts(T.BM[:, 0:47], T.OBW[:, 0:47], 0.0, None, O.is_equal, None, obt, ["BM"], 47)
+        vtt(T.BS[:, 0:15], f[0], T.BM[:, 16:31], O.mult, ["BF", "BM"], ["BS"], 15)
+        vtt(T.BS[:, 0:15], T.BS[:, 0:15], f[1], O.add, ["BF"], ["BS"], 15)
+        vtt(T.BS[:, 0:15], T.BS[:, 0:15], T.BM[:, 32:47], O.mult, ["BM"], ["BS"], 15)
+        vtt(T.BS[:, 0:15], T.BS[:, 0:15], f[2], O.add, ["BF"], ["BS"], 15)
+        vcp(T.BW2[:, 0:15], T.BS[:, 0:15], ["BS"], ["BW2"], 15)
+        tk("V", cost(CAP, GA), ZBT + ["BW2", "XF" + p], ["XD"],
+           lambda: V.tensor_tensor(T.XD[:], T.ZB[:, 0:WB].indirect(T.BW2[:, 0:15]), XFP, O.subtract))
+        vts(T.XC[:], T.XD[:], -2.0, 2.0, O.max, O.min, ["XD"], ["XC"], CAP, .5)
+        SC = B[5][:, 0:CAP]
+        act(SC, T["NO" + p][:], F.Copy, ["NO%s%d" % (p, k) for k in range(3)], ["ps5"], CAP, scale=-1.0, bias=1.0)
+        vtt(SC, SC, T.XC[:], O.mult, ["XC"], ["ps5"], CAP, 1)
+        vtt(T.XN[:], SC, XFP, O.add, ["XF" + p], ["XN", "ps5"], CAP, 1)
+        tk("V", cost(CAP, SCA), ["XN", "AW" + p], ["XA"], lambda: V.tensor_copy(T.XA[:, 0:WE].indirect(AW15), T.XN[:]))
+
+    for w in range(RO):
+        wave(w)
+    vts(T.YM[:], T.FX[:, 0:VA], 0.0, 2559.0 + OFF, O.is_equal, O.mult, ["FX"], ["YM"], VA)
+    act(T.Y1[:], T.FX[:, 0:VA], F.Copy, ["FX"], ["Y1"], VA, bias=-float(OFF))
+    vtt(T.YO[:], T.Y1[:], T.YM[:], O.add, ["Y1", "YM"], ["YO"], VA)
+    tk("S", 0.1, ["YO"], ["yf"], lambda: SY.dma_start(T.yf[:], T.YO[:]), sem="oy", val=16)
+    tk("S", 0.1, ["XA"], ["ya"], lambda: SY.dma_start(T.ya[:], T.XA[:, 0:VA]), sem="ox", val=16)
+    return tasks, sent
+
+
+LAT = {"V": 0.05, "A": 0.08, "P": 0.1, "G": 0.1, None: 0.0}
+EPS = 0.06
+BONUS = {}
+
+
+def plan(tasks):
+    n = len(tasks)
+    succ = [[] for _ in range(n)]
+    for i, t in enumerate(tasks):
+        for d in t["deps"]:
+            succ[d].append(i)
+    lat = [LAT[t["q"]] if t["sem"] is None or t["q"] is None else 2.2 for t in tasks]
+    prio = [0.0] * n
+    for i in range(n - 1, -1, -1):
+        prio[i] = tasks[i]["dur"] + lat[i] + max([prio[j] for j in succ[i]] + [0.0])
+    prio = [p + BONUS.get(t["tag"], 0.0) for p, t in zip(prio, tasks)]
+    left = [len(t["deps"]) for t in tasks]
+    est, fin, free, order = [0.0] * n, [0.0] * n, {}, []
+    ready = {}
+    for i in range(n):
+        if left[i] == 0:
+            ready.setdefault(tasks[i]["q"], []).append(i)
+    while len(order) < n:
+        best = None
+        for q, lst in ready.items():
+            if not lst:
+                continue
+            f = free.get(q, 0.0) if q is not None else 0.0
+            t0 = min(max(f, est[i]) for i in lst)
+            c = max((i for i in lst if max(f, est[i]) <= t0 + EPS), key=lambda i: prio[i])
+            if best is None or t0 < best[0]:
+                best = (t0, q, c)
+        t0, q, i = best
+        ready[q].remove(i)
+        fin[i] = (est[i] if q is None else max(t0, est[i])) + tasks[i]["dur"]
+        if q is not None:
+            free[q] = fin[i]
+        order.append(i)
+        for j in succ[i]:
+            est[j] = max(est[j], fin[i] + lat[i])
+            left[j] -= 1
+            if left[j] == 0:
+                ready.setdefault(tasks[j]["q"], []).append(j)
+    return order, fin
+
+
+def emit(g, T, tasks, order):
+    queues = {"V": g.vector, "A": g.scalar, "P": g.tensor, "G": g, "S": g.sync}
+    esem = {"V": "sV", "A": "sA", "P": "sP", "G": "sG"}
+    cnt = {k: 0 for k in esem}
+    known = {k: {} for k in queues}
+    done, clock, final = [None] * len(tasks), [None] * len(tasks), {}
+    for i in order:
+        t = tasks[i]
+        q = t["q"]
+        if q is None:
+            done[i] = (t["sem"], t["val"])
+            clock[i] = {t["sem"]: t["val"]}
+            final[t["sem"]] = t["val"]
+            continue
+        kn = known[q]
+        need = [d for d, hard in t["deps"].items() if done[d] is not None and (hard or tasks[d]["q"] != q or tasks[d]["sem"] is not None)]
+        need.sort(key=lambda d: -done[d][1])
+        for d in need:
+            s, v = done[d]
+            if kn.get(s, 0) < v:
+                queues[q].wait_ge(T.sem[s], v)
+            for a, b in clock[d].items():
+                if kn.get(a, 0) < b:
+                    kn[a] = b
+        x = t["fn"]()
+        if t["sem"] == "none":
+            continue
+        if t["sem"] is not None:
+            x.then_inc(T.sem[t["sem"]], 16)
+            done[i] = (t["sem"], 16)
+        else:
+            cnt[q] += 1
+            x.then_inc(T.sem[esem[q]], 1)
+            done[i] = (esem[q], cnt[q])
+        clock[i] = dict(kn)
+        clock[i][done[i][0]] = done[i][1]
+        final[done[i][0]] = max(final.get(done[i][0], 0), done[i][1])
+    return final
+
+
+def rank_program(g, core, T, topo):
+    msgs = messages(topo, T.cores)
+    if T.rank_of(core) is None:
+        relay_program(g, core, T, topo, msgs)
+        return
+    tasks, sent = build(g, core, T, topo, msgs)
+    order, _fin = plan(tasks)
+    final = emit(g, T, tasks, order)
+    for s, v in final.items():
+        g.wait_ge(T.sem[s], v)
+    g.wait_ge(T.sem["ls"], sent[0])

@@ -1,3 +1,4 @@
+import numpy as np
 from concourse.mybir import AluOpType as O, ActivationFunctionType as F
 
 VA, GH, OB, CAP, S0, RO = 640, 384, 1280, 240, 176, 5
@@ -5,28 +6,34 @@ OFF, NULLC, ZC = 9, 2568, 1288
 EXT = OFF + OB
 WB = 2576
 WE = 1264
+WF = 2288
 NB_HALF = 640
-CH = ((0, 96), (96, 64), (160, 80))
-S_ACT = (1,)
+BIG = 30000.0
+CH = ((0, 128), (128, 112))
+SEEDS = ((0, 64, "V"), (64, 64, "A"), (128, 112, "A"))
+XRQ = ((0, 128, "V"), (128, 112, "G"))
+CUTS = ((64,), (), ())
+NC = len(CH)
 
 SCRATCH = {}
 _L = {
-    "bfloat16": "ZB:2576 XA:1264 EM:1264 FLB:640 MB:176 ONB:128 BD:128 BDT:128 ID:128 SLM:128 SUM:128 LU:128 FU:128 IDH:128 IDB:128 "
-                "SLN:128 TRIX:128 BDN:128 BDM:128 GS:2048 EB:2048 HB:512 DJ:240 EL:40 XD:240 XC:240 XN:240 RX:640 "
-                "XR0:3840 XR1:3840 XF0:240 XF1:240 NO0:240 NO1:240 D:3840 SQ:3840 NR:3840 SG:240 NN:240",
-    "float16": "LWH:240 BDH:128 SELH:8 Y:384 EH:2048 HS:512 TT:256 TTT:256 NFH0:240 NFH1:240 ST:3840 SP:240",
-    "float32": "NB:2576 FX:1264 FL:1264 LW:1280 MF:176 FA:176 EF:2048 O16:128 COL:8 JR:240 MQ:128 MASK:128 BF:48 BM:48 BS:16 "
-               "DUMROW:240 IOTAF:640 DUMA0:40 DUMPA:40 C20:240 ZROW:240 ONE40:40 CUM:40 PO1:40 PO2:40 THR:8 NFAIL:16 "
-               "YM:640 Y1:640 YO:640 SF:3840 Z:240 OK:240 NW:240 NX:240",
-    "int32": "NBB:1280 NBA:1264 F0I:176 BDI:24 ICOL:4 KI:240 NI:240",
-    "uint16": "NBX:1280 LN:1280 BDU:24 POU:40 FT:256 BW2:16 RN:640 GHS:1920 RG:1920 LG:1920 NFU0:240 NFU1:240 AW0:16 AW1:16 "
-              "LU0:240 LU1:240 OFS:240 OBW:48",
+    "bfloat16": "ZB:2576 XAB:640 Q:3840 RX:640 YA:640",
+    "float16": "ONE:1024 BD:128 BDT:128 ID:128 IK:128 IN1:128 IN2:128 SLM:128 SLN:128 TRIX:128 GI:128 NEG:64 NGC:64 SEL:8 EH:2048 CM:1024 "
+               "HS:512 C2:240 MB:176 FH0:640 FH1:640 LFH:640 EL:40 LWH:240 FT0:256 SG:24 NOH:240 XFN0:240 XFN1:240 TT:256 TTT:256 XR0:3840 XR1:3840 "
+               "NR:3840 ST:3840 ZN:240 IDT:384 UR:768 UM:2304 DM:2304 S:768 MG:2304",
+    "float32": "NB:2576 FX:1264 FL0:2288 FL1:2288 LF:1264 LW:1280 XA:1264 MF:176 FA:176 O16:128 COL:8 MQ:16 MQI:16 KS:64 SB:192 IOTAF:640 DUMA0:40 "
+               "DUMPA:40 CMK:128 ONE40:40 CUM:40 PO1:40 PO2:40 THR:8 NFAIL:16 LFV:240 HL:480 XT:240 NI:240 Y1:640 YO:640",
+    "int32": "NBB:1280 NBA:640 NFW:1280 F0I:176 BDI:24 ICOL:4",
+    "uint16": "NBX:1280 LN:1280 BDU:24 POU:40 FT:256 RN:640 GHS:1920 RG:1920 LG:1920 NFU:240 AW0:16 AW1:16 OFS:240 OBW:48",
 }
 for _d in _L:
     for _x in _L[_d].split():
         SCRATCH[_x.split(":")[0]] = ("sbuf", [128, int(_x.split(":")[1])], _d)
-for _i in range(7):
+for _i in range(8):
     SCRATCH["ps%d" % _i] = ("psum", [128, 512], "float32")
+PC = ["ps%d" % k for k in range(NC)]
+PD = ["ps%d" % (NC + k) for k in range(NC)]
+PF, PM, PH = "ps6", "ps7", "ps5" if NC < 3 else "ps6"
 
 LOADS = ["xb", "f0", "bd", "nba", "xa", "nbb"]
 SEMAPHORES = ["sV", "sA", "sP", "sG", "ls", "oy", "ox", "rx", "rn", "ax0", "ax1", "an0", "an1"] + \
@@ -73,412 +80,519 @@ def relay_program(g, core, T, topo, msgs):
         g.wait_ge(T.sem["ls"], total)
 
 
-CY = 0.00083 * 1.25
-GA, SCA = 1.5, 3.6
+CY = 0.00083 * 1.1
+GA, SCA = 1.56, 3.8
+PE = 0.0006
+FLY = 5.0
 
 
 def build(g, core, T, topo, msgs):
-    tasks, lastw, readers = [], {}, {}
+    tasks, rec, bank = [], {}, {}
     V, A, P, SY = g.vector, g.scalar, g.tensor, g.sync
-    COL = {x: T.COL[:, i:i + 1] for i, x in enumerate(("PF", "BIASL", "BIASF", "M0", "M1", "C0", "C2", "C02"))}
-    ICOL = {x: T.ICOL[:, i:i + 1] for i, x in enumerate(("PI", "PJ", "EI", "EJ"))}
+
+    def R(name, a=0, b=None, s=1, n=128):
+        w, dt = SCRATCH[name][1][1], SCRATCH[name][2]
+        cols = range(w)[a:b:s]
+        lo, hi = min(cols[0], cols[-1]), max(cols[0], cols[-1]) + 1
+        bits = ((1 << (abs(s) * len(cols))) - 1) // ((1 << abs(s)) - 1) << lo
+        return dict(ap=T[name][0:n, a:b:s], f=(name, bits, (1 << hi) - (1 << lo), abs(s) == 1 and n == 128), o=None, n=len(cols),
+                    two=dt in ("bfloat16", "float16", "uint16"), ps=name[:2] == "ps")
+
+    def IX(win, off):
+        f = win["f"]
+        return dict(ap=win["ap"].indirect(off["ap"]), f=(f[0], f[1], f[2], False), o=off["f"], n=16 * off["n"], two=False, ps=False)
+
+    def TAG(name):
+        return dict(f=(name, 1, 1, True), o=None, ps=False)
 
     def tk(q, dur, rd, wr, fn, sem=None, val=0):
-        deps = {}
-        i = len(tasks)
-        for b in rd:
-            if b in lastw:
-                deps[lastw[b]] = True
-        for b in wr:
-            if b in lastw:
-                deps[lastw[b]] = True
-            for x in readers.get(b, []):
-                deps.setdefault(x, False)
-        for b in rd:
-            if b not in wr:
-                readers.setdefault(b, []).append(i)
-        for b in wr:
-            lastw[b] = i
-            readers[b] = []
-        tag = "".join(x for x in wr[0] if x.isalpha()) + (q or "")
-        tasks.append(dict(q=q, dur=dur, deps=deps, fn=fn, sem=sem, val=val, tag=tag))
+        deps, i = {}, len(tasks)
+        rd = [x for x in rd if isinstance(x, dict)]
+        reads = [x["f"] for x in rd] + [x["o"] for x in rd + wr if x["o"]]
+        writes = [x["f"] for x in wr]
+        for fs, isw in ((reads, False), (writes, True)):
+            for f in fs:
+                for r in rec.get(f[0], []):
+                    same = r[3] == q and tasks[r[2]]["sem"] is None and sem is None
+                    if (r[0] & f[1]) if same else (r[1] & f[2]):
+                        if r[4] and (WAW or not (isw and same)):
+                            deps[r[2]] = True
+                        elif isw:
+                            deps.setdefault(r[2], False)
+        for x in rd + wr:
+            if x["ps"]:
+                last = bank.setdefault(x["f"][0], {})
+                for e, t in last.items():
+                    if e != q:
+                        deps[t] = True
+        for x in rd + wr:
+            if x["ps"]:
+                bank[x["f"][0]][q] = i
+        for f in writes:
+            if f[3]:
+                rec[f[0]] = [r for r in rec.get(f[0], []) if r[1] & ~f[2]]
+        for f in writes:
+            rec.setdefault(f[0], []).append((f[1], f[2], i, q, True))
+        for f in reads:
+            rec.setdefault(f[0], []).append((f[1], f[2], i, q, False))
+        kind = 2 if wr[0]["o"] else 1 if rd and rd[0]["o"] else 0
+        tasks.append(dict(q=q, dur=dur, deps=deps, fn=fn, sem=sem, val=val, kind=kind, tag=wr[0]["f"][0] + (q or "")))
 
-    def cost(n, c):
-        return 0.06 + max(64, n * c) * CY
+    def ap(x):
+        return x["ap"] if isinstance(x, dict) else x
 
-    def vts(out, in0, s1, s2, o0, o1, rd, wr, n, c=1.0):
+    def cost(out, a, c, fix=0.06, least=64):
+        if out["o"]:
+            return fix + out["n"] * SCA * CY
+        if a is not None and a["o"]:
+            return fix + out["n"] * GA * CY
+        return fix + max(least, out["n"] * c) * CY
+
+    def half(*x):
+        return 0.5 if all(y["two"] for y in x) else 1.0
+
+    def vts(out, a, s1, s2, o0, o1=None):
         if o1 is None:
-            tk("V", cost(n, c), rd, wr, lambda: V.tensor_scalar(out, in0, s1, None, op0=o0))
+            tk("V", cost(out, a, half(out, a)), [a, s1], [out], lambda: V.tensor_scalar(out["ap"], a["ap"], ap(s1), None, op0=o0))
         else:
-            tk("V", cost(n, c), rd, wr, lambda: V.tensor_scalar(out, in0, s1, s2, op0=o0, op1=o1))
+            tk("V", cost(out, a, half(out, a)), [a, s1, s2], [out], lambda: V.tensor_scalar(out["ap"], a["ap"], ap(s1), ap(s2), op0=o0, op1=o1))
 
-    def vtt(out, a, b, op, rd, wr, n, c=2.0):
-        tk("V", cost(n, c), rd, wr, lambda: V.tensor_tensor(out, a, b, op))
+    def vtt(out, a, b, op):
+        tk("V", cost(out, a, 1.0 if a["ps"] or b["ps"] else 2.0), [a, b], [out], lambda: V.tensor_tensor(out["ap"], a["ap"], b["ap"], op))
 
-    def vcp(out, in_, rd, wr, n, c=1.0):
-        tk("V", cost(n, c), rd, wr, lambda: V.tensor_copy(out, in_))
+    def vcp(out, a):
+        tk("V", cost(out, a, half(out, a)), [a], [out], lambda: V.tensor_copy(out["ap"], a["ap"]))
 
-    def vms(ap, x, wr, n, c=1.0):
-        tk("V", cost(n, c), [], wr, lambda: V.memset(ap, x))
+    def vms(out, x):
+        tk("V", cost(out, None, half(out)), [], [out], lambda: V.memset(out["ap"], x))
 
-    def act(out, in_, fn, rd, wr, n, c=1.0, **kw):
-        tk("A", 0.07 + n * c * CY, rd, wr, lambda: A.activation(out, in_, fn, **kw))
+    def scan(out, d0, d1, init, o0=O.min, o1=O.max):
+        tk("V", cost(out, d0, half(out, d0, d1)), [d0, d1], [out], lambda: V.tensor_tensor_scan(out["ap"], d0["ap"], d1["ap"], init, o0, o1))
 
-    def mm(lst, rd, wr, cyc):
+    def act(out, a, fn, acc=None, **kw):
+        k = {x: ap(y) for x, y in kw.items()}
+        if acc:
+            k["accum_out"] = acc["ap"]
+        tk("A", cost(out, a, 1.0, 0.07, 0), [a] + list(kw.values()), [out] + ([acc] if acc else []), lambda: A.activation(out["ap"], a["ap"], fn, **k))
+
+    def mm(lst):
         def fn():
             x = None
             for o, l, r, a, b in lst:
-                x = P.matmul(o, l, r, a, b)
+                x = P.matmul(o["ap"], l["ap"], r["ap"], a, b)
             return x
-        tk("P", 0.05 + cyc * 0.00075, rd, wr, fn)
+        cyc = sum(max(min(64, l["n"]), r["n"]) * (1 if l["two"] else 4) for o, l, r, a, b in lst)
+        tk("P", 0.03 + cyc * PE, [x[1] for x in lst] + [x[2] for x in lst], [x[0] for x in lst], fn)
 
-    def iota(out, pat, base, wr, n, rd=()):
-        tk("G", 0.13 + 2 * n * CY, list(rd), wr, lambda: g.iota(out, pat, base, 0, allow_small_or_imprecise_dtypes=True))
+    def iota(out, pat, base, cm=0):
+        if SCRATCH[out["f"][0]][2] == "int32":
+            tk("G", 0.13 + 2 * out["n"] * CY, [], [out], lambda: g.iota(out["ap"], pat, base, cm))
+        else:
+            tk("G", 0.13 + 2 * out["n"] * CY, [], [out], lambda: g.iota(out["ap"], pat, base, cm, allow_small_or_imprecise_dtypes=True))
 
-    def asel(out, in_, pat, op, base, cm, rd, wr, n):
-        tk("G", 0.17 + 2 * n * CY, rd, wr, lambda: g.affine_select(out, in_, pat, op, 0.0, base, cm))
+    def asel(out, a, pat, op, base, cm):
+        tk("G", 0.17 + 2 * out["n"] * CY, [a], [out], lambda: g.affine_select(out["ap"], a["ap"], pat, op, 0.0, base, cm))
+
+    def copy(q, out, a):
+        if q == "V":
+            vcp(out, a)
+        elif q == "A":
+            act(out, a, F.Copy)
+        else:
+            asel(out, a, [[0, out["n"]]], O.is_ge, 0, 0)
 
     def ch(name, k, w=1):
-        return T[name][:, w * CH[k][0]:w * (CH[k][0] + CH[k][1])]
+        return R(name, w * CH[k][0], w * (CH[k][0] + CH[k][1]))
 
     def by(name, k, q):
-        return T[name][:, 16 * CH[k][0] + q:16 * (CH[k][0] + CH[k][1]):16]
+        return R(name, 16 * CH[k][0] + q, 16 * (CH[k][0] + CH[k][1]), 16)
 
-    def load(q, name, out, wr, rd):
+    def blk(name, i, n=128):
+        return R(name, 128 * i, 128 * i + 128, 1, n)
+
+    def load(q, name, out):
         e = SY if q == "S" else A
-        tk(q, 0.1, rd, wr, lambda: e.dma_start(out, T[name][:]), sem="l" + name, val=16)
+        tk(q, 0.1, [], [out], lambda: e.dma_start(out["ap"], T[name][:]), sem="l" + name, val=16)
 
-    vms(T.ZB[:, 0:OFF], 1000.0, ["ZBf"], OFF)
-    vms(T.ZB[:, NULLC:WB], 1000.0, ["ZBg"], 8)
-    load("S", "f0", T.F0I[:], ["F0I"], [])
-    load("A", "xb", T.ZB[:, OFF:EXT], ["ZBo"], ["ZBf"])
-    load("S", "bd", T.BDI[:], ["BDI"], [])
-    load("S", "nba", T.NBA[:, 0:VA], ["NBA"], [])
-    load("A", "xa", T.XA[:, 0:VA], ["XA"], [])
-    load("S", "nbb", T.NBB[:], ["NBB"], [])
+    COL = {x: R("COL", i, i + 1) for i, x in enumerate(("PF",))}
+    ICOL = {x: R("ICOL", i, i + 1) for i, x in enumerate(("PI", "PJ", "EI", "EJ"))}
+    ZB, NB, FX, XA, LF = R("ZB"), R("NB"), R("FX"), R("XA"), R("LF")
+
+    vms(R("ZB", 0, 16), 1000.0)
+    vms(R("ZB", NULLC, WB), 1000.0)
+    load("S", "f0", R("F0I"))
+    load("A", "xb", R("ZB", OFF, EXT))
+    load("S", "bd", R("BDI"))
+    load("S", "nba", R("NBA", 0, VA))
+    load("A", "xa", R("XAB"))
+    load("S", "nbb", R("NBB"))
 
     mine = [m for m in msgs if m[0] == core]
     inb = {m[8]: m for m in msgs if m[2] == core}
     sent = [0]
 
-    def remote(m, rd):
+    def remote(m):
         def fn():
             sent[0] += send(g, topo, core, m[1], m[3], m[4], m[9], m[10], T, m[5])
-        tk("G", 0.6, rd, ["snt" + m[8]], fn, sem="none")
+        tk("G", 2.6 if m is mine[0] else 0.6, [R(m[9], m[10][0], m[10][1])], [TAG("snt" + m[8])], fn, sem="none")
 
-    def arrive(sem, wr, delay):
+    def arrive(sem, delay):
         m = inb[sem]
-        tk(None, delay, ["snt" + sem], wr, None, sem=sem, val=len(topo.engines(m[1], core)))
+        tk(None, delay, [TAG("snt" + sem)], [R(m[6], m[7][0], m[7][1])], None, sem=sem, val=len(topo.engines(m[1], core)))
 
     for m in mine[0:2]:
-        remote(m, ["ZBo"])
+        remote(m)
 
-    vms(T.ONB[:], 1.0, ["ONB"], 128, .5)
-    asel(T.BDT[:], T.ONB[:], [[-16, 8], [0, 16]], O.is_ge, 0, 1, ["ONB"], ["BDT"], 128)
-    asel(T.BD[:], T.BDT[:], [[16, 8], [0, 16]], O.is_ge, 15, -1, ["BDT"], ["BD"], 128)
-    asel(T.ID[:], T.ONB[:], [[-1, 128]], O.is_equal, 0, 1, ["ONB"], ["ID"], 128)
-    tk("G", 0.15, [], ["PI"], lambda: g.iota(ICOL["PI"], [[0, 1]], 0, 1))
-    iota(T.IOTAF[:], [[1, VA]], 0, ["IOTAF"], VA, ["BD"])
-    iota(T.DUMROW[:], [[1, CAP]], 1024, ["DUMROW"], CAP)
-    iota(T.DUMA0[:], [[16, 40]], VA, ["DUMA0"], 40)
-    iota(T.MQ[:], [[0, 8], [1, 16]], 0, ["MQ"], 128)
-    asel(T.SLM[:], T.BD[:], [[-1, 128]], O.is_gt, 0, 1, ["BD"], ["SLM"], 128)
-    asel(T.SUM[:], T.BD[:], [[1, 128]], O.is_gt, 0, -1, ["BD"], ["SUM"], 128)
-    iota(T.JR[:], [[1, CAP]], 0, ["JR"], CAP)
-    for ap, x, n, b in ((T.GS[:, 0:1024], 0, 1024, "GS"), (T.GS[:, 1024:2048], 0, 1024, "GSz"), (T.XA[:, VA:WE], 0, WE - VA, "XAd"), (T.ZROW[:], 0, CAP, "ZROW"),
-                        (T.FL[:], 1, WE, "FL"), (T.C20[:], 20, CAP, "C20"), (T.HB[:], 0, 512, "HB")):
-        iota(ap, [[0, n]], x, [b], n)
-    tk("G", 0.13 + 2 * (WE - VA) * CY, [], ["NBAd"], lambda: g.iota(T.NBA[:, VA:WE], [[0, WE - VA]], 1024, 0))
+    vms(R("ONE"), 1.0)
+    one = R("ONE", 0, 128)
+    asel(R("BDT"), one, [[-16, 8], [0, 16]], O.is_ge, 0, 1)
+    asel(R("BD"), R("BDT"), [[16, 8], [0, 16]], O.is_ge, 15, -1)
+    asel(R("ID"), one, [[-1, 128]], O.is_equal, 0, 1)
+    iota(ICOL["PI"], [[0, 1]], 0, 1)
+    iota(R("MQI"), [[1, 16]], 0)
+    iota(R("DUMA0"), [[16, 40]], VA)
+    asel(R("SLM"), R("BD"), [[-1, 128]], O.is_gt, 0, 1)
+    iota(R("IOTAF"), [[1, VA]], 32)
+    asel(R("GI"), one, [[-1, 8], [0, 16]], O.is_equal, 0, 1)
+    vms(R("NGC"), -2 * BIG)
+    asel(R("NEG"), R("NGC"), [[0, 8], [-1, 8]], O.not_equal, 0, 1)
+    asel(R("CM"), R("ONE"), [[-16, 8], [0, 8], [-1, 16]], O.is_equal, 0, 1)
 
-    vms(T.FX[:, S0:VA], 0.0, ["FX"], VA - S0)
-    vms(T.FX[:, VA + GH:WE], 0.0, ["FX"], CAP)
-    vts(T.MF[:], T.F0I[:], 2559, None, O.is_lt, None, ["F0I"], ["MF"], S0)
-    vts(T.FA[:], T.F0I[:], OFF, None, O.add, None, ["F0I"], ["FA"], S0)
-    vtt(T.FX[:, 0:S0], T.FA[:], T.MF[:], O.mult, ["FA", "MF"], ["FX"], S0)
-    vcp(T.BDU[:], T.BDI[:], ["BDI"], ["BDU"], 24)
-    vcp(T.MB[:], T.MF[:], ["MF"], ["MB"], S0)
-    vms(T.EM[:], 1.0, ["EM"], WE, .5)
-    vms(T.EB[:], 0.0, ["EB"], 2048, .5)
-    EBT, GST, HBT = ["EB"], ["GS"], ["HB"]
+    vms(R("FX", S0, VA), 0.0)
+    vms(R("FX", VA + GH, WE), 0.0)
+    vts(R("MF"), R("F0I"), 2559, None, O.is_lt)
+    vts(R("FA"), R("F0I"), OFF, None, O.add)
+    vtt(R("FX", 0, S0), R("FA"), R("MF"), O.mult)
+    vcp(R("BDU"), R("BDI"))
+    act(R("MB"), R("MF"), F.Copy)
+    vts(ICOL["PJ"], ICOL["PI"], 15, None, O.bitwise_and)
+    vcp(COL["PF"], ICOL["PJ"])
+    vts(R("MQ"), R("MQI"), COL["PF"], None, O.is_equal)
     for q in range(16):
-        act(T.EB[:, 128 * q + q:128 * q + 128:16], T.ID[:, q:128:16], F.Copy, ["ID", "EB"], ["EB%d" % q], 8)
-        EBT.append("EB%d" % q)
-    if S_ACT:
-        act(T.EF[:], T.EB[:], F.Copy, EBT, ["EF"], 2048)
-    vcp(T.EH[:], T.EB[:], EBT, ["EH"], 2048, .5)
-    for q in range(16):
-        act(T.GS[:, 128 * q + q:128 * q + 128:16], T.BD[:, q:128:16], F.Copy, ["BD", "GS", "GSz"], ["GS%d" % q], 8, scale=32768.0)
-        GST.append("GS%d" % q)
-    vts(ICOL["PJ"], ICOL["PI"], 15, None, O.bitwise_and, None, ["PI"], ["PJ"], 1)
-    vcp(COL["PF"], ICOL["PJ"], ["PJ"], ["PF"], 1)
-    vts(T.DUMPA[:], T.DUMA0[:], COL["PF"], None, O.add, None, ["DUMA0", "PF"], ["DUMPA"], 40)
-    vts(COL["BIASL"], COL["PF"], -14.5, None, O.add, None, ["PF"], ["BIASL"], 1)
-    vts(COL["BIASF"], COL["PF"], -1.0, 0.5, O.mult, O.add, ["PF"], ["BIASF"], 1)
-    vts(COL["M0"], COL["PF"], 0.0, -float(ZC), O.is_equal, O.mult, ["PF"], ["M0"], 1)
-    vts(T.BDM[:], T.BD[:], COL["M0"], None, O.mult, None, ["BD", "M0"], ["BDM"], 128)
-    vcp(T.BDH[:], T.BD[:], ["BD"], ["BDH"], 128, .5)
-    vcp(T.SELH[:], T.BD[:, 0:128:16], ["BD"], ["SELH"], 8)
-    vts(T.MASK[:], T.MQ[:], COL["PF"], None, O.is_equal, None, ["MQ", "PF"], ["MASK"], 128)
-    vts(COL["M1"], COL["PF"], 1.0, None, O.is_equal, None, ["PF"], ["M1"], 1)
-    vts(COL["C0"], COL["PF"], 0.0, 1024.0, O.is_equal, O.mult, ["PF"], ["C0"], 1)
-    vts(COL["C2"], COL["PF"], 2.0, -32768.0, O.is_equal, O.mult, ["PF"], ["C2"], 1)
-    vtt(COL["C02"], COL["C0"], COL["C2"], O.add, ["C0", "C2"], ["C02"], 1)
-    vts(T.DJ[:], T.JR[:], COL["M1"], COL["C02"], O.mult, O.add, ["JR", "M1", "C02"], ["DJ"], CAP)
-    vts(T.IDH[:], T.ID[:], 0.5, None, O.mult, None, ["ID"], ["IDH"], 128, .5)
-    vtt(T.LU[:], T.IDH[:], T.SLM[:], O.subtract, ["IDH", "SLM"], ["LU"], 128)
-    vtt(T.FU[:], T.IDH[:], T.SUM[:], O.subtract, ["IDH", "SUM"], ["FU"], 128)
-    vts(T.IDB[:], T.ID[:], 2048.0, None, O.mult, None, ["ID"], ["IDB"], 128, .5)
-    vts(T.SLN[:], T.SLM[:], -1.0, None, O.mult, None, ["SLM"], ["SLN"], 128, .5)
-    vtt(T.TRIX[:], T.SLN[:], T.IDB[:], O.subtract, ["SLN", "IDB"], ["TRIX"], 128)
-    vts(T.BDN[:], T.BD[:], -2048.0, None, O.mult, None, ["BD"], ["BDN"], 128, .5)
+        if q % 8 < 5:
+            vts(blk("EH", q), R("ID"), R("MQ", q, q + 1), None, O.mult)
+        else:
+            act(blk("EH", q), R("ID"), F.Copy, scale=R("MQ", q, q + 1))
+    vts(R("DUMPA"), R("DUMA0"), COL["PF"], None, O.add)
+    vts(R("SEL"), R("BD", 0, 128, 16), 4096.0, None, O.mult)
+    for x, c in (("IK", -512.0), ("IN1", -1.0), ("IN2", -2.0)):
+        vts(R(x), R("ID"), c, None, O.mult)
+    vts(R("SLN"), R("ID"), -2048.0, None, O.mult)
+    vtt(R("TRIX"), R("SLN"), R("SLM"), O.subtract)
+    vms(R("HS"), 0.0)
     for h in range(2):
         for e in range(2):
             for a in range(4):
                 c = 128 * (2 * h + e) + 32 * a + 16 * e
-                HBT.append("HB%d" % c)
-                act(T.HB[:, c:c + 16], T.ID[:, 32 * a + 16 * h:32 * a + 16 * h + 16], F.Copy, ["ID", "HB"], [HBT[-1]], 16)
-    vcp(T.HS[:], T.HB[:], HBT, ["HS"], 512, .5)
-    vms(T.O16[:], 1.0 / 16.0, ["O16"], 128)
-    vms(T.ONE40[:], 1.0, ["ONE40"], 40)
-    vms(T.THR[:, 0:1], 9.0, ["THR0"], 1)
-    vms(T.OBW[:], 0, ["OBW%d%d" % (x, k) for x in range(3) for k in range(3)], 48)
-    vms(T.NB[:, 0:OFF], float(NULLC), ["NBf"], OFF)
-    vms(T.NB[:, NULLC:WB], float(NULLC), ["NBg"], 8)
-    vts(T.TT[:, 240:256], T.ONB[:, 0:16], 1024.0, None, O.mult, None, ["ONB"], ["TTp"], 16)
+                act(R("HS", c, c + 16), R("ID", 32 * a + 16 * h, 32 * a + 16 * h + 16), F.Copy)
+    vms(R("O16"), 1.0 / 16.0)
+    vms(R("ONE40"), 1.0)
+    vms(R("THR", 0, 1), 1544.0)
+    vms(R("C2"), 2.0)
+    vms(R("NB", 0, OFF), float(NULLC))
+    vms(R("NB", NULLC, WB), float(NULLC))
+    vms(R("TT", CAP, 256), 0.0)
+    vms(R("KS"), BIG * BIG)
+    vms(R("KS", 0, 64, 8), -BIG * BIG)
+    vms(R("XA", 1024, WE), 0.0)
+    act(R("XA", 0, VA), R("XAB"), F.Copy)
+    act(R("FL0", 0, VA), R("ONE", 0, VA), F.Silu, scale=10.0)
+    iota(R("FL1", 0, VA), [[0, VA]], 10)
+    iota(R("LF", S0, VA), [[0, VA - S0]], 2000)
+    for k in range(NC):
+        u, r = 768 * k, 256 * k
+        for a in range(u, u + 768, 256):
+            act(R("UM", a, a + 256), R("ONE", 0, 256), F.Copy, scale=BIG)
+            act(R("DM", a, a + 256), R("ONE", 0, 256), F.Copy, scale=-BIG)
+        vms(R("UM", u + 2, u + 768, 6), -BIG)
+        vms(R("UM", u, u + 768, 96), -BIG)
+        vms(R("UM", u + 1, u + 768, 96), -BIG)
+        vms(R("UR", r, r + 256), BIG)
+        vms(R("UR", r + 31, r + 256, 32), -BIG)
 
     def ghosts_out(w):
-        vts(T.GHS[:, w * GH:(w + 1) * GH], T.FX[:, 0:VA].indirect(T.BDU[:, 0:24]), float(OB + 8), -float(OB), O.max, O.add,
-            ["FX", "BDU"], ["GHS%d" % w], GH, GA)
-        remote(mine[4 + w], ["GHS%d" % w])
+        vts(R("GHS", w * GH, (w + 1) * GH), IX(R("FX", 0, VA), R("BDU")), float(OB + 8), -float(OB), O.max, O.add)
+        remote(mine[4 + w])
 
     def ghosts_in(w):
-        arrive("ag%d" % w, ["LG%d" % w], 4.0)
-        vcp(T.FX[:, VA:VA + GH], T.LG[:, w * GH:(w + 1) * GH], ["LG%d" % w], ["FX"], GH)
+        arrive("ag%d" % w, FLY if w else FLY + 1.5)
+        vcp(R("FX", VA, VA + GH), R("LG", w * GH, (w + 1) * GH))
 
     ghosts_out(0)
-    vts(T.NBX[:], T.NBB[:], EXT, NULLC, O.add, O.min, ["NBB"], ["NBX"], OB)
+    vts(R("NBX"), R("NBB"), EXT, NULLC, O.add, O.min)
     for m in mine[2:4]:
-        remote(m, ["NBX"])
-    vts(T.NB[:, OFF:EXT], T.NBB[:], OFF, None, O.add, None, ["NBB"], ["NBo"], OB)
+        remote(m)
+    vts(R("NB", OFF, EXT), R("NBB"), OFF, None, O.add)
     for i in range(2):
-        arrive("ax%d" % i, ["ZBe%d" % i], 8.0)
+        arrive("ax%d" % i, FLY + 3.0)
     for i in range(2):
-        arrive("an%d" % i, ["LN%d" % i], 10.0)
-    ZBT = ["ZBf", "ZBg", "ZBo", "ZBe0", "ZBe1"]
-    NBT = ["NBf", "NBg", "NBo", "NBe0", "NBe1"]
-    B = [T["ps%d" % i] for i in range(7)]
+        arrive("an%d" % i, FLY + 3.0)
 
     def front(w):
         p = str(w % 2)
-        el = B[6][:, 0:40]
+        AW = R("AW" + p, 0, 15)
+        el = R(PF, 0, 40)
+        iota(R("LW", 0, CAP), [[1, CAP]], 1024 + 32)
         if w == 0:
-            mm([(B[6][:, 40:40 + S0], T.BD[:], T.MB[:], True, True)], ["BD", "MB"], ["ps6"], S0)
-            vts(T.EM[:, 0:S0], B[6][:, 40:40 + S0], 0.0, None, O.is_equal, None, ["ps6"], ["EM", "ps6"], S0)
-        mm([(el, T.EB[:, 128 * q:128 * q + 128], T.EM[:, q:VA:16], q == 0, w == 0 and q == 15) for q in range(16)], ["EM"] + EBT, ["ps6"], 1024)
-        if w:
-            act(T.FLB[:], T.FL[:, 0:VA], F.Copy, ["FL"], ["FLB"], VA)
-            mm([(el, T.EB[:, 128 * q:128 * q + 128], T.FLB[:, q:VA:16], False, q == 15) for q in range(16)], ["FLB"] + EBT, ["ps6"], 1024)
-        vts(T.EL[:], el, 1.5 if w else 0.5, None, O.is_ge, None, ["ps6"], ["EL", "ps6"], 40)
-        mm([(B[6][:, 40:80], T.BD[:], T.EL[:], True, True), (B[6][:, 80:120], T.TRIX[:], T.EL[:], True, True)], ["BD", "TRIX", "EL"], ["ps6"], 128)
-        tk("V", cost(40, 1), ["ONE40"], ["CUM", "ps6"], lambda: V.tensor_tensor_scan(T.CUM[:], T.ONE40[:], B[6][:, 40:80], 2047.0, O.mult, O.add))
-        vtt(T.PO1[:], T.CUM[:], B[6][:, 80:120], O.add, ["CUM"], ["PO1", "ps6"], 40, 1)
-        vtt(T.PO2[:], T.PO1[:], T.DUMPA[:], O.min, ["PO1", "DUMPA"], ["PO2"], 40)
-        vcp(T.POU[:], T.PO2[:], ["PO2"], ["POU"], 40)
-        act(T.LW[:, 0:CAP], T.DUMROW[:], F.Copy, ["DUMROW"], ["LW"], CAP)
-        tk("V", cost(VA, SCA), ["POU", "IOTAF"], ["LW"], lambda: V.tensor_copy(T.LW[:, 0:1280].indirect(T.POU[:, 0:40]), T.IOTAF[:]))
-        vcp(T.LWH[:], T.LW[:, 0:CAP], ["LW"], ["LWH"], CAP)
-        mm([(B[6][:, 120:135], T.EH[:, 128 * q:128 * q + 128], T.LWH[:, q:CAP:16], q == 0, q == 15) for q in range(16)], ["LWH", "EH"], ["ps6"], 1024)
-        vcp(T["LU" + p][:], T.LW[:, 0:CAP], ["LW"], ["LU" + p], CAP)
-        vcp(T["AW" + p][:, 0:15], B[6][:, 120:135], [], ["AW" + p, "ps6"], 15)
-        vcp(T["NFU" + p][:], T.NBA[:, 0:WE].indirect(T["AW" + p][:, 0:15]), ["NBA", "NBAd", "AW" + p], ["NFU" + p], CAP, GA)
-        vcp(T["NFH" + p][:], T["NFU" + p][:], ["NFU" + p], ["NFH" + p], CAP, .5)
-        act(T["XF" + p][:], T.XA[:, 0:WE].indirect(T["AW" + p][:, 0:15]), F.Copy, ["XA", "XAd", "AW" + p], ["XF" + p], CAP, GA)
-        for k in range(3):
-            act(ch("XR" + p, k, 16), T.XA[:, 0:WE].indirect(ch("LU" + p, k)), F.Copy, ["XA", "XAd", "LU" + p], ["XR%s%d" % (p, k)], 16 * CH[k][1], GA)
-        if w < RO - 1:
-            act(T.FL[:, 0:WE].indirect(T["AW" + p][:, 0:15]), T.ZROW[:], F.Tanh, ["ZROW", "AW" + p], ["FL"], CAP, SCA)
-
-    front(0)
-    for i in range(2):
-        a, b = (0, NB_HALF) if i == 0 else (NB_HALF, OB - 1)
-        vcp(T.NB[:, EXT + a:EXT + b], T.LN[:, a:b], ["LN%d" % i], ["NBe%d" % i], b - a)
-
-    def test(w, k, step):
-        p, s, pa, pb = str(w % 2), str(k), "ps%d" % k, "ps%d" % (3 + k)
-        c0, n = CH[k]
-        PA, PB = B[k], B[3 + k]
-        cnt, pick, none = PA[:, 0:n], PB[:, 192:192 + n], PB[:, 288:288 + n]
-        tk("V", cost(16 * n, GA), ZBT + ["OFS" + s, "XR" + p + s], ["D" + s],
-           lambda: V.tensor_tensor(ch("D", k, 16), T.ZB[:, 0:WB].indirect(ch("OFS", k)), ch("XR" + p, k, 16), O.subtract))
-        act(ch("SQ", k, 16), ch("D", k, 16), F.Square, ["D" + s], ["SQ" + s], 16 * n)
-        vts(ch("NR", k, 16), ch("SQ", k, 16), T.THR[:, w:w + 1], 0.84375, O.is_le, O.subtract, ["SQ" + s, "THR%d" % w], ["NR" + s], 16 * n, .5)
-        mm([(cnt, T.GS[:, 128 * q:128 * q + 128], by("NR", k, q), q == 0, q == 15) for q in range(16)], ["NR" + s] + GST, [pa], 16 * n)
-        act(ch("SG", k), cnt, F.Sign, [], ["SG" + s, pa], n)
-        U = "LU" if step else "FU"
-        mm([(pick, T[U][:], ch("SG", k), True, True), (none, T.BD[:], ch("SG", k), True, True)], [U, "BD", "SG" + s], [pb], 2 * n)
-        act(pick, pick, F.Relu, ["BIASL", "BIASF"], [pb], n, bias=COL["BIASL" if step else "BIASF"])
-        nn = ch("NO" + p, k) if step == 0 else ch("NN", k)
-        nt = "NO" + p + s if step == 0 else "NN" + s
-        kw = dict(accum_out=T.NFAIL[:, 4 * (w % 2) + k:4 * (w % 2) + k + 1]) if step == 0 else {}
-        act(nn, none, F.Relu, [], [nt, pb] + (["NFAIL%d%d" % (w % 2, k)] if step == 0 else []), n, scale=-0.5, bias=-7.0, **kw)
-        vtt(ch("SP", k), pick, ch("Z", k), O.mult, ["Z" + s], ["SP" + s, pb], n, 1)
-        m, turned, ob = n // 16, PB[0:n, 384:512], PB[:, 96:96 + n // 16]
-        Y = T.Y[0:n, 128 * k:128 * k + 128]
-        mm([(turned, nn, T.BDM[:], True, False), (turned, ch("SP", k), T.BDH[:], False, True)], ["BDM", "BDH", nt, "SP" + s], [pb], 256)
-        vtt(Y, turned, T.MASK[0:n, :], O.mult, ["MASK"], ["Y" + s, pb], 128, 1)
-        mm([(ob, Y, T.SELH[0:n, 0:m], True, True)], ["Y" + s, "SELH"], [pb], 64)
-        vts(T.OBW[:, 16 * step + c0 // 16:16 * step + c0 // 16 + m], ob, float(ZC), None, O.add, None, [], ["OBW%d%s" % (step, s), pb], m)
-        cand, ct = (ch("Z", k), "Z") if step == 0 else (ch("OK", k), "OK")
-        vtt(cnt, cnt, cand, O.min, [ct + s], [pa], n, 1)
-        if step == 0:
-            vts(ch("NW", k), cnt, -float(ZC), float(ZC), O.max, O.add, [], ["NW" + s, pa], n)
-        elif step == 1:
-            vtt(ch("NX", k), ch("NW", k), cnt, O.max, ["NW" + s], ["NX" + s, pa], n, 1)
+            m = S0 // 16
+            mm([(R(PF, 200, 200 + S0), R("BD"), R("MB"), True, True)])
+            act(R("LFH", 0, S0), R(PF, 200, 200 + S0), F.Copy)
+            act(R("LF", 0, S0), R(PF, 200, 200 + S0), F.Copy, scale=-2000.0, bias=2000.0)
+            mm([(R(PF, 0, m), blk("EH", q), R("LFH", q, S0, 16), q == 0, q == 15) for q in range(16)])
+            vms(R("EL", m, 40), 1.0)
+            vts(R("EL", 0, m), R(PF, 0, m), 0.0, None, O.is_equal)
         else:
-            vtt(ch("KI", k), ch("NX", k), cnt, O.max, ["NX" + s], ["KI" + s, pa], n, 1)
-            vts(ch("NI", k), ch("KI", k), 4095, None, O.bitwise_and, None, ["KI" + s], ["NI" + s], n)
+            copy("G", R("LFH"), R("LF", 0, VA))
+            mm([(el, blk("EH", q), R("LFH", q, VA, 16), q == 0, False) for q in range(16)])
+            for i in (1, 0):
+                act(R("FH%d" % i), R("FL%d" % i, 0, VA), F.Copy)
+                mm([(el, blk("EH", q), R("FH%d" % i, q, VA, 16), False, i == 0 and q == 15) for q in range(16)])
+            vts(R("EL"), el, 2000.0, None, O.is_ge)
+        mm([(R(PF, 40, 80), R("BD"), R("EL"), True, True), (R(PF, 80, 120), R("TRIX"), R("EL"), True, True)])
+        scan(R("CUM"), R("ONE40"), R(PF, 40, 80), 2047.0, O.mult, O.add)
+        vtt(R("PO1"), R("CUM"), R(PF, 80, 120), O.add)
+        vtt(R("PO2"), R("PO1"), R("DUMPA"), O.min)
+        vcp(R("POU"), R("PO2"))
+        iota(R("NFW", 0, CAP), [[1, CAP]], 1024)
+        vcp(IX(R("NFW"), R("POU")), R("NBA"))
+        vcp(R("NFU"), R("NFW", 0, CAP))
+        act(IX(R("LW"), R("POU")), R("IOTAF"), F.Silu)
+        act(R("LWH"), R("LW", 0, CAP), F.Copy, bias=-32.0)
+        mm([(R(PF, 120, 135), blk("EH", q), R("LWH", q, CAP, 16), q == 0, q == 15) for q in range(16)])
+        vcp(AW, R(PF, 120, 135))
+        act(R("XFN" + p), IX(XA, AW), F.Identity, scale=-1.0, bias=R("THR", w, w + 1))
+        for c0, n, e in XRQ:
+            for q in range(16):
+                copy(e, R("XR" + p, 16 * c0 + q, 16 * (c0 + n), 16), R("XFN" + p, c0, c0 + n))
+        if w < RO - 1:
+            mark_tables()
+            iota(R("CMK"), [[0, 128]], 30 * 3 ** w)
+
+    def pieces(k, t):
+        c0, n = CH[k]
+        cut = [c0] + [x for x in CUTS[t] if c0 < x < c0 + n] + [c0 + n]
+        return [(a, b - a) for a, b in zip(cut, cut[1:])]
+
+    def turn(k, z):
+        n = CH[k][1]
+        mm([(R(PD[k], 128, 256, 1, n), z, R("ID"), True, True)])
+        act(blk("IDT", k, n), R(PD[k], 128, 256, 1, n), F.Copy)
+
+    def test(w, k, t):
+        p = str(w % 2)
+        c0, n = CH[k]
+        m, u, r = n // 16, 768 * k, 256 * k
+        c = R(PC[k], 0, 128, 1, n)
+        for a, b in pieces(k, t):
+            vtt(R("Q", 16 * a, 16 * (a + b)), IX(ZB, R("OFS", a, a + b)), R("XR" + p, 16 * a, 16 * (a + b)), O.add)
+        vts(ch("NR", k, 16), ch("Q", k, 16), R("THR", w, w + 1), 0.84375, O.is_equal, O.subtract)
+        mm([(R(PC[k], q, 128, 16, n), by("NR", k, q), R("SEL"), True, True) for q in range(16)])
+        act(R("UM", u + 2 + t, u + 768, 6, n) if t else R("UR", r, r + 256, 2, n), c, F.Copy, scale=-1.0)
+        vtt(R("DM", u + 2 + t, u + 768, 6, n), c, blk("IDT", k, n), O.min)
+        if t == 2:
+            scan(R("MG", u, u + 768, 1, n), R("UM", u, u + 768, 1, n), R("DM", u, u + 768, 1, n), -BIG)
+            mm([(R(PD[k], 256, 256 + n), R("MG", u + 4, u + 768, 6, n), R("ID", 0, n, 1, n), True, True)])
+            act(ch("NI", k), R(PD[k], 256, 256 + n), F.Relu, bias=float(ZC))
+            vcp(IX(FX, R("AW" + p, c0 // 16, c0 // 16 + m)), ch("NI", k))
+        if t:
+            scan(R("S", r, r + 256, 1, n), R("UM", u + t - 1, u + 768, 3, n), R("DM", u + t - 1, u + 768, 3, n), -BIG)
+            b = R("S", r + 31, r + 256, 32, n)
+        else:
+            back = (r - 1) if r else None
+            scan(R("S", r + 255, back, -1, n), R("UR", r + 255, back, -1, n), R("DM", u + 767, (u - 1) if u else None, -3, n), -BIG)
+            b = R("S", r, r + 256, 32, n)
+        if t < 2:
+            act(R("DM", u + t, u + 768, 96, n), b, F.Copy)
+        x = R(PC[k], 128, 128 + 8 * m)
+        mm([(x, R("GI", 0, 128, 1, 8), R("NEG", 0, 8 * m, 1, 8), True, False)] +
+           [(R(PC[k], 128 + 8 * i, 136 + 8 * i), blk("CM", i, n), b, False, i == m - 1) for i in range(m)])
+        scan(R("SB", 64 * k, 64 * k + 8 * m), R("KS", 0, 8 * m), x, 0.0)
+        ob = R("OBW", 16 * t + c0 // 16, 16 * t + c0 // 16 + m)
+        vts(ob, R("SB", 64 * k + 7, 64 * k + 8 * m, 8), float(ZC), None, O.add)
+        if t < 2:
+            vcp(ch("OFS", k), IX(NB, ob))
+            act(ch("ZN", k), IX(NB, ob), F.Copy, bias=-float(ZC))
+            turn(k, ch("ZN", k))
+        if t == 0:
+            act(ch("NOH", k), IX(ZB, ob), F.Relu, acc=R("NFAIL", 4 * (w % 2) + k, 4 * (w % 2) + k + 1), bias=-999.0)
 
     def mark(w, k):
-        p, s = str(w % 2), str(k)
         c0, n = CH[k]
-        nb = (n + 31) // 32
-        mm([(B[6][:, c0:c0 + n], T.BD[:], ch("DJ", k), True, False), (B[6][:, c0:c0 + n], T.BDN[:], ch("SG", k), False, True)],
-           ["BD", "DJ", "BDN", "SG" + s], ["ps6"], 2 * n)
-        vtt(ch("TT", k), ch("NFH" + p, k), B[6][:, c0:c0 + n], O.max, ["NFH" + p], ["TT" + s, "ps6"], n, 1)
-        tk("V", cost(32 * nb, .5), ["TT" + s, "TTp"], ["TTT" + s], lambda: V.transpose(T.TTT[:, c0:c0 + 32 * nb], T.TT[:, c0:c0 + 32 * nb]))
-        lst, z = [], 240 + c0
-        for b in range(nb):
-            for h in range(2):
-                for e in range(2):
-                    i, a = 2 * h + e, c0 + 32 * b + 16 * e
-                    lst.append((B[6][:, z + h * nb + b:z + 32 * nb:2 * nb], T.HS[:, 128 * i:128 * i + 128], T.TTT[:, a:a + 16], e == 0, e == 1))
-        mm(lst, ["TTT" + s, "HS"], ["ps6"], 64 * len(lst))
-        vcp(T.FT[:, c0:c0 + 32 * nb], B[6][:, z:z + 32 * nb], [], ["FT" + s, "ps6"], 32 * nb)
+        nb, m, z = (n + 31) // 32, n // 16, 256 + c0
+        sg = R("SG", 8 * k, 8 * k + m)
+        act(sg, R("SB", 64 * k + 7, 64 * k + 8 * m, 8), F.Sign, bias=2000.0)
+        mm([(R(PM, z, z + 32 * nb), R("ID"), R("FT0", c0, c0 + 32 * nb), True, False)] +
+           [(R(PM, z + 2 * nb * q, z + 2 * nb * q + m), R("IK"), sg, False, q == 15) for q in range(16)])
+        vts(R("FT", c0, c0 + 32 * nb), R(PM, z, z + 32 * nb), 512.0, None, O.add)
         for q in range(16):
-            a = c0 + 2 * nb * q
-            act(T.FL[:, 0:WE].indirect(T.FT[:, a:a + n // 16]), T.C20[:, 0:n], F.Tanh, ["C20", "FT" + s], ["FL"], n, SCA)
+            j = c0 + 2 * nb * q
+            act(IX(R("FL%d" % (q % 2 if q < 15 or k < NC - 1 else 0)), R("FT", j, j + m)), R("CMK", 0, n), F.Silu)
+
+    def mark_tables():
+        copy("G", R("TT", 0, CAP), R("NFU"))
+        tk("V", cost(R("TTT"), None, 0.5), [R("TT")], [R("TTT")], lambda: V.transpose(T.TTT[:], T.TT[:]))
+        lst = []
+        for c0, n in CH:
+            nb = (n + 31) // 32
+            for i in range(nb):
+                for h in range(2):
+                    for e in range(2):
+                        j = c0 + 32 * i + 16 * e
+                        lst.append((R(PM, c0 + 2 * i + h, c0 + 32 * nb, 2 * nb), blk("HS", 2 * h + e), R("TTT", j, j + 16), e == 0, e == 1))
+        mm(lst)
+        act(R("FT0"), R(PM, 0, 256), F.Copy)
 
     def wave(w):
         p = str(w % 2)
         last = w == RO - 1
-        AW15 = T["AW" + p][:, 0:15]
+        AW = R("AW" + p, 0, 15)
         ghosts_in(w)
-        for k in range(3):
-            s = str(k)
-            c0, n = CH[k]
-            PA = B[k]
-            off = ch("NFU" + p, k)
-            if k in S_ACT:
-                act(ch("SF", k, 16), T.FX[:, 0:WE].indirect(off), F.Copy, ["FX", "NFU" + p], ["SF" + s], 16 * n, GA, bias=-float(ZC))
-                src, E, cyc = "SF", "EF", 64 * n
+        for c0, n, q in SEEDS:
+            out, src = R("ST", 16 * c0, 16 * (c0 + n)), IX(FX, R("NFU", c0, c0 + n))
+            if q == "A":
+                act(out, src, F.Copy, bias=-float(ZC))
             else:
-                vts(ch("ST", k, 16), T.FX[:, 0:WE].indirect(off), -float(ZC), None, O.add, None, ["FX", "NFU" + p], ["ST" + s], 16 * n, GA)
-                src, E, cyc = "ST", "EH", 16 * n
-            mm([(PA[:, 96:96 + n], T[E][:, 128 * q:128 * q + 128], by(src, k, q), q == 0, q == 15) for q in range(16)], [src + s, E], ["ps%d" % k], cyc)
-            vts(ch("OFS", k), PA[:, 96:96 + n], float(ZC), None, O.add, None, [], ["OFS" + s, "ps%d" % k], n)
-            act(ch("Z", k), PA[:, 96:96 + n], F.Copy, [], ["Z" + s, "ps%d" % k], n)
+                vts(out, src, -float(ZC), None, O.add)
+        for k in range(NC):
+            for c0, n in pieces(k, 0):
+                sd = R(PD[k], c0 - CH[k][0], c0 - CH[k][0] + n)
+                mm([(sd, blk("EH", q), R("ST", 16 * c0 + q, 16 * (c0 + n), 16), q == 0, q == 15) for q in range(16)])
+                vts(R("OFS", c0, c0 + n), sd, float(ZC), None, O.add)
+            act(ch("ZN", k), R(PD[k], 0, CH[k][1]), F.Copy)
+            turn(k, ch("ZN", k))
             test(w, k, 0)
             if not last:
                 mark(w, k)
         if not last:
-            tk("V", cost(CAP, SCA), ["NO%s%d" % (p, k) for k in range(3)] + ["AW" + p], ["EM"],
-               lambda: V.tensor_copy(T.EM[:, 0:WE].indirect(AW15), T["NO" + p][:]))
+            act(R("LFV"), R("NOH"), F.Copy, scale=2000.0 - 25 * 3 ** w)
+            act(IX(LF, AW), R("LFV"), F.Silu)
             nf = 4 * (w % 2)
-            mm([(B[6][:, 500:501], T.O16[:], T.NFAIL[:, nf + k:nf + k + 1], k == 0, k == 2) for k in range(3)],
-               ["O16"] + ["NFAIL%d%d" % (w % 2, k) for k in range(3)], ["ps6"], 768)
-            vcp(ICOL["EI"], B[6][:, 500:501], [], ["EI", "ps6"], 1)
-            vts(ICOL["EJ"], ICOL["EI"], 1, None, O.bitwise_and, None, ["EI"], ["EJ"], 1)
-            vts(T.THR[:, w + 1:w + 2], ICOL["EJ"], 7.0, 9.0, O.mult, O.add, ["EJ"], ["THR%d" % (w + 1)], 1)
-        for step in (1, 2):
-            up = 4096.0 * step
-            for k in range(3):
-                s, n = str(k), CH[k][1]
-                c = 16 * (step - 1) + CH[k][0] // 16
-                nbr, ot = T.NB[:, 0:WB].indirect(T.OBW[:, c:c + n // 16]), "OBW%d%s" % (step - 1, s)
-                vcp(ch("OFS", k), nbr, NBT + [ot], ["OFS" + s], n, GA)
-                act(ch("Z", k), nbr, F.Copy, NBT + [ot], ["Z" + s], n, GA, bias=-float(ZC))
-                act(ch("OK", k), ch("Z", k), F.Copy, ["Z" + s], ["OK" + s], n, bias=up + ZC)
-                test(w, k, step)
-        for k in range(3):
-            c0, n = CH[k]
-            tk("V", cost(n, SCA), ["NI%d" % k, "AW" + p], ["FX"],
-               lambda k=k, c0=c0, n=n: V.tensor_copy(T.FX[:, 0:WE].indirect(T["AW" + p][:, c0 // 16:(c0 + n) // 16]), ch("NI", k)))
+            mm([(R(PF, 500, 501), R("O16"), R("NFAIL", nf + k, nf + k + 1), k == 0, k == NC - 1) for k in range(NC)])
+            vcp(ICOL["EI"], R(PF, 500, 501))
+            vts(ICOL["EJ"], ICOL["EI"], 1, None, O.bitwise_and)
+            vts(R("THR", w + 1, w + 2), ICOL["EJ"], -8.0, 1544.0, O.mult, O.add)
+        hi, lo = R(PH, 0, CAP), R(PH, CAP, 2 * CAP)
+        mm([(hi, R("IN1"), R("XFN" + p), True, False), (hi, R("IN2"), R("NOH"), False, False), (hi, R("ID"), R("C2"), False, True),
+            (lo, R("IN1"), R("XFN" + p), True, False), (lo, R("IN1"), R("C2"), False, True)])
+        act(R("HL"), R(PH, 0, 2 * CAP), F.Identity, bias=R("THR", w, w + 1))
+        for t in (1, 2):
+            for k in range(NC):
+                test(w, k, t)
         if not last:
             ghosts_out(w + 1)
             front(w + 1)
-        XFP = T["XF" + p][:]
-        obt = ["OBW%d%d" % (x, k) for x in range(3) for k in range(3)]
-        f = [T.BF[:, 16 * x:16 * x + 15] for x in range(3)]
-        vcp(T.BF[:, 0:47], T.OBW[:, 0:47], obt, ["BF"], 47)
-        vts(T.BM[:, 0:47], T.OBW[:, 0:47], 0.0, None, O.is_equal, None, obt, ["BM"], 47)
-        vtt(T.BS[:, 0:15], f[0], T.BM[:, 16:31], O.mult, ["BF", "BM"], ["BS"], 15)
-        vtt(T.BS[:, 0:15], T.BS[:, 0:15], f[1], O.add, ["BF"], ["BS"], 15)
-        vtt(T.BS[:, 0:15], T.BS[:, 0:15], T.BM[:, 32:47], O.mult, ["BM"], ["BS"], 15)
-        vtt(T.BS[:, 0:15], T.BS[:, 0:15], f[2], O.add, ["BF"], ["BS"], 15)
-        vcp(T.BW2[:, 0:15], T.BS[:, 0:15], ["BS"], ["BW2"], 15)
-        tk("V", cost(CAP, GA), ZBT + ["BW2", "XF" + p], ["XD"],
-           lambda: V.tensor_tensor(T.XD[:], T.ZB[:, 0:WB].indirect(T.BW2[:, 0:15]), XFP, O.subtract))
-        vts(T.XC[:], T.XD[:], -2.0, 2.0, O.max, O.min, ["XD"], ["XC"], CAP, .5)
-        SC = B[5][:, 0:CAP]
-        act(SC, T["NO" + p][:], F.Copy, ["NO%s%d" % (p, k) for k in range(3)], ["ps5"], CAP, scale=-1.0, bias=1.0)
-        vtt(SC, SC, T.XC[:], O.mult, ["XC"], ["ps5"], CAP, 1)
-        vtt(T.XN[:], SC, XFP, O.add, ["XF" + p], ["XN", "ps5"], CAP, 1)
-        tk("V", cost(CAP, SCA), ["XN", "AW" + p], ["XA"], lambda: V.tensor_copy(T.XA[:, 0:WE].indirect(AW15), T.XN[:]))
+        vtt(R("XT"), IX(ZB, R("OBW", 32, 47)), R("HL", 0, CAP), O.min)
+        vtt(IX(XA, AW), R("XT"), R("HL", CAP, 2 * CAP), O.max)
 
+    front(0)
+    for i in range(2):
+        a, b = (0, NB_HALF) if i == 0 else (NB_HALF, OB - 1)
+        copy("G", R("NB", EXT + a, EXT + b), R("LN", a, b))
     for w in range(RO):
         wave(w)
-    vts(T.YM[:], T.FX[:, 0:VA], 0.0, 2559.0 + OFF, O.is_equal, O.mult, ["FX"], ["YM"], VA)
-    act(T.Y1[:], T.FX[:, 0:VA], F.Copy, ["FX"], ["Y1"], VA, bias=-float(OFF))
-    vtt(T.YO[:], T.Y1[:], T.YM[:], O.add, ["Y1", "YM"], ["YO"], VA)
-    tk("S", 0.1, ["YO"], ["yf"], lambda: SY.dma_start(T.yf[:], T.YO[:]), sem="oy", val=16)
-    tk("S", 0.1, ["XA"], ["ya"], lambda: SY.dma_start(T.ya[:], T.XA[:, 0:VA]), sem="ox", val=16)
+    vts(R("Y1"), R("FX", 0, VA), -float(OFF), None, O.add)
+    for i in range(2):
+        a, b = 320 * i, 320 * i + 320
+        act(R(PD[i], 0, 320), R("FX", a, b), F.Copy, scale=-1000.0, bias=2559.0)
+        vtt(R("YO", a, b), R(PD[i], 0, 320), R("Y1", a, b), O.max)
+    act(R("YA"), R("XA", 0, VA), F.Copy)
+    tk("S", 0.1, [R("YO")], [TAG("yf")], lambda: SY.dma_start(T.yf[:], T.YO[:]), sem="oy", val=16)
+    tk("S", 0.1, [R("YA")], [TAG("ya")], lambda: SY.dma_start(T.ya[:], T.YA[:]), sem="ox", val=16)
     return tasks, sent
 
 
-LAT = {"V": 0.05, "A": 0.08, "P": 0.1, "G": 0.1, None: 0.0}
-EPS = 0.06
+LAT = {"V": 0.12, "A": 0.15, "P": 0.15, "G": 0.2, None: 0.0}
+EPS = (0.05, 0.1, 0.2, 0.3)
+TURNS = 6
+CASES = ((1.0, 1.0, 1.0, 0.13), (0.9, 0.9, 0.9, 0.2), (0.8, 1.5, 1.1, 0.13), (1.35, 0.6, 1.1, 0.13))
 BONUS = {}
+WAW = True
 
 
-def plan(tasks):
-    n = len(tasks)
-    succ = [[] for _ in range(n)]
-    for i, t in enumerate(tasks):
-        for d in t["deps"]:
-            succ[d].append(i)
-    lat = [LAT[t["q"]] if t["sem"] is None or t["q"] is None else 2.2 for t in tasks]
-    prio = [0.0] * n
-    for i in range(n - 1, -1, -1):
-        prio[i] = tasks[i]["dur"] + lat[i] + max([prio[j] for j in succ[i]] + [0.0])
-    prio = [p + BONUS.get(t["tag"], 0.0) for p, t in zip(prio, tasks)]
-    left = [len(t["deps"]) for t in tasks]
-    est, fin, free, order = [0.0] * n, [0.0] * n, {}, []
-    ready = {}
+def span(qs, dur, pred, order, wake):
+    fin, free = [0.0] * len(qs), {}
+    for i in order:
+        t = max([fin[d] + (gap if gap > 1 or gap == 0 else wake) for d, gap in pred[i]] + [0.0])
+        if qs[i] is not None:
+            t = max(t, free.get(qs[i], 0.0))
+            free[qs[i]] = t + dur[i]
+        fin[i] = t + dur[i]
+    return max(fin)
+
+
+def sweep(qs, dur, succ, prio, eps):
+    n = len(qs)
+    left = [0] * n
+    for i in range(n):
+        for j, gap in succ[i]:
+            left[j] += 1
+    est, fin, free, order, ready = [0.0] * n, [0.0] * n, {}, [], {}
     for i in range(n):
         if left[i] == 0:
-            ready.setdefault(tasks[i]["q"], []).append(i)
+            ready.setdefault(qs[i], []).append(i)
     while len(order) < n:
         best = None
         for q, lst in ready.items():
             if not lst:
                 continue
             f = free.get(q, 0.0) if q is not None else 0.0
-            t0 = min(max(f, est[i]) for i in lst)
-            c = max((i for i in lst if max(f, est[i]) <= t0 + EPS), key=lambda i: prio[i])
+            t0 = max(f, min([est[i] for i in lst]))
             if best is None or t0 < best[0]:
-                best = (t0, q, c)
-        t0, q, i = best
+                best = (t0, q)
+        t0, q = best
+        now = [i for i in ready[q] if est[i] <= t0 + eps]
+        i = max(now, key=lambda i: prio[i])
+        soon = [j for j in ready[q] if t0 + eps < est[j] < t0 + dur[i] and prio[j] > prio[i]]
+        if soon and q is not None:
+            j = max(soon, key=lambda j: prio[j])
+            if max(est[j] + prio[j], est[j] + dur[j] + prio[i]) < max(t0 + prio[i], t0 + dur[i] + prio[j]) - eps:
+                fit = [x for x in now if t0 + dur[x] <= est[j] + eps]
+                i = max(fit, key=lambda x: prio[x]) if fit else j
         ready[q].remove(i)
-        fin[i] = (est[i] if q is None else max(t0, est[i])) + tasks[i]["dur"]
+        fin[i] = (est[i] if q is None else max(t0, est[i])) + dur[i]
         if q is not None:
             free[q] = fin[i]
         order.append(i)
-        for j in succ[i]:
-            est[j] = max(est[j], fin[i] + lat[i])
+        for j, gap in succ[i]:
+            est[j] = max(est[j], fin[i] + gap)
             left[j] -= 1
             if left[j] == 0:
-                ready.setdefault(tasks[j]["q"], []).append(j)
+                ready.setdefault(qs[j], []).append(j)
     return order, fin
+
+
+PLAN = []
+
+
+def plan(tasks):
+    if PLAN:
+        return PLAN[0]
+    n = len(tasks)
+    qs, dur = [t["q"] for t in tasks], [t["dur"] for t in tasks]
+    succ, pred = [[] for _ in range(n)], [[] for _ in range(n)]
+    for i, t in enumerate(tasks):
+        for d, hard in t["deps"].items():
+            u = tasks[d]
+            gap = LAT[u["q"]] if u["sem"] is None or u["q"] is None else 0.0 if u["sem"] == "none" else 2.0
+            if not hard and u["q"] == t["q"] and u["sem"] is None:
+                gap = 0.0
+            succ[d].append((i, gap))
+            pred[i].append((d, gap))
+    way = [0.0] * n
+    for i in range(n - 1, -1, -1):
+        way[i] = dur[i] + max([way[j] + gap for j, gap in succ[i]] + [0.0])
+    cases = [([d * (a if t["kind"] == 1 else b if t["kind"] == 2 else c) for d, t in zip(dur, tasks)], wake) for a, b, c, wake in CASES]
+    best = None
+    for eps in EPS:
+        prio = way
+        for _ in range(TURNS):
+            order, fin = sweep(qs, dur, succ, [x + BONUS.get(t["tag"], 0.0) for x, t in zip(prio, tasks)], eps)
+            end = sum(span(qs, d, pred, order, wake) for d, wake in cases) / len(cases)
+            if best is None or end < best[2]:
+                best = (order, fin, end)
+            prio = sweep(qs, dur, pred, fin, eps)[1]
+    PLAN.append(best)
+    return best
 
 
 def emit(g, T, tasks, order):
@@ -527,7 +641,7 @@ def rank_program(g, core, T, topo):
         relay_program(g, core, T, topo, msgs)
         return
     tasks, sent = build(g, core, T, topo, msgs)
-    order, _fin = plan(tasks)
+    order = plan(tasks)[0]
     final = emit(g, T, tasks, order)
     for s, v in final.items():
         g.wait_ge(T.sem[s], v)

@@ -13,16 +13,20 @@ CH = ((0, 128), (128, 112))
 SEEDS = ((0, 64, "V"), (64, 64, "A"), (128, 112, "A"))
 XRQ = ((0, 128, "V"), (128, 112, "G"))
 CUTS = ((64,), (), ())
+ALT = (((32, 32), (0, 0), (0, 0)), ((32, 32), (32, 32), (32, 32)))
+WHO = {"FT": "A", "OB": "VVV", "OFS": "VVV", "AW": "A", "GW": "A", "B": "G", "ZN": "GG", "FH": "AG", "NFU": "A", "LF": "A"}
+MV = (0, 0)
+NFW = (0, 0, 0, 0, 0)
 NC = len(CH)
 
 SCRATCH = {}
 _L = {
-    "bfloat16": "ZB:2576 XAB:640 Q:3840 RX:640 YA:640",
-    "float16": "ONE:1024 BD:128 BDT:128 ID:128 IK:128 IN1:128 IN2:128 SLM:128 SLN:128 TRIX:128 GI:128 NEG:64 NGC:64 SEL:8 EH:2048 CM:1024 "
-               "HS:512 C2:240 MB:176 FH0:640 FH1:640 LFH:640 EL:40 LWH:240 FT0:256 SG:24 NOH:240 XFN0:240 XFN1:240 TT:256 TTT:256 XR0:3840 XR1:3840 "
+    "bfloat16": "ZB:2576 XAB:640 Q:3840 RX:640 YA:1264 GB:1024 XN:240 FL2:2288",
+    "float16": "ONE:1024 BD:128 BDT:128 ID:128 IK:128 IN1:128 IN2:128 SLM:128 SLN:128 TRIX:128 TRIY:128 GI:128 NEG:64 NGC:64 SEL:8 EH:2048 CM:1024 "
+               "HS:512 C2:240 MB:176 FH0:640 FH1:640 LFH:640 EL:40 LWH:240 GR:240 FT0:256 SG:24 NOH:240 XFN0:240 XFN1:240 TT:256 TTT:256 XR0:3840 XR1:3840 "
                "NR:3840 ST:3840 ZN:240 IDT:384 UR:768 UM:2304 DM:2304 S:768 MG:2304",
-    "float32": "NB:2576 FX:1264 FL0:2288 FL1:2288 LF:1264 LW:1280 XA:1264 MF:176 FA:176 O16:128 COL:8 MQ:16 MQI:16 KS:64 SB:192 IOTAF:640 DUMA0:40 "
-               "DUMPA:40 CMK:128 ONE40:40 CUM:40 PO1:40 PO2:40 THR:8 NFAIL:16 LFV:240 HL:480 XT:240 NI:240 Y1:640 YO:640",
+    "float32": "NB:2576 FX:2528 INV:1264 GK:384 NBF:1264 IDF:128 ZF:240 FL0:2288 FL1:2288 LF:1264 LW:1280 XA:1264 MF:176 FA:176 O16:128 COL:8 MQ:16 MQI:16 KS:64 SB:192 IOTAF:640 DUMA0:40 "
+               "DUMPA:40 CMK:128 ONE40:80 CUM:80 THR:8 NFAIL:16 LFV:240 HL:480 XT:240 NI:240 Y1:640 YO:1264",
     "int32": "NBB:1280 NBA:640 NFW:1280 F0I:176 BDI:24 ICOL:4",
     "uint16": "NBX:1280 LN:1280 BDU:24 POU:40 FT:256 RN:640 GHS:1920 RG:1920 LG:1920 NFU:240 AW0:16 AW1:16 OFS:240 OBW:48",
 }
@@ -33,11 +37,12 @@ for _i in range(8):
     SCRATCH["ps%d" % _i] = ("psum", [128, 512], "float32")
 PC = ["ps%d" % k for k in range(NC)]
 PD = ["ps%d" % (NC + k) for k in range(NC)]
-PF, PM, PH = "ps6", "ps7", "ps5" if NC < 3 else "ps6"
+PF, PM, PH = "ps6", "ps7", "ps5"
+PA = ["ps4", "ps5"]
 
 LOADS = ["xb", "f0", "bd", "nba", "xa", "nbb"]
 SEMAPHORES = ["sV", "sA", "sP", "sG", "ls", "oy", "ox", "rx", "rn", "ax0", "ax1", "an0", "an1"] + \
-    ["l" + n for n in LOADS] + ["rg%d" % w for w in range(RO)] + ["ag%d" % w for w in range(RO)]
+    ["l" + n for n in LOADS] + ["rg", "ag"] + [x + "%d%d" % (w, k) for x in ("rg", "ag") for w in range(RO - 1) for k in range(NC)]
 
 
 def relays(topo, src, dst):
@@ -56,12 +61,20 @@ def messages(topo, cores):
             out.append((src, rb[i], prev, "RX", (0, w[i]), "rx", "ZB", (EXT + a, EXT + b), "ax%d" % i, "ZB", (OFF + a, OFF + b)))
         for i in range(2):
             a, b = i * NB_HALF, i * NB_HALF + w[i]
-            out.append((src, rb[2 + i], prev, "RN", (0, w[i]), "rn", "LN", (a, b), "an%d" % i, "NBX", (a, b)))
+            m = (src, rb[3 - i], prev, "RN", (0, w[i]), "rn", "LN", (a, b), "an%d" % i, "NBX", (a, b))
+            if i:
+                out.append((src, relays(topo, src, nxt)[2], nxt, "RG", (0, GH), "rg", "LG", (0, GH), "ag", "GHS", (0, GH)))
+            out.append(m)
         rg = relays(topo, src, nxt)
-        for k in range(RO):
-            s = (k * GH, (k + 1) * GH)
-            out.append((src, rg[0], nxt, "RG", s, "rg%d" % k, "LG", s, "ag%d" % k, "GHS", s))
+        for v in range(RO - 1):
+            for k in range(NC):
+                s = (slot(v, k), slot(v, k) + 8 + CH[k][1])
+                out.append((src, rg[k % 2], nxt, "RG", s, "rg%d%d" % (v, k), "LG", s, "ag%d%d" % (v, k), "GHS", s))
     return out
+
+
+def slot(w, k):
+    return GH + 136 * (NC * w + k)
 
 
 def send(g, topo, src, dst, dbuf, dcol, sbuf, scol, T, rsem):
@@ -87,7 +100,7 @@ FLY = 5.0
 
 
 def build(g, core, T, topo, msgs):
-    tasks, rec, bank = [], {}, {}
+    tasks, rec, bank, part, seen = [], {}, {}, ["s", -1], {}
     V, A, P, SY = g.vector, g.scalar, g.tensor, g.sync
 
     def R(name, a=0, b=None, s=1, n=128):
@@ -119,24 +132,25 @@ def build(g, core, T, topo, msgs):
                             deps[r[2]] = True
                         elif isw:
                             deps.setdefault(r[2], False)
-        for x in rd + wr:
-            if x["ps"]:
-                last = bank.setdefault(x["f"][0], {})
-                for e, t in last.items():
-                    if e != q:
-                        deps[t] = True
-        for x in rd + wr:
-            if x["ps"]:
-                bank[x["f"][0]][q] = i
+        for name in {x["f"][0] for x in rd + wr if x["ps"]}:
+            e, run, before = bank.get(name, (q, [], []))
+            if e != q:
+                run, before = [], run
+            for t in before:
+                deps[t] = True
+            bank[name] = (q, run + [i], before)
         for f in writes:
-            if f[3]:
-                rec[f[0]] = [r for r in rec.get(f[0], []) if r[1] & ~f[2]]
+            rec[f[0]] = [r for r in rec.get(f[0], []) if r[0] & ~f[1]]
         for f in writes:
             rec.setdefault(f[0], []).append((f[1], f[2], i, q, True))
         for f in reads:
             rec.setdefault(f[0], []).append((f[1], f[2], i, q, False))
         kind = 2 if wr[0]["o"] else 1 if rd and rd[0]["o"] else 0
-        tasks.append(dict(q=q, dur=dur, deps=deps, fn=fn, sem=sem, val=val, kind=kind, tag=wr[0]["f"][0] + (q or "")))
+        tag = wr[0]["f"][0] + (q or "")
+        role = "".join(c for c in tag if c.isalpha()) + part[0]
+        seen[(part[1], role)] = seen.get((part[1], role), 0) + 1
+        tasks.append(dict(q=q, dur=dur, deps=deps, fn=fn, sem=sem, val=val, kind=kind, tag=tag, role=role,
+                          key=(part[1], role + str(seen[(part[1], role)]))))
 
     def ap(x):
         return x["ap"] if isinstance(x, dict) else x
@@ -201,6 +215,12 @@ def build(g, core, T, topo, msgs):
         else:
             asel(out, a, [[0, out["n"]]], O.is_ge, 0, 0)
 
+    def places(q, out, a, x):
+        if q == "V":
+            vts(out, a, x, None, O.add)
+        else:
+            act(out, a, F.Relu, bias=x)
+
     def ch(name, k, w=1):
         return R(name, w * CH[k][0], w * (CH[k][0] + CH[k][1]))
 
@@ -213,10 +233,11 @@ def build(g, core, T, topo, msgs):
     def load(q, name, out):
         e = SY if q == "S" else A
         tk(q, 0.1, [], [out], lambda: e.dma_start(out["ap"], T[name][:]), sem="l" + name, val=16)
+        tasks[-1]["lat"] = 1.5 + out["n"] * (1 if out["two"] else 2) * 0.0013
 
     COL = {x: R("COL", i, i + 1) for i, x in enumerate(("PF",))}
     ICOL = {x: R("ICOL", i, i + 1) for i, x in enumerate(("PI", "PJ", "EI", "EJ"))}
-    ZB, NB, FX, XA, LF = R("ZB"), R("NB"), R("FX"), R("XA"), R("LF")
+    ZB, NB, FX, XA, LF = R("ZB"), R("NB"), R("FX", 0, WE), R("XA"), R("LF")
 
     vms(R("ZB", 0, 16), 1000.0)
     vms(R("ZB", NULLC, WB), 1000.0)
@@ -229,6 +250,7 @@ def build(g, core, T, topo, msgs):
 
     mine = [m for m in msgs if m[0] == core]
     inb = {m[8]: m for m in msgs if m[2] == core}
+    by_sem = {m[8]: m for m in mine}
     sent = [0]
 
     def remote(m):
@@ -253,6 +275,10 @@ def build(g, core, T, topo, msgs):
     iota(R("DUMA0"), [[16, 40]], VA)
     asel(R("SLM"), R("BD"), [[-1, 128]], O.is_gt, 0, 1)
     iota(R("IOTAF"), [[1, VA]], 32)
+    iota(R("NBF", 1024, WE), [[1, CAP]], 1024)
+    vcp(R("NBF", 0, VA), R("NBA"))
+    act(R("IDF"), R("ID"), F.Copy)
+    vms(R("FL2", 0, VA), 0.0)
     asel(R("GI"), one, [[-1, 8], [0, 16]], O.is_equal, 0, 1)
     vms(R("NGC"), -2 * BIG)
     asel(R("NEG"), R("NGC"), [[0, 8], [-1, 8]], O.not_equal, 0, 1)
@@ -277,8 +303,9 @@ def build(g, core, T, topo, msgs):
     vts(R("SEL"), R("BD", 0, 128, 16), 4096.0, None, O.mult)
     for x, c in (("IK", -512.0), ("IN1", -1.0), ("IN2", -2.0)):
         vts(R(x), R("ID"), c, None, O.mult)
-    vts(R("SLN"), R("ID"), -2048.0, None, O.mult)
-    vtt(R("TRIX"), R("SLN"), R("SLM"), O.subtract)
+    vts(R("SLN"), R("ID"), 2047.0, None, O.mult)
+    vtt(R("TRIY"), R("SLN"), R("SLM"), O.add)
+    vtt(R("TRIX"), R("BD"), R("TRIY"), O.subtract)
     vms(R("HS"), 0.0)
     for h in range(2):
         for e in range(2):
@@ -310,18 +337,25 @@ def build(g, core, T, topo, msgs):
         vms(R("UR", r, r + 256), BIG)
         vms(R("UR", r + 31, r + 256, 32), -BIG)
 
-    def ghosts_out(w):
-        vts(R("GHS", w * GH, (w + 1) * GH), IX(R("FX", 0, VA), R("BDU")), float(OB + 8), -float(OB), O.max, O.add)
-        remote(mine[4 + w])
-
     def ghosts_in(w):
-        arrive("ag%d" % w, FLY if w else FLY + 1.5)
-        vcp(R("FX", VA, VA + GH), R("LG", w * GH, (w + 1) * GH))
+        if w == 0:
+            arrive("ag", FLY + 1.5)
+            vcp(R("FX", VA, VA + GH), R("LG", 0, GH))
+            return
+        for k in range(NC):
+            s, n = slot(w - 1, k), CH[k][1]
+            arrive("ag%d%d" % (w - 1, k), FLY - 0.5)
+            vcp(IX(R("FX"), R("LG", s, s + n // 16)), R("LG", s + 8, s + 8 + n))
 
-    ghosts_out(0)
+    vts(R("GHS", 0, GH), IX(R("FX", 0, VA), R("BDU")), float(OB + 8), -float(OB), O.max, O.add)
+    remote(by_sem["ag"])
     vts(R("NBX"), R("NBB"), EXT, NULLC, O.add, O.min)
-    for m in mine[2:4]:
-        remote(m)
+    for i in range(2):
+        remote(by_sem["an%d" % i])
+    iota(R("INV"), [[1, WE]], WE - 1024)
+    iota(R("GK"), [[1, GH]], VA - 1024)
+    vcp(IX(R("INV"), R("BDU")), R("GK"))
+    vms(R("GHS", GH, None), 0)
     vts(R("NB", OFF, EXT), R("NBB"), OFF, None, O.add)
     for i in range(2):
         arrive("ax%d" % i, FLY + 3.0)
@@ -332,6 +366,7 @@ def build(g, core, T, topo, msgs):
         p = str(w % 2)
         AW = R("AW" + p, 0, 15)
         el = R(PF, 0, 40)
+        part[0] = "f"
         iota(R("LW", 0, CAP), [[1, CAP]], 1024 + 32)
         if w == 0:
             m = S0 // 16
@@ -345,33 +380,43 @@ def build(g, core, T, topo, msgs):
             copy("G", R("LFH"), R("LF", 0, VA))
             mm([(el, blk("EH", q), R("LFH", q, VA, 16), q == 0, False) for q in range(16)])
             for i in (1, 0):
-                act(R("FH%d" % i), R("FL%d" % i, 0, VA), F.Copy)
+                if i and sum(MV):
+                    mm([(el, blk("EH", q), R("FL2", q, VA, 16), False, False) for q in range(16)])
+                copy(WHO["FH"][i], R("FH%d" % i), R("FL%d" % i, 0, VA))
                 mm([(el, blk("EH", q), R("FH%d" % i, q, VA, 16), False, i == 0 and q == 15) for q in range(16)])
             vts(R("EL"), el, 2000.0, None, O.is_ge)
-        mm([(R(PF, 40, 80), R("BD"), R("EL"), True, True), (R(PF, 80, 120), R("TRIX"), R("EL"), True, True)])
-        scan(R("CUM"), R("ONE40"), R(PF, 40, 80), 2047.0, O.mult, O.add)
-        vtt(R("PO1"), R("CUM"), R(PF, 80, 120), O.add)
-        vtt(R("PO2"), R("PO1"), R("DUMPA"), O.min)
-        vcp(R("POU"), R("PO2"))
-        iota(R("NFW", 0, CAP), [[1, CAP]], 1024)
-        vcp(IX(R("NFW"), R("POU")), R("NBA"))
-        vcp(R("NFU"), R("NFW", 0, CAP))
+        mm([(R(PF, 40, 120, 2), R("TRIX"), R("EL"), True, True), (R(PF, 41, 120, 2), R("TRIY"), R("EL"), True, True)])
+        scan(R("CUM"), R("ONE40"), R(PF, 40, 120), 2046.0, O.mult, O.add)
+        vtt(R("POU"), R("CUM", 0, 80, 2), R("DUMPA"), O.min)
+        if NFW[w]:
+            iota(R("NFW", 0, CAP), [[1, CAP]], 1024)
+            vcp(IX(R("NFW"), R("POU")), R("NBA", 0, VA))
+            vcp(R("NFU"), R("NFW", 0, CAP))
         act(IX(R("LW"), R("POU")), R("IOTAF"), F.Silu)
         act(R("LWH"), R("LW", 0, CAP), F.Copy, bias=-32.0)
         mm([(R(PF, 120, 135), blk("EH", q), R("LWH", q, CAP, 16), q == 0, q == 15) for q in range(16)])
-        vcp(AW, R(PF, 120, 135))
+        places(WHO["AW"], AW, R(PF, 120, 135), 0.0)
+        if not NFW[w]:
+            copy(WHO["NFU"], R("NFU"), IX(R("NBF"), AW))
         act(R("XFN" + p), IX(XA, AW), F.Identity, scale=-1.0, bias=R("THR", w, w + 1))
         for c0, n, e in XRQ:
             for q in range(16):
                 copy(e, R("XR" + p, 16 * c0 + q, 16 * (c0 + n), 16), R("XFN" + p, c0, c0 + n))
         if w < RO - 1:
             mark_tables()
+            act(R("GR"), IX(R("INV"), AW), F.Copy)
+            mm([(R(PF, 140, 155), blk("EH", q), R("GR", q, CAP, 16), q == 0, q == 15) for q in range(16)])
+            for k in range(NC):
+                c0, n = CH[k]
+                places(WHO["GW"], R("GHS", slot(w, k), slot(w, k) + n // 16), R(PF, 140 + c0 // 16, 140 + (c0 + n) // 16), 1024.0)
             iota(R("CMK"), [[0, 128]], 30 * 3 ** w)
 
     def pieces(k, t):
         c0, n = CH[k]
         cut = [c0] + [x for x in CUTS[t] if c0 < x < c0 + n] + [c0 + n]
         return [(a, b - a) for a, b in zip(cut, cut[1:])]
+
+    turns = [0]
 
     def turn(k, z):
         n = CH[k][1]
@@ -382,9 +427,20 @@ def build(g, core, T, topo, msgs):
         p = str(w % 2)
         c0, n = CH[k]
         m, u, r = n // 16, 768 * k, 256 * k
+        part[0] = "t%d%d" % (t, k)
         c = R(PC[k], 0, 128, 1, n)
+        cut = c0 + n - ALT[w == RO - 1][t][k]
         for a, b in pieces(k, t):
-            vtt(R("Q", 16 * a, 16 * (a + b)), IX(ZB, R("OFS", a, a + b)), R("XR" + p, 16 * a, 16 * (a + b)), O.add)
+            b = min(a + b, cut)
+            if a < b:
+                vtt(R("Q", 16 * a, 16 * b), IX(ZB, R("OFS", a, b)), R("XR" + p, 16 * a, 16 * b), O.add)
+        for a in range(cut, c0 + n, 32):
+            b, i = min(a + 32, c0 + n), turns[0] % 2
+            turns[0] += 1
+            gb, pa = R("GB", 512 * i, 512 * i + 16 * (b - a)), R(PA[i], 0, 16 * (b - a))
+            act(gb, IX(ZB, R("OFS", a, b)), F.Copy)
+            mm([(pa, R("ID"), R("XR" + p, 16 * a, 16 * b), True, False), (pa, R("ID"), gb, False, True)])
+            act(R("Q", 16 * a, 16 * b), pa, F.Copy)
         vts(ch("NR", k, 16), ch("Q", k, 16), R("THR", w, w + 1), 0.84375, O.is_equal, O.subtract)
         mm([(R(PC[k], q, 128, 16, n), by("NR", k, q), R("SEL"), True, True) for q in range(16)])
         act(R("UM", u + 2 + t, u + 768, 6, n) if t else R("UR", r, r + 256, 2, n), c, F.Copy, scale=-1.0)
@@ -392,8 +448,16 @@ def build(g, core, T, topo, msgs):
         if t == 2:
             scan(R("MG", u, u + 768, 1, n), R("UM", u, u + 768, 1, n), R("DM", u, u + 768, 1, n), -BIG)
             mm([(R(PD[k], 256, 256 + n), R("MG", u + 4, u + 768, 6, n), R("ID", 0, n, 1, n), True, True)])
-            act(ch("NI", k), R(PD[k], 256, 256 + n), F.Relu, bias=float(ZC))
-            vcp(IX(FX, R("AW" + p, c0 // 16, c0 // 16 + m)), ch("NI", k))
+            new, aw = R(PD[k], 256, 256 + n), R("AW" + p, c0 // 16, c0 // 16 + m)
+            if w < RO - 1:
+                vts(R("GHS", slot(w, k) + 8, slot(w, k) + 8 + n), new, 0.0, 8.0, O.max, O.add)
+                remote(by_sem["ag%d%d" % (w, k)])
+                act(ch("NI", k), new, F.Relu, bias=float(ZC))
+                vcp(IX(FX, aw), ch("NI", k))
+            else:
+                act(ch("NI", k), new, F.Copy, bias=float(ZC - OFF))
+                vts(ch("LFV", k), ch("NI", k), -10.0, 2559.0, O.mult, O.min)
+                vtt(IX(R("YO"), aw), ch("NI", k), ch("LFV", k), O.max)
         if t:
             scan(R("S", r, r + 256, 1, n), R("UM", u + t - 1, u + 768, 3, n), R("DM", u + t - 1, u + 768, 3, n), -BIG)
             b = R("S", r + 31, r + 256, 32, n)
@@ -402,17 +466,22 @@ def build(g, core, T, topo, msgs):
             scan(R("S", r + 255, back, -1, n), R("UR", r + 255, back, -1, n), R("DM", u + 767, (u - 1) if u else None, -3, n), -BIG)
             b = R("S", r, r + 256, 32, n)
         if t < 2:
-            act(R("DM", u + t, u + 768, 96, n), b, F.Copy)
+            copy(WHO["B"], R("DM", u + t, u + 768, 96, n), b)
         x = R(PC[k], 128, 128 + 8 * m)
         mm([(x, R("GI", 0, 128, 1, 8), R("NEG", 0, 8 * m, 1, 8), True, False)] +
            [(R(PC[k], 128 + 8 * i, 136 + 8 * i), blk("CM", i, n), b, False, i == m - 1) for i in range(m)])
         scan(R("SB", 64 * k, 64 * k + 8 * m), R("KS", 0, 8 * m), x, 0.0)
         ob = R("OBW", 16 * t + c0 // 16, 16 * t + c0 // 16 + m)
-        vts(ob, R("SB", 64 * k + 7, 64 * k + 8 * m, 8), float(ZC), None, O.add)
+        places(WHO["OB"][t], ob, R("SB", 64 * k + 7, 64 * k + 8 * m, 8), float(ZC))
         if t < 2:
-            vcp(ch("OFS", k), IX(NB, ob))
-            act(ch("ZN", k), IX(NB, ob), F.Copy, bias=-float(ZC))
-            turn(k, ch("ZN", k))
+            copy(WHO["OFS"][t + 1], ch("OFS", k), IX(NB, ob))
+            if WHO["ZN"][t] == "A":
+                act(ch("ZN", k), IX(NB, ob), F.Copy, bias=-float(ZC))
+                turn(k, ch("ZN", k))
+            else:
+                copy("G", ch("ZF", k), ch("OFS", k))
+                mm([(R(PD[k], 128, 256, 1, n), ch("ZF", k), R("IDF"), True, True)])
+                act(blk("IDT", k, n), R(PD[k], 128, 256, 1, n), F.Copy, bias=-float(ZC))
         if t == 0:
             act(ch("NOH", k), IX(ZB, ob), F.Relu, acc=R("NFAIL", 4 * (w % 2) + k, 4 * (w % 2) + k + 1), bias=-999.0)
 
@@ -423,10 +492,13 @@ def build(g, core, T, topo, msgs):
         act(sg, R("SB", 64 * k + 7, 64 * k + 8 * m, 8), F.Sign, bias=2000.0)
         mm([(R(PM, z, z + 32 * nb), R("ID"), R("FT0", c0, c0 + 32 * nb), True, False)] +
            [(R(PM, z + 2 * nb * q, z + 2 * nb * q + m), R("IK"), sg, False, q == 15) for q in range(16)])
-        vts(R("FT", c0, c0 + 32 * nb), R(PM, z, z + 32 * nb), 512.0, None, O.add)
+        places(WHO["FT"], R("FT", c0, c0 + 32 * nb), R(PM, z, z + 32 * nb), 512.0)
         for q in range(16):
             j = c0 + 2 * nb * q
-            act(IX(R("FL%d" % (q % 2 if q < 15 or k < NC - 1 else 0)), R("FT", j, j + m)), R("CMK", 0, n), F.Silu)
+            if q < MV[k]:
+                vcp(IX(R("FL2"), R("FT", j, j + m)), R("CMK", 0, n))
+            else:
+                act(IX(R("FL%d" % (q % 2 if q < 15 or k < NC - 1 else 0)), R("FT", j, j + m)), R("CMK", 0, n), F.Silu)
 
     def mark_tables():
         copy("G", R("TT", 0, CAP), R("NFU"))
@@ -446,7 +518,15 @@ def build(g, core, T, topo, msgs):
         p = str(w % 2)
         last = w == RO - 1
         AW = R("AW" + p, 0, 15)
+        part[0], part[1] = "w", w
         ghosts_in(w)
+        if last:
+            act(R("Y1"), R("FX", 0, VA), F.Copy, bias=-float(OFF))
+            for i in range(2):
+                a, b = 320 * i, 320 * i + 320
+                act(R(PM, 0, 320), R("FX", a, b), F.Copy, scale=-1000.0, bias=2559.0)
+                vtt(R("YO", a, b), R(PM, 0, 320), R("Y1", a, b), O.max)
+            act(R("YA", 0, VA), R("XA", 0, VA), F.Copy)
         for c0, n, q in SEEDS:
             out, src = R("ST", 16 * c0, 16 * (c0 + n)), IX(FX, R("NFU", c0, c0 + n))
             if q == "A":
@@ -457,7 +537,7 @@ def build(g, core, T, topo, msgs):
             for c0, n in pieces(k, 0):
                 sd = R(PD[k], c0 - CH[k][0], c0 - CH[k][0] + n)
                 mm([(sd, blk("EH", q), R("ST", 16 * c0 + q, 16 * (c0 + n), 16), q == 0, q == 15) for q in range(16)])
-                vts(R("OFS", c0, c0 + n), sd, float(ZC), None, O.add)
+                places(WHO["OFS"][0], R("OFS", c0, c0 + n), sd, float(ZC))
             act(ch("ZN", k), R(PD[k], 0, CH[k][1]), F.Copy)
             turn(k, ch("ZN", k))
             test(w, k, 0)
@@ -465,7 +545,10 @@ def build(g, core, T, topo, msgs):
                 mark(w, k)
         if not last:
             act(R("LFV"), R("NOH"), F.Copy, scale=2000.0 - 25 * 3 ** w)
-            act(IX(LF, AW), R("LFV"), F.Silu)
+            if WHO["LF"] == "A":
+                act(IX(LF, AW), R("LFV"), F.Silu)
+            else:
+                vcp(IX(LF, AW), R("LFV"))
             nf = 4 * (w % 2)
             mm([(R(PF, 500, 501), R("O16"), R("NFAIL", nf + k, nf + k + 1), k == 0, k == NC - 1) for k in range(NC)])
             vcp(ICOL["EI"], R(PF, 500, 501))
@@ -479,10 +562,15 @@ def build(g, core, T, topo, msgs):
             for k in range(NC):
                 test(w, k, t)
         if not last:
-            ghosts_out(w + 1)
             front(w + 1)
-        vtt(R("XT"), IX(ZB, R("OBW", 32, 47)), R("HL", 0, CAP), O.min)
-        vtt(IX(XA, AW), R("XT"), R("HL", CAP, 2 * CAP), O.max)
+            vtt(R("XT"), IX(ZB, R("OBW", 32, 47)), R("HL", 0, CAP), O.min)
+            vtt(IX(XA, AW), R("XT"), R("HL", CAP, 2 * CAP), O.max)
+            return
+        for k in range(NC):
+            c0, n = CH[k]
+            vtt(ch("XT", k), IX(ZB, R("OBW", 32 + c0 // 16, 32 + (c0 + n) // 16)), R("HL", c0, c0 + n), O.min)
+            vtt(ch("XN", k), ch("XT", k), R("HL", CAP + c0, CAP + c0 + n), O.max)
+            vcp(IX(R("YA"), R("AW" + p, c0 // 16, (c0 + n) // 16)), ch("XN", k))
 
     front(0)
     for i in range(2):
@@ -490,14 +578,8 @@ def build(g, core, T, topo, msgs):
         copy("G", R("NB", EXT + a, EXT + b), R("LN", a, b))
     for w in range(RO):
         wave(w)
-    vts(R("Y1"), R("FX", 0, VA), -float(OFF), None, O.add)
-    for i in range(2):
-        a, b = 320 * i, 320 * i + 320
-        act(R(PD[i], 0, 320), R("FX", a, b), F.Copy, scale=-1000.0, bias=2559.0)
-        vtt(R("YO", a, b), R(PD[i], 0, 320), R("Y1", a, b), O.max)
-    act(R("YA"), R("XA", 0, VA), F.Copy)
-    tk("S", 0.1, [R("YO")], [TAG("yf")], lambda: SY.dma_start(T.yf[:], T.YO[:]), sem="oy", val=16)
-    tk("S", 0.1, [R("YA")], [TAG("ya")], lambda: SY.dma_start(T.ya[:], T.YA[:]), sem="ox", val=16)
+    tk("S", 0.1, [R("YO")], [TAG("yf")], lambda: SY.dma_start(T.yf[:], T.YO[:, 0:VA]), sem="oy", val=16)
+    tk("A", 0.1, [R("YA")], [TAG("ya")], lambda: A.dma_start(T.ya[:], T.YA[:, 0:VA]), sem="ox", val=16)
     return tasks, sent
 
 
@@ -505,19 +587,25 @@ LAT = {"V": 0.12, "A": 0.15, "P": 0.15, "G": 0.2, None: 0.0}
 EPS = (0.05, 0.1, 0.2, 0.3)
 TURNS = 6
 CASES = ((1.0, 1.0, 1.0, 0.13), (0.9, 0.9, 0.9, 0.2), (0.8, 1.5, 1.1, 0.13), (1.35, 0.6, 1.1, 0.13))
-BONUS = {}
+MOVES = 5000
 WAW = True
 
 
 def span(qs, dur, pred, order, wake):
-    fin, free = [0.0] * len(qs), {}
+    fin, why, last = [0.0] * len(qs), [-1] * len(qs), {}
     for i in order:
-        t = max([fin[d] + (gap if gap > 1 or gap == 0 else wake) for d, gap in pred[i]] + [0.0])
-        if qs[i] is not None:
-            t = max(t, free.get(qs[i], 0.0))
-            free[qs[i]] = t + dur[i]
-        fin[i] = t + dur[i]
-    return max(fin)
+        t, w = 0.0, -1
+        for d, gap in pred[i]:
+            x = fin[d] + (gap if gap > 1 or gap == 0 else wake)
+            if x > t:
+                t, w = x, d
+        q = qs[i]
+        if q is not None:
+            if q in last and fin[last[q]] >= t:
+                t, w = fin[last[q]], -2 - last[q]
+            last[q] = i
+        fin[i], why[i] = t + dur[i], w
+    return fin, why
 
 
 def sweep(qs, dur, succ, prio, eps):
@@ -573,7 +661,7 @@ def plan(tasks):
     for i, t in enumerate(tasks):
         for d, hard in t["deps"].items():
             u = tasks[d]
-            gap = LAT[u["q"]] if u["sem"] is None or u["q"] is None else 0.0 if u["sem"] == "none" else 2.0
+            gap = LAT[u["q"]] if u["sem"] is None or u["q"] is None else 0.0 if u["sem"] == "none" else u["lat"]
             if not hard and u["q"] == t["q"] and u["sem"] is None:
                 gap = 0.0
             succ[d].append((i, gap))
@@ -582,17 +670,76 @@ def plan(tasks):
     for i in range(n - 1, -1, -1):
         way[i] = dur[i] + max([way[j] + gap for j, gap in succ[i]] + [0.0])
     cases = [([d * (a if t["kind"] == 1 else b if t["kind"] == 2 else c) for d, t in zip(dur, tasks)], wake) for a, b, c, wake in CASES]
+
+
+    def tried(prio, eps):
+        order, fin = sweep(qs, dur, succ, prio, eps)
+        ends = [max(span(qs, d, pred, order, wake)[0]) for d, wake in cases]
+        return order, fin, sum(ends) / len(ends), ends, prio, eps
+
     best = None
     for eps in EPS:
         prio = way
         for _ in range(TURNS):
-            order, fin = sweep(qs, dur, succ, [x + BONUS.get(t["tag"], 0.0) for x, t in zip(prio, tasks)], eps)
-            end = sum(span(qs, d, pred, order, wake) for d, wake in cases) / len(cases)
-            if best is None or end < best[2]:
-                best = (order, fin, end)
-            prio = sweep(qs, dur, pred, fin, eps)[1]
+            x = tried(prio, eps)
+            if best is None or x[2] < best[2]:
+                best = x
+            prio = sweep(qs, dur, pred, x[1], eps)[1]
+    best = (mend(qs, pred, cases, [t["key"] for t in tasks], best[0]),) + best[1:]
     PLAN.append(best)
     return best
+
+
+def mend(qs, pred, cases, key, order):
+    at = {k: i for i, k in enumerate(key)}
+    needs = [set(d for d, gap in p) for p in pred]
+    rng = np.random.RandomState(0)
+
+    def ends(o):
+        r = [span(qs, d, pred, o, wake) for d, wake in cases]
+        return sum(max(x[0]) for x in r) / len(r), r
+
+    cur, r = ends(order)
+    best = (cur, order)
+    for _ in range(MOVES):
+        fin, why = r[rng.randint(len(r))]
+        i, held = fin.index(max(fin)), []
+        while i >= 0:
+            if why[i] <= -2:
+                held.append((-2 - why[i], i))
+            i = -2 - why[i] if why[i] <= -2 else why[i]
+        a, b = held[rng.randint(len(held))]
+        line = [x for x in order if qs[x] == qs[a]]
+        a = line[max(0, line.index(a) - rng.randint(3))]
+        o, up = list(order), rng.rand() < 0.5
+        for s in (range(1 - RO, RO) if rng.rand() < 0.8 else (0,)):
+            x, y = at.get((key[a][0] + s, key[a][1])), at.get((key[b][0] + s, key[b][1]))
+            if x is None or y is None or o.index(x) > o.index(y):
+                continue
+            px, py = o.index(x), o.index(y) + 1
+            seg = o[px:py]
+            if up:
+                need, m = set(needs[y]), {y}
+                for z in seg[-2::-1]:
+                    if z in need:
+                        m.add(z)
+                        need |= needs[z]
+                if x not in m:
+                    o[px:py] = [z for z in seg if z in m] + [z for z in seg if z not in m]
+            else:
+                m = {x}
+                for z in seg[1:]:
+                    if needs[z] & m:
+                        m.add(z)
+                if y not in m:
+                    o[px:py] = [z for z in seg if z not in m] + [z for z in seg if z in m]
+        if o != order:
+            v, r2 = ends(o)
+            if v < cur + 0.025 * rng.exponential():
+                cur, r, order = v, r2, o
+                if v < best[0]:
+                    best = (v, o)
+    return best[1]
 
 
 def emit(g, T, tasks, order):

@@ -1,5 +1,5 @@
 import numpy as np
-from concourse.mybir import AluOpType as O, ActivationFunctionType as F
+from concourse.mybir import AluOpType as O, ActivationFunctionType as F, AxisListType
 
 VA, GH, OB, CAP, S0, RO = 640, 384, 1280, 240, 176, 5
 OFF, NULLC, ZC = 9, 2568, 1288
@@ -10,35 +10,39 @@ WF = 2288
 NB_HALF = 640
 BIG = 30000.0
 CH = ((0, 128), (128, 112))
-SEEDS = ((0, 64, "V"), (64, 64, "A"), (128, 112, "A"))
+SEEDS = ((0, 64, "A"), (64, 64, "A"), (128, 32, "V"), (160, 80, "A"))
 XRQ = ((0, 128, "V"), (128, 112, "G"))
 CUTS = ((64,), (), ())
-ALT = (((32, 32), (0, 0), (0, 0)), ((32, 32), (32, 32), (32, 32)))
-WHO = {"FT": "A", "OB": "VVV", "OFS": "VVV", "AW": "A", "GW": "A", "B": "G", "ZN": "GG", "FH": "AG", "NFU": "A", "LF": "A"}
-MV = (0, 0)
+ALT = (((0, 32), (0, 0), (0, 32)), ((0, 32), (64, 48), (64, 48)))
+WHO = {"FT": "A", "OB": "VVV", "OFS": "VVV", "AW": "A", "GW": "A", "B": "G", "ZN": "GG", "FH": "AG", "NFU": "A", "LF": "A", "U": "AAAAVV", "TT": "V"}
+START = ("ag", "ax0", "ax1", "an0", "an1")
+FIRST = START[0]
+MV = (0, 4)
+NRC = ((), (), ())
 NFW = (0, 0, 0, 0, 0)
 NC = len(CH)
 
 SCRATCH = {}
 _L = {
     "bfloat16": "ZB:2576 XAB:640 Q:3840 RX:640 YA:1264 GB:1024 XN:240 FL2:2288",
-    "float16": "ONE:1024 BD:128 BDT:128 ID:128 IK:128 IN1:128 IN2:128 SLM:128 SLN:128 TRIX:128 TRIY:128 GI:128 NEG:64 NGC:64 SEL:8 EH:2048 CM:1024 "
+    "float16": "ONE:1024 BD:128 BDT:128 ID:128 IK:128 IN1:128 IN2:128 SLM:128 SLN:128 TRIX:128 TRIY:128 GI:128 NEG:72 NGC:72 SEL:8 EH:2048 CM:1024 "
                "HS:512 C2:240 MB:176 FH0:640 FH1:640 LFH:640 EL:40 LWH:240 GR:240 FT0:256 SG:24 NOH:240 XFN0:240 XFN1:240 TT:256 TTT:256 XR0:3840 XR1:3840 "
                "NR:3840 ST:3840 ZN:240 IDT:384 UR:768 UM:2304 DM:2304 S:768 MG:2304",
-    "float32": "NB:2576 FX:2528 INV:1264 GK:384 NBF:1264 IDF:128 ZF:240 FL0:2288 FL1:2288 LF:1264 LW:1280 XA:1264 MF:176 FA:176 O16:128 COL:8 MQ:16 MQI:16 KS:64 SB:192 IOTAF:640 DUMA0:40 "
-               "DUMPA:40 CMK:128 ONE40:80 CUM:80 THR:8 NFAIL:16 LFV:240 HL:480 XT:240 NI:240 Y1:640 YO:1264",
-    "int32": "NBB:1280 NBA:640 NFW:1280 F0I:176 BDI:24 ICOL:4",
-    "uint16": "NBX:1280 LN:1280 BDU:24 POU:40 FT:256 RN:640 GHS:1920 RG:1920 LG:1920 NFU:240 AW0:16 AW1:16 OFS:240 OBW:48",
+    "float32": "FX:2528 INV:1264 GK:384 IDF:128 ZF:240 FL0:2288 FL1:2288 LF:1264 LW:1408 XA:1264 FA:176 O16:128 COL:8 IOTAF:640 DUMA0:40 "
+               "DUMPA:40 CMK:128 ONE40:80 CUM:80 THR:8 NFAIL:16 FAIL:16 LFV:240 HL:480 XT:240 NI:240 Y1:640 YO:1264",
+    "int32": "NB:2576 NBA:1264 PK:640 NFI:240 NFW:1408 F0I:176 BDI:24 ICOL:4",
+    "uint16": "NBX:1280 LN:1280 BDU:24 POU:40 FT:256 RN:640 GHS:2016 RG:2016 LG:2016 NFU:240 AW0:16 AW1:16 OFS:240 OBW:48 REP:8",
 }
 for _d in _L:
     for _x in _L[_d].split():
         SCRATCH[_x.split(":")[0]] = ("sbuf", [128, int(_x.split(":")[1])], _d)
 for _i in range(8):
     SCRATCH["ps%d" % _i] = ("psum", [128, 512], "float32")
-PC = ["ps%d" % k for k in range(NC)]
-PD = ["ps%d" % (NC + k) for k in range(NC)]
+SCRATCH["ps4"] = ("psum", [128, 24, 9], "float32")
+PC = ["ps0", "ps1"]
+PD = PC
 PF, PM, PH = "ps6", "ps7", "ps5"
-PA = ["ps4", "ps5"]
+PA = ["ps2", "ps3"]
 
 LOADS = ["xb", "f0", "bd", "nba", "xa", "nbb"]
 SEMAPHORES = ["sV", "sA", "sP", "sG", "ls", "oy", "ox", "rx", "rn", "ax0", "ax1", "an0", "an1"] + \
@@ -115,6 +119,9 @@ def build(g, core, T, topo, msgs):
         f = win["f"]
         return dict(ap=win["ap"].indirect(off["ap"]), f=(f[0], f[1], f[2], False), o=off["f"], n=16 * off["n"], two=False, ps=False)
 
+    def nine(x, k, n):
+        return dict(ap=x, f=("ps4", 1 << k, 1 << k, False), o=None, n=n, two=False, ps=True)
+
     def TAG(name):
         return dict(f=(name, 1, 1, True), o=None, ps=False)
 
@@ -127,7 +134,7 @@ def build(g, core, T, topo, msgs):
             for f in fs:
                 for r in rec.get(f[0], []):
                     same = r[3] == q and tasks[r[2]]["sem"] is None and sem is None
-                    if (r[0] & f[1]) if same else (r[1] & f[2]):
+                    if (r[0] & f[1]) if same or f[0][:2] == "XR" else (r[1] & f[2]):
                         if r[4] and (WAW or not (isw and same)):
                             deps[r[2]] = True
                         elif isw:
@@ -145,7 +152,7 @@ def build(g, core, T, topo, msgs):
             rec.setdefault(f[0], []).append((f[1], f[2], i, q, True))
         for f in reads:
             rec.setdefault(f[0], []).append((f[1], f[2], i, q, False))
-        kind = 2 if wr[0]["o"] else 1 if rd and rd[0]["o"] else 0
+        kind = 3 if q is None else 2 if wr[0]["o"] else 1 if rd and rd[0]["o"] else 0
         tag = wr[0]["f"][0] + (q or "")
         role = "".join(c for c in tag if c.isalpha()) + part[0]
         seen[(part[1], role)] = seen.get((part[1], role), 0) + 1
@@ -204,8 +211,8 @@ def build(g, core, T, topo, msgs):
         else:
             tk("G", 0.13 + 2 * out["n"] * CY, [], [out], lambda: g.iota(out["ap"], pat, base, cm, allow_small_or_imprecise_dtypes=True))
 
-    def asel(out, a, pat, op, base, cm):
-        tk("G", 0.17 + 2 * out["n"] * CY, [a], [out], lambda: g.affine_select(out["ap"], a["ap"], pat, op, 0.0, base, cm))
+    def asel(out, a, pat, op, base, cm, fill=0.0):
+        tk("G", 0.17 + 2 * out["n"] * CY, [a], [out], lambda: g.affine_select(out["ap"], a["ap"], pat, op, fill, base, cm))
 
     def copy(q, out, a):
         if q == "V":
@@ -240,13 +247,15 @@ def build(g, core, T, topo, msgs):
     ZB, NB, FX, XA, LF = R("ZB"), R("NB"), R("FX", 0, WE), R("XA"), R("LF")
 
     vms(R("ZB", 0, 16), 1000.0)
-    vms(R("ZB", NULLC, WB), 1000.0)
+    vms(R("NB", 0, 12), 2559)
     load("S", "f0", R("F0I"))
     load("A", "xb", R("ZB", OFF, EXT))
     load("S", "bd", R("BDI"))
-    load("S", "nba", R("NBA", 0, VA))
+    load("S", "nbb", R("NB", OFF, EXT))
     load("A", "xa", R("XAB"))
-    load("S", "nbb", R("NBB"))
+    load("S", "nba", R("NBA", 0, VA))
+    vms(R("ZB", NULLC, WB), 1000.0)
+    vms(R("NB", NULLC, WB), 2559)
 
     mine = [m for m in msgs if m[0] == core]
     inb = {m[8]: m for m in msgs if m[2] == core}
@@ -256,57 +265,52 @@ def build(g, core, T, topo, msgs):
     def remote(m):
         def fn():
             sent[0] += send(g, topo, core, m[1], m[3], m[4], m[9], m[10], T, m[5])
-        tk("G", 2.6 if m is mine[0] else 0.6, [R(m[9], m[10][0], m[10][1])], [TAG("snt" + m[8])], fn, sem="none")
+        tk("G", 2.6 if m[8] == FIRST else 0.6, [R(m[9], m[10][0], m[10][1])], [TAG("snt" + m[8]), TAG("line")], fn, sem="none")
 
     def arrive(sem, delay):
         m = inb[sem]
         tk(None, delay, [TAG("snt" + sem)], [R(m[6], m[7][0], m[7][1])], None, sem=sem, val=len(topo.engines(m[1], core)))
 
-    for m in mine[0:2]:
-        remote(m)
-
-    vms(R("ONE"), 1.0)
+    vms(R("ONE", 0, 128), 1.0)
+    vms(R("ONE", 128, 1024), 1.0)
     one = R("ONE", 0, 128)
     asel(R("BDT"), one, [[-16, 8], [0, 16]], O.is_ge, 0, 1)
     asel(R("BD"), R("BDT"), [[16, 8], [0, 16]], O.is_ge, 15, -1)
     asel(R("ID"), one, [[-1, 128]], O.is_equal, 0, 1)
-    iota(ICOL["PI"], [[0, 1]], 0, 1)
-    iota(R("MQI"), [[1, 16]], 0)
-    iota(R("DUMA0"), [[16, 40]], VA)
+    iota(R("DUMPA"), [[16, 40]], VA, 1)
+    iota(R("NFI", 0, 8), [[0, 8]], 0, 1)
+    vts(R("NFI", 8, 16), R("NFI", 0, 8), 7, None, O.bitwise_and)
+    vcp(R("REP"), R("NFI", 8, 16))
+    vms(R("FAIL"), 0.0)
     asel(R("SLM"), R("BD"), [[-1, 128]], O.is_gt, 0, 1)
     iota(R("IOTAF"), [[1, VA]], 32)
-    iota(R("NBF", 1024, WE), [[1, CAP]], 1024)
-    vcp(R("NBF", 0, VA), R("NBA"))
+    iota(R("NBA", 1024, WE), [[1, CAP]], 1024)
+    if sum(NFW):
+        act(R("Y1"), R("XAB"), F.Copy, scale=4096.0)
+        vtt(R("PK"), R("Y1"), R("NBA", 0, VA), O.add)
     act(R("IDF"), R("ID"), F.Copy)
-    vms(R("FL2", 0, VA), 0.0)
     asel(R("GI"), one, [[-1, 8], [0, 16]], O.is_equal, 0, 1)
     vms(R("NGC"), -2 * BIG)
-    asel(R("NEG"), R("NGC"), [[0, 8], [-1, 8]], O.not_equal, 0, 1)
+    asel(R("NEG"), R("NGC"), [[0, 8], [-1, 9]], O.not_equal, 0, 1, float(ZC))
+    vms(R("NEG", 8, 72, 9), 0.0)
     asel(R("CM"), R("ONE"), [[-16, 8], [0, 8], [-1, 16]], O.is_equal, 0, 1)
 
     vms(R("FX", S0, VA), 0.0)
-    vms(R("FX", VA + GH, WE), 0.0)
-    vts(R("MF"), R("F0I"), 2559, None, O.is_lt)
-    vts(R("FA"), R("F0I"), OFF, None, O.add)
-    vtt(R("FX", 0, S0), R("FA"), R("MF"), O.mult)
-    vcp(R("BDU"), R("BDI"))
-    act(R("MB"), R("MF"), F.Copy)
-    vts(ICOL["PJ"], ICOL["PI"], 15, None, O.bitwise_and)
-    vcp(COL["PF"], ICOL["PJ"])
-    vts(R("MQ"), R("MQI"), COL["PF"], None, O.is_equal)
+    act(R("FX", VA + GH, WE), R("ONE", 0, CAP), F.Copy, scale=0.0)
+    vts(R("MB"), R("F0I"), 2559, None, O.is_lt)
+    act(R("FA"), R("F0I"), F.Copy, bias=float(OFF))
+    vtt(R("FX", 0, S0), R("FA"), R("MB"), O.mult)
+    act(R("BDU"), R("BDI"), F.Copy)
+    for h in range(2):
+        vms(R("EH", 1024 * h, 1024 * h + 1024), 0.0)
     for q in range(16):
-        if q % 8 < 5:
-            vts(blk("EH", q), R("ID"), R("MQ", q, q + 1), None, O.mult)
-        else:
-            act(blk("EH", q), R("ID"), F.Copy, scale=R("MQ", q, q + 1))
-    vts(R("DUMPA"), R("DUMA0"), COL["PF"], None, O.add)
-    vts(R("SEL"), R("BD", 0, 128, 16), 4096.0, None, O.mult)
-    for x, c in (("IK", -512.0), ("IN1", -1.0), ("IN2", -2.0)):
-        vts(R(x), R("ID"), c, None, O.mult)
-    vts(R("SLN"), R("ID"), 2047.0, None, O.mult)
-    vtt(R("TRIY"), R("SLN"), R("SLM"), O.add)
+        copy("VA"[q // 8], R("EH", 128 * q + q, 128 * q + 128, 16), R("ID", q, 128, 16))
+    act(R("SEL"), R("BD", 0, 128, 16), F.Copy, scale=4096.0)
+    for x, c in (("IN1", -1.0), ("IN2", -2.0)):
+        act(R(x), R("ID"), F.Copy, scale=c)
+    asel(R("TRIY"), R("SLM"), [[-1, 128]], O.not_equal, 0, 1, 2047.0)
     vtt(R("TRIX"), R("BD"), R("TRIY"), O.subtract)
-    vms(R("HS"), 0.0)
+    act(R("HS"), R("ONE", 0, 512), F.Copy, scale=0.0)
     for h in range(2):
         for e in range(2):
             for a in range(4):
@@ -316,16 +320,13 @@ def build(g, core, T, topo, msgs):
     vms(R("ONE40"), 1.0)
     vms(R("THR", 0, 1), 1544.0)
     vms(R("C2"), 2.0)
-    vms(R("NB", 0, OFF), float(NULLC))
-    vms(R("NB", NULLC, WB), float(NULLC))
     vms(R("TT", CAP, 256), 0.0)
-    vms(R("KS"), BIG * BIG)
-    vms(R("KS", 0, 64, 8), -BIG * BIG)
-    vms(R("XA", 1024, WE), 0.0)
+    act(R("XA", 1024, WE), R("ONE", 0, CAP), F.Copy, scale=0.0)
     act(R("XA", 0, VA), R("XAB"), F.Copy)
     act(R("FL0", 0, VA), R("ONE", 0, VA), F.Silu, scale=10.0)
     iota(R("FL1", 0, VA), [[0, VA]], 10)
-    iota(R("LF", S0, VA), [[0, VA - S0]], 2000)
+    iota(R("LF", S0, VA), [[0, VA - S0]], 8000)
+    iota(R("FL2", 0, VA), [[0, VA]], 0)
     for k in range(NC):
         u, r = 768 * k, 256 * k
         for a in range(u, u + 768, 256):
@@ -348,15 +349,13 @@ def build(g, core, T, topo, msgs):
             vcp(IX(R("FX"), R("LG", s, s + n // 16)), R("LG", s + 8, s + 8 + n))
 
     vts(R("GHS", 0, GH), IX(R("FX", 0, VA), R("BDU")), float(OB + 8), -float(OB), O.max, O.add)
-    remote(by_sem["ag"])
-    vts(R("NBX"), R("NBB"), EXT, NULLC, O.add, O.min)
-    for i in range(2):
-        remote(by_sem["an%d" % i])
+    vts(R("NBX"), R("NB", OFF, EXT), OB, 2559, O.add, O.min)
+    for x in START:
+        remote(by_sem[x])
     iota(R("INV"), [[1, WE]], WE - 1024)
     iota(R("GK"), [[1, GH]], VA - 1024)
     vcp(IX(R("INV"), R("BDU")), R("GK"))
-    vms(R("GHS", GH, None), 0)
-    vts(R("NB", OFF, EXT), R("NBB"), OFF, None, O.add)
+    vms(R("GHS", slot(0, NC - 1) + 7, slot(RO - 1, 0), 136 * NC), 0)
     for i in range(2):
         arrive("ax%d" % i, FLY + 3.0)
     for i in range(2):
@@ -372,7 +371,7 @@ def build(g, core, T, topo, msgs):
             m = S0 // 16
             mm([(R(PF, 200, 200 + S0), R("BD"), R("MB"), True, True)])
             act(R("LFH", 0, S0), R(PF, 200, 200 + S0), F.Copy)
-            act(R("LF", 0, S0), R(PF, 200, 200 + S0), F.Copy, scale=-2000.0, bias=2000.0)
+            act(R("LF", 0, S0), R(PF, 200, 200 + S0), F.Relu, scale=-8000.0, bias=8000.0)
             mm([(R(PF, 0, m), blk("EH", q), R("LFH", q, S0, 16), q == 0, q == 15) for q in range(16)])
             vms(R("EL", m, 40), 1.0)
             vts(R("EL", 0, m), R(PF, 0, m), 0.0, None, O.is_equal)
@@ -380,28 +379,30 @@ def build(g, core, T, topo, msgs):
             copy("G", R("LFH"), R("LF", 0, VA))
             mm([(el, blk("EH", q), R("LFH", q, VA, 16), q == 0, False) for q in range(16)])
             for i in (1, 0):
-                if i and sum(MV):
-                    mm([(el, blk("EH", q), R("FL2", q, VA, 16), False, False) for q in range(16)])
                 copy(WHO["FH"][i], R("FH%d" % i), R("FL%d" % i, 0, VA))
-                mm([(el, blk("EH", q), R("FH%d" % i, q, VA, 16), False, i == 0 and q == 15) for q in range(16)])
-            vts(R("EL"), el, 2000.0, None, O.is_ge)
+                mm([(el, blk("EH", q), R("FH%d" % i, q, VA, 16), False, i == 0 and q == 15 and not sum(MV)) for q in range(16)])
+            if sum(MV):
+                mm([(el, blk("EH", q), R("FL2", q, VA, 16), False, q == 15) for q in range(16)])
+            vts(R("EL"), el, 8000.0, None, O.is_ge)
         mm([(R(PF, 40, 120, 2), R("TRIX"), R("EL"), True, True), (R(PF, 41, 120, 2), R("TRIY"), R("EL"), True, True)])
         scan(R("CUM"), R("ONE40"), R(PF, 40, 120), 2046.0, O.mult, O.add)
         vtt(R("POU"), R("CUM", 0, 80, 2), R("DUMPA"), O.min)
         if NFW[w]:
             iota(R("NFW", 0, CAP), [[1, CAP]], 1024)
-            vcp(IX(R("NFW"), R("POU")), R("NBA", 0, VA))
-            vcp(R("NFU"), R("NFW", 0, CAP))
+            vcp(IX(R("NFW"), R("POU")), R("PK"))
+            vts(R("NFI"), R("NFW", 0, CAP), 4095, None, O.bitwise_and)
+            vcp(R("NFU"), R("NFI"))
+            vts(R("XFN" + p), R("NFW", 0, CAP), -1.0 / 4096, R("THR", w, w + 1), O.mult, O.add)
         act(IX(R("LW"), R("POU")), R("IOTAF"), F.Silu)
         act(R("LWH"), R("LW", 0, CAP), F.Copy, bias=-32.0)
         mm([(R(PF, 120, 135), blk("EH", q), R("LWH", q, CAP, 16), q == 0, q == 15) for q in range(16)])
         places(WHO["AW"], AW, R(PF, 120, 135), 0.0)
         if not NFW[w]:
-            copy(WHO["NFU"], R("NFU"), IX(R("NBF"), AW))
-        act(R("XFN" + p), IX(XA, AW), F.Identity, scale=-1.0, bias=R("THR", w, w + 1))
+            copy(WHO["NFU"], R("NFU"), IX(R("NBA"), AW))
+            act(R("XFN" + p), IX(XA, AW), F.Identity, scale=-1.0, bias=R("THR", w, w + 1))
         for c0, n, e in XRQ:
             for q in range(16):
-                copy(e, R("XR" + p, 16 * c0 + q, 16 * (c0 + n), 16), R("XFN" + p, c0, c0 + n))
+                copy(e[q % len(e)], R("XR" + p, 16 * c0 + q, 16 * (c0 + n), 16), R("XFN" + p, c0, c0 + n))
         if w < RO - 1:
             mark_tables()
             act(R("GR"), IX(R("INV"), AW), F.Copy)
@@ -409,7 +410,7 @@ def build(g, core, T, topo, msgs):
             for k in range(NC):
                 c0, n = CH[k]
                 places(WHO["GW"], R("GHS", slot(w, k), slot(w, k) + n // 16), R(PF, 140 + c0 // 16, 140 + (c0 + n) // 16), 1024.0)
-            iota(R("CMK"), [[0, 128]], 30 * 3 ** w)
+            iota(R("CMK"), [[0, 128]], 40 * 4 ** w)
 
     def pieces(k, t):
         c0, n = CH[k]
@@ -428,7 +429,7 @@ def build(g, core, T, topo, msgs):
         c0, n = CH[k]
         m, u, r = n // 16, 768 * k, 256 * k
         part[0] = "t%d%d" % (t, k)
-        c = R(PC[k], 0, 128, 1, n)
+        c = R(PC[k], 384, 512, 1, n)
         cut = c0 + n - ALT[w == RO - 1][t][k]
         for a, b in pieces(k, t):
             b = min(a + b, cut)
@@ -441,9 +442,15 @@ def build(g, core, T, topo, msgs):
             act(gb, IX(ZB, R("OFS", a, b)), F.Copy)
             mm([(pa, R("ID"), R("XR" + p, 16 * a, 16 * b), True, False), (pa, R("ID"), gb, False, True)])
             act(R("Q", 16 * a, 16 * b), pa, F.Copy)
-        vts(ch("NR", k, 16), ch("Q", k, 16), R("THR", w, w + 1), 0.84375, O.is_equal, O.subtract)
-        mm([(R(PC[k], q, 128, 16, n), by("NR", k, q), R("SEL"), True, True) for q in range(16)])
-        act(R("UM", u + 2 + t, u + 768, 6, n) if t else R("UR", r, r + 256, 2, n), c, F.Copy, scale=-1.0)
+        cut = [c0] + [x for x in NRC[t] if c0 < x < c0 + n] + [c0 + n]
+        for a, b in zip(cut, cut[1:]):
+            vts(R("NR", 16 * a, 16 * b), R("Q", 16 * a, 16 * b), R("THR", w, w + 1), 0.84375, O.is_equal, O.subtract)
+        mm([(R(PC[k], 384 + q, 512, 16, n), by("NR", k, q), R("SEL"), True, True) for q in range(16)])
+        minus = R("UM", u + 2 + t, u + 768, 6, n) if t else R("UR", r, r + 256, 2, n)
+        if WHO["U"][NC * t + k] == "A":
+            act(minus, c, F.Copy, scale=-1.0)
+        else:
+            vts(minus, c, -1.0, None, O.mult)
         vtt(R("DM", u + 2 + t, u + 768, 6, n), c, blk("IDT", k, n), O.min)
         if t == 2:
             scan(R("MG", u, u + 768, 1, n), R("UM", u, u + 768, 1, n), R("DM", u, u + 768, 1, n), -BIG)
@@ -467,16 +474,15 @@ def build(g, core, T, topo, msgs):
             b = R("S", r, r + 256, 32, n)
         if t < 2:
             copy(WHO["B"], R("DM", u + t, u + 768, 96, n), b)
-        x = R(PC[k], 128, 128 + 8 * m)
-        mm([(x, R("GI", 0, 128, 1, 8), R("NEG", 0, 8 * m, 1, 8), True, False)] +
-           [(R(PC[k], 128 + 8 * i, 136 + 8 * i), blk("CM", i, n), b, False, i == m - 1) for i in range(m)])
-        scan(R("SB", 64 * k, 64 * k + 8 * m), R("KS", 0, 8 * m), x, 0.0)
+        x = nine(T.ps4[:, 8 * k:8 * k + m, :], k, 9 * m)
+        mm([(x, R("GI", 0, 128, 1, 8), R("NEG", 0, 9 * m, 1, 8), True, False)] +
+           [(nine(T.ps4[:, 8 * k + i, 0:8], k, 8), blk("CM", i, n), b, False, i == m - 1) for i in range(m)])
         ob = R("OBW", 16 * t + c0 // 16, 16 * t + c0 // 16 + m)
-        places(WHO["OB"][t], ob, R("SB", 64 * k + 7, 64 * k + 8 * m, 8), float(ZC))
+        tk("V", cost(x, None, 1.0), [x], [ob], lambda: V.tensor_reduce(ob["ap"], x["ap"], AxisListType.X, O.max))
         if t < 2:
-            copy(WHO["OFS"][t + 1], ch("OFS", k), IX(NB, ob))
+            places(WHO["OFS"][t + 1], ch("OFS", k), IX(NB, ob), float(OFF))
             if WHO["ZN"][t] == "A":
-                act(ch("ZN", k), IX(NB, ob), F.Copy, bias=-float(ZC))
+                act(ch("ZN", k), IX(NB, ob), F.Copy, bias=float(OFF - ZC))
                 turn(k, ch("ZN", k))
             else:
                 copy("G", ch("ZF", k), ch("OFS", k))
@@ -488,11 +494,8 @@ def build(g, core, T, topo, msgs):
     def mark(w, k):
         c0, n = CH[k]
         nb, m, z = (n + 31) // 32, n // 16, 256 + c0
-        sg = R("SG", 8 * k, 8 * k + m)
-        act(sg, R("SB", 64 * k + 7, 64 * k + 8 * m, 8), F.Sign, bias=2000.0)
-        mm([(R(PM, z, z + 32 * nb), R("ID"), R("FT0", c0, c0 + 32 * nb), True, False)] +
-           [(R(PM, z + 2 * nb * q, z + 2 * nb * q + m), R("IK"), sg, False, q == 15) for q in range(16)])
-        places(WHO["FT"], R("FT", c0, c0 + 32 * nb), R(PM, z, z + 32 * nb), 512.0)
+        vts(R("FAIL", 8 * k, 8 * k + m), R("OBW", c0 // 16, c0 // 16 + m), 0.0, 1024.0, O.is_equal, O.mult)
+        vtt(R("FT", c0, c0 + 128), IX(R("FAIL", 8 * k, 8 * k + 8), R("REP")), R("FT0", c0, c0 + 128), O.add)
         for q in range(16):
             j = c0 + 2 * nb * q
             if q < MV[k]:
@@ -501,7 +504,7 @@ def build(g, core, T, topo, msgs):
                 act(IX(R("FL%d" % (q % 2 if q < 15 or k < NC - 1 else 0)), R("FT", j, j + m)), R("CMK", 0, n), F.Silu)
 
     def mark_tables():
-        copy("G", R("TT", 0, CAP), R("NFU"))
+        copy(WHO["TT"], R("TT", 0, CAP), R("NFU"))
         tk("V", cost(R("TTT"), None, 0.5), [R("TT")], [R("TTT")], lambda: V.transpose(T.TTT[:], T.TT[:]))
         lst = []
         for c0, n in CH:
@@ -544,7 +547,7 @@ def build(g, core, T, topo, msgs):
             if not last:
                 mark(w, k)
         if not last:
-            act(R("LFV"), R("NOH"), F.Copy, scale=2000.0 - 25 * 3 ** w)
+            act(R("LFV"), R("NOH"), F.Copy, scale=8000.0 - 35 * 4 ** w)
             if WHO["LF"] == "A":
                 act(IX(LF, AW), R("LFV"), F.Silu)
             else:
@@ -586,8 +589,8 @@ def build(g, core, T, topo, msgs):
 LAT = {"V": 0.12, "A": 0.15, "P": 0.15, "G": 0.2, None: 0.0}
 EPS = (0.05, 0.1, 0.2, 0.3)
 TURNS = 6
-CASES = ((1.0, 1.0, 1.0, 0.13), (0.9, 0.9, 0.9, 0.2), (0.8, 1.5, 1.1, 0.13), (1.35, 0.6, 1.1, 0.13))
-MOVES = 5000
+CASES = ((1.0, 1.0, 1.0, 0.7, 0.13), (0.9, 0.9, 0.9, 0.9, 0.2), (1.1, 0.8, 1.5, 1.1, 0.13), (1.1, 1.35, 0.6, 1.1, 0.13))
+MOVES = 8000
 WAW = True
 
 
@@ -669,7 +672,7 @@ def plan(tasks):
     way = [0.0] * n
     for i in range(n - 1, -1, -1):
         way[i] = dur[i] + max([way[j] + gap for j, gap in succ[i]] + [0.0])
-    cases = [([d * (a if t["kind"] == 1 else b if t["kind"] == 2 else c) for d, t in zip(dur, tasks)], wake) for a, b, c, wake in CASES]
+    cases = [([d * x[t["kind"]] for d, t in zip(dur, tasks)], x[4]) for x in CASES]
 
 
     def tried(prio, eps):
@@ -710,7 +713,7 @@ def mend(qs, pred, cases, key, order):
             i = -2 - why[i] if why[i] <= -2 else why[i]
         a, b = held[rng.randint(len(held))]
         line = [x for x in order if qs[x] == qs[a]]
-        a = line[max(0, line.index(a) - rng.randint(3))]
+        a = line[max(0, line.index(a) - rng.randint(3 if rng.rand() < 0.7 else 20))]
         o, up = list(order), rng.rand() < 0.5
         for s in (range(1 - RO, RO) if rng.rand() < 0.8 else (0,)):
             x, y = at.get((key[a][0] + s, key[a][1])), at.get((key[b][0] + s, key[b][1]))

import numpy as np
from concourse.mybir import AluOpType as O, ActivationFunctionType as F, AxisListType

VA, GH, OB, CAP, S0, RO = 640, 384, 1280, 240, 176, 5
OFF, NULLC, ZC = 9, 2568, 1288
EXT = OFF + OB
WB = 2576
WE = 1264
WF = 2288
NB_HALF = 640
BIG = 30000.0
CH = ((0, 128), (128, 112))
SEEDS = ((0, 64, "A"), (64, 64, "A"), (128, 32, "V"), (160, 80, "A"))
XRQ = ((0, 128, "V"), (128, 112, "G"))
CUTS = ((64,), (), ())
ALT = (((0, 32), (0, 0), (0, 32)), ((0, 32), (64, 48), (64, 48)))
WHO = {"FT": "A", "OB": "VVV", "OFS": "VVV", "AW": "A", "GW": "A", "B": "G", "ZN": "GG", "FH": "AG", "NFU": "A", "LF": "A", "U": "AAAAVV", "TT": "V"}
START = ("ag", "ax0", "ax1", "an0", "an1")
FIRST = START[0]
MV = (0, 4)
NRC = ((), (), ())
NFW = (0, 0, 0, 0, 0)
NC = len(CH)

SCRATCH = {}
_L = {
    "bfloat16": "ZB:2576 XAB:640 Q:3840 RX:640 YA:1264 GB:1024 XN:240 FL2:2288",
    "float16": "ONE:1024 BD:128 BDT:128 ID:128 IK:128 IN1:128 IN2:128 SLM:128 SLN:128 TRIX:128 TRIY:128 GI:128 NEG:72 NGC:72 SEL:8 EH:2048 CM:1024 "
               "HS:512 C2:240 MB:176 FH0:640 FH1:640 LFH:640 EL:40 LWH:240 GR:240 FT0:256 SG:24 NOH:240 XFN0:240 XFN1:240 TT:256 TTT:256 XR0:3840 XR1:3840 "
               "NR:3840 ST:3840 ZN:240 IDT:384 UR:768 UM:2304 DM:2304 S:768 MG:2304",
    "float32": "FX:2528 INV:1264 GK:384 IDF:128 ZF:240 FL0:2288 FL1:2288 LF:1264 LW:1408 XA:1264 FA:176 O16:128 COL:8 IOTAF:640 DUMA0:40 "
               "DUMPA:40 CMK:128 ONE40:80 CUM:80 THR:8 NFAIL:16 FAIL:16 LFV:240 HL:480 XT:240 NI:240 Y1:640 YO:1264",
    "int32": "NB:2576 NBA:1264 PK:640 NFI:240 NFW:1408 F0I:176 BDI:24 ICOL:4",
    "uint16": "NBX:1280 LN:1280 BDU:24 POU:40 FT:256 RN:640 GHS:2016 RG:2016 LG:2016 NFU:240 AW0:16 AW1:16 OFS:240 OBW:48 REP:8",
}
for _d in _L:
    for _x in _L[_d].split():
        SCRATCH[_x.split(":")[0]] = ("sbuf", [128, int(_x.split(":")[1])], _d)
for _i in range(8):
    SCRATCH["ps%d" % _i] = ("psum", [128, 512], "float32")
SCRATCH["ps4"] = ("psum", [128, 24, 9], "float32")
PC = ["ps0", "ps1"]
PD = PC
PF, PM, PH = "ps6", "ps7", "ps5"
PA = ["ps2", "ps3"]

LOADS = ["xb", "f0", "bd", "nba", "xa", "nbb"]
SEMAPHORES = ["sV", "sA", "sP", "sG", "ls", "oy", "ox", "rx", "rn", "ax0", "ax1", "an0", "an1"] + \
    ["l" + n for n in LOADS] + ["rg", "ag"] + [x + "%d%d" % (w, k) for x in ("rg", "ag") for w in range(RO - 1) for k in range(NC)]


def relays(topo, src, dst):
    c = [x for x in topo.cores_of(src) if x != src and topo.may_write(x, dst)]
    return sorted(c, key=lambda x: (topo.die(x) != topo.die(src), x))


def messages(topo, cores):
    n, out = len(cores), []
    for r in range(n):
        src, prev, nxt = cores[r], cores[(r - 1) % n], cores[(r + 1) % n]
        rb = relays(topo, src, prev)
        w = (NB_HALF, OB - 1 - NB_HALF)
        for i in range(2):
            a, b = i * NB_HALF, i * NB_HALF + w[i]
            out.append((src, rb[i], prev, "RX", (0, w[i]), "rx", "ZB", (EXT + a, EXT + b), "ax%d" % i, "ZB", (OFF + a, OFF + b)))
        for i in range(2):
            a, b = i * NB_HALF, i * NB_HALF + w[i]
            m = (src, rb[3 - i], prev, "RN", (0, w[i]), "rn", "LN", (a, b), "an%d" % i, "NBX", (a, b))
            if i:
                out.append((src, relays(topo, src, nxt)[2], nxt, "RG", (0, GH), "rg", "LG", (0, GH), "ag", "GHS", (0, GH)))
            out.append(m)
        rg = relays(topo, src, nxt)
        for v in range(RO - 1):
            for k in range(NC):
                s = (slot(v, k), slot(v, k) + 8 + CH[k][1])
                out.append((src, rg[k % 2], nxt, "RG", s, "rg%d%d" % (v, k), "LG", s, "ag%d%d" % (v, k), "GHS", s))
    return out


def slot(w, k):
    return GH + 136 * (NC * w + k)


def send(g, topo, src, dst, dbuf, dcol, sbuf, scol, T, rsem):
    rid, pid = topo.addr(dst, src)
    g.remote_dma(T[dbuf][:, dcol[0]:dcol[1]], T[sbuf][:, scol[0]:scol[1]], T.sem[rsem], T.sem["ls"], pid, rid, topo.mask(src, dst))
    return len(topo.engines(src, dst))


def relay_program(g, core, T, topo, msgs):
    total = 0
    for m in msgs:
        if m[1] == core:
            g.wait_ge(T.sem[m[5]], len(topo.engines(m[0], core)))
            total += send(g, topo, core, m[2], m[6], m[7], m[3], m[4], T, m[8])
    if total:
        g.wait_ge(T.sem["ls"], total)


CY = 0.00083 * 1.1
GA, SCA = 1.56, 3.8
PE = 0.0006
FLY = 5.0


def build(g, core, T, topo, msgs):
    tasks, rec, bank, part, seen = [], {}, {}, ["s", -1], {}
    V, A, P, SY = g.vector, g.scalar, g.tensor, g.sync

    def R(name, a=0, b=None, s=1, n=128):
        w, dt = SCRATCH[name][1][1], SCRATCH[name][2]
        cols = range(w)[a:b:s]
        lo, hi = min(cols[0], cols[-1]), max(cols[0], cols[-1]) + 1
        bits = ((1 << (abs(s) * len(cols))) - 1) // ((1 << abs(s)) - 1) << lo
        return dict(ap=T[name][0:n, a:b:s], f=(name, bits, (1 << hi) - (1 << lo), abs(s) == 1 and n == 128), o=None, n=len(cols),
                    two=dt in ("bfloat16", "float16", "uint16"), ps=name[:2] == "ps")

    def IX(win, off):
        f = win["f"]
        return dict(ap=win["ap"].indirect(off["ap"]), f=(f[0], f[1], f[2], False), o=off["f"], n=16 * off["n"], two=False, ps=False)

    def nine(x, k, n):
        return dict(ap=x, f=("ps4", 1 << k, 1 << k, False), o=None, n=n, two=False, ps=True)

    def TAG(name):
        return dict(f=(name, 1, 1, True), o=None, ps=False)

    def tk(q, dur, rd, wr, fn, sem=None, val=0):
        deps, i = {}, len(tasks)
        rd = [x for x in rd if isinstance(x, dict)]
        reads = [x["f"] for x in rd] + [x["o"] for x in rd + wr if x["o"]]
        writes = [x["f"] for x in wr]
        for fs, isw in ((reads, False), (writes, True)):
            for f in fs:
                for r in rec.get(f[0], []):
                    same = r[3] == q and tasks[r[2]]["sem"] is None and sem is None
                    if (r[0] & f[1]) if same or f[0][:2] == "XR" else (r[1] & f[2]):
                        if r[4] and (WAW or not (isw and same)):
                            deps[r[2]] = True
                        elif isw:
                            deps.setdefault(r[2], False)
        for name in {x["f"][0] for x in rd + wr if x["ps"]}:
            e, run, before = bank.get(name, (q, [], []))
            if e != q:
                run, before = [], run
            for t in before:
                deps[t] = True
            bank[name] = (q, run + [i], before)
        for f in writes:
            rec[f[0]] = [r for r in rec.get(f[0], []) if r[0] & ~f[1]]
        for f in writes:
            rec.setdefault(f[0], []).append((f[1], f[2], i, q, True))
        for f in reads:
            rec.setdefault(f[0], []).append((f[1], f[2], i, q, False))
        kind = 3 if q is None else 2 if wr[0]["o"] else 1 if rd and rd[0]["o"] else 0
        tag = wr[0]["f"][0] + (q or "")
        role = "".join(c for c in tag if c.isalpha()) + part[0]
        seen[(part[1], role)] = seen.get((part[1], role), 0) + 1
        tasks.append(dict(q=q, dur=dur, deps=deps, fn=fn, sem=sem, val=val, kind=kind, tag=tag, role=role,
                          key=(part[1], role + str(seen[(part[1], role)]))))

    def ap(x):
        return x["ap"] if isinstance(x, dict) else x

    def cost(out, a, c, fix=0.06, least=64):
        if out["o"]:
            return fix + out["n"] * SCA * CY
        if a is not None and a["o"]:
            return fix + out["n"] * GA * CY
        return fix + max(least, out["n"] * c) * CY

    def half(*x):
        return 0.5 if all(y["two"] for y in x) else 1.0

    def vts(out, a, s1, s2, o0, o1=None):
        if o1 is None:
            tk("V", cost(out, a, half(out, a)), [a, s1], [out], lambda: V.tensor_scalar(out["ap"], a["ap"], ap(s1), None, op0=o0))
        else:
            tk("V", cost(out, a, half(out, a)), [a, s1, s2], [out], lambda: V.tensor_scalar(out["ap"], a["ap"], ap(s1), ap(s2), op0=o0, op1=o1))

    def vtt(out, a, b, op):
        tk("V", cost(out, a, 1.0 if a["ps"] or b["ps"] else 2.0), [a, b], [out], lambda: V.tensor_tensor(out["ap"], a["ap"], b["ap"], op))

    def vcp(out, a):
        tk("V", cost(out, a, half(out, a)), [a], [out], lambda: V.tensor_copy(out["ap"], a["ap"]))

    def vms(out, x):
        tk("V", cost(out, None, half(out)), [], [out], lambda: V.memset(out["ap"], x))

    def scan(out, d0, d1, init, o0=O.min, o1=O.max):
        tk("V", cost(out, d0, half(out, d0, d1)), [d0, d1], [out], lambda: V.tensor_tensor_scan(out["ap"], d0["ap"], d1["ap"], init, o0, o1))

    def act(out, a, fn, acc=None, **kw):
        k = {x: ap(y) for x, y in kw.items()}
        if acc:
            k["accum_out"] = acc["ap"]
        tk("A", cost(out, a, 1.0, 0.07, 0), [a] + list(kw.values()), [out] + ([acc] if acc else []), lambda: A.activation(out["ap"], a["ap"], fn, **k))

    def mm(lst):
        def fn():
            x = None
            for o, l, r, a, b in lst:
                x = P.matmul(o["ap"], l["ap"], r["ap"], a, b)
            return x
        cyc = sum(max(min(64, l["n"]), r["n"]) * (1 if l["two"] else 4) for o, l, r, a, b in lst)
        tk("P", 0.03 + cyc * PE, [x[1] for x in lst] + [x[2] for x in lst], [x[0] for x in lst], fn)

    def iota(out, pat, base, cm=0):
        if SCRATCH[out["f"][0]][2] == "int32":
            tk("G", 0.13 + 2 * out["n"] * CY, [], [out], lambda: g.iota(out["ap"], pat, base, cm))
        else:
            tk("G", 0.13 + 2 * out["n"] * CY, [], [out], lambda: g.iota(out["ap"], pat, base, cm, allow_small_or_imprecise_dtypes=True))

    def asel(out, a, pat, op, base, cm, fill=0.0):
        tk("G", 0.17 + 2 * out["n"] * CY, [a], [out], lambda: g.affine_select(out["ap"], a["ap"], pat, op, fill, base, cm))

    def copy(q, out, a):
        if q == "V":
            vcp(out, a)
        elif q == "A":
            act(out, a, F.Copy)
        else:
            asel(out, a, [[0, out["n"]]], O.is_ge, 0, 0)

    def places(q, out, a, x):
        if q == "V":
            vts(out, a, x, None, O.add)
        else:
            act(out, a, F.Relu, bias=x)

    def ch(name, k, w=1):
        return R(name, w * CH[k][0], w * (CH[k][0] + CH[k][1]))

    def by(name, k, q):
        return R(name, 16 * CH[k][0] + q, 16 * (CH[k][0] + CH[k][1]), 16)

    def blk(name, i, n=128):
        return R(name, 128 * i, 128 * i + 128, 1, n)

    def load(q, name, out):
        e = SY if q == "S" else A
        tk(q, 0.1, [], [out], lambda: e.dma_start(out["ap"], T[name][:]), sem="l" + name, val=16)
        tasks[-1]["lat"] = 1.5 + out["n"] * (1 if out["two"] else 2) * 0.0013

    COL = {x: R("COL", i, i + 1) for i, x in enumerate(("PF",))}
    ICOL = {x: R("ICOL", i, i + 1) for i, x in enumerate(("PI", "PJ", "EI", "EJ"))}
    ZB, NB, FX, XA, LF = R("ZB"), R("NB"), R("FX", 0, WE), R("XA"), R("LF")

    vms(R("ZB", 0, 16), 1000.0)
    vms(R("NB", 0, 12), 2559)
    load("S", "f0", R("F0I"))
    load("A", "xb", R("ZB", OFF, EXT))
    load("S", "bd", R("BDI"))
    load("S", "nbb", R("NB", OFF, EXT))
    load("A", "xa", R("XAB"))
    load("S", "nba", R("NBA", 0, VA))
    vms(R("ZB", NULLC, WB), 1000.0)
    vms(R("NB", NULLC, WB), 2559)

    mine = [m for m in msgs if m[0] == core]
    inb = {m[8]: m for m in msgs if m[2] == core}
    by_sem = {m[8]: m for m in mine}
    sent = [0]

    def remote(m):
        def fn():
            sent[0] += send(g, topo, core, m[1], m[3], m[4], m[9], m[10], T, m[5])
        tk("G", 2.6 if m[8] == FIRST else 0.6, [R(m[9], m[10][0], m[10][1])], [TAG("snt" + m[8]), TAG("line")], fn, sem="none")

    def arrive(sem, delay):
        m = inb[sem]
        tk(None, delay, [TAG("snt" + sem)], [R(m[6], m[7][0], m[7][1])], None, sem=sem, val=len(topo.engines(m[1], core)))

    vms(R("ONE", 0, 128), 1.0)
    vms(R("ONE", 128, 1024), 1.0)
    one = R("ONE", 0, 128)
    asel(R("BDT"), one, [[-16, 8], [0, 16]], O.is_ge, 0, 1)
    asel(R("BD"), R("BDT"), [[16, 8], [0, 16]], O.is_ge, 15, -1)
    asel(R("ID"), one, [[-1, 128]], O.is_equal, 0, 1)
    iota(R("DUMPA"), [[16, 40]], VA, 1)
    iota(R("NFI", 0, 8), [[0, 8]], 0, 1)
    vts(R("NFI", 8, 16), R("NFI", 0, 8), 7, None, O.bitwise_and)
    vcp(R("REP"), R("NFI", 8, 16))
    vms(R("FAIL"), 0.0)
    asel(R("SLM"), R("BD"), [[-1, 128]], O.is_gt, 0, 1)
    iota(R("IOTAF"), [[1, VA]], 32)
    iota(R("NBA", 1024, WE), [[1, CAP]], 1024)
    if sum(NFW):
        act(R("Y1"), R("XAB"), F.Copy, scale=4096.0)
        vtt(R("PK"), R("Y1"), R("NBA", 0, VA), O.add)
    act(R("IDF"), R("ID"), F.Copy)
    asel(R("GI"), one, [[-1, 8], [0, 16]], O.is_equal, 0, 1)
    vms(R("NGC"), -2 * BIG)
    asel(R("NEG"), R("NGC"), [[0, 8], [-1, 9]], O.not_equal, 0, 1, float(ZC))
    vms(R("NEG", 8, 72, 9), 0.0)
    asel(R("CM"), R("ONE"), [[-16, 8], [0, 8], [-1, 16]], O.is_equal, 0, 1)

    vms(R("FX", S0, VA), 0.0)
    act(R("FX", VA + GH, WE), R("ONE", 0, CAP), F.Copy, scale=0.0)
    vts(R("MB"), R("F0I"), 2559, None, O.is_lt)
    act(R("FA"), R("F0I"), F.Copy, bias=float(OFF))
    vtt(R("FX", 0, S0), R("FA"), R("MB"), O.mult)
    act(R("BDU"), R("BDI"), F.Copy)
    for h in range(2):
        vms(R("EH", 1024 * h, 1024 * h + 1024), 0.0)
    for q in range(16):
        copy("VA"[q // 8], R("EH", 128 * q + q, 128 * q + 128, 16), R("ID", q, 128, 16))
    act(R("SEL"), R("BD", 0, 128, 16), F.Copy, scale=4096.0)
    for x, c in (("IN1", -1.0), ("IN2", -2.0)):
        act(R(x), R("ID"), F.Copy, scale=c)
    asel(R("TRIY"), R("SLM"), [[-1, 128]], O.not_equal, 0, 1, 2047.0)
    vtt(R("TRIX"), R("BD"), R("TRIY"), O.subtract)
    act(R("HS"), R("ONE", 0, 512), F.Copy, scale=0.0)
    for h in range(2):
        for e in range(2):
            for a in range(4):
                c = 128 * (2 * h + e) + 32 * a + 16 * e
                act(R("HS", c, c + 16), R("ID", 32 * a + 16 * h, 32 * a + 16 * h + 16), F.Copy)
    vms(R("O16"), 1.0 / 16.0)
    vms(R("ONE40"), 1.0)
    vms(R("THR", 0, 1), 1544.0)
    vms(R("C2"), 2.0)
    vms(R("TT", CAP, 256), 0.0)
    act(R("XA", 1024, WE), R("ONE", 0, CAP), F.Copy, scale=0.0)
    act(R("XA", 0, VA), R("XAB"), F.Copy)
    act(R("FL0", 0, VA), R("ONE", 0, VA), F.Silu, scale=10.0)
    iota(R("FL1", 0, VA), [[0, VA]], 10)
    iota(R("LF", S0, VA), [[0, VA - S0]], 8000)
    iota(R("FL2", 0, VA), [[0, VA]], 0)
    for k in range(NC):
        u, r = 768 * k, 256 * k
        for a in range(u, u + 768, 256):
            act(R("UM", a, a + 256), R("ONE", 0, 256), F.Copy, scale=BIG)
            act(R("DM", a, a + 256), R("ONE", 0, 256), F.Copy, scale=-BIG)
        vms(R("UM", u + 2, u + 768, 6), -BIG)
        vms(R("UM", u, u + 768, 96), -BIG)
        vms(R("UM", u + 1, u + 768, 96), -BIG)
        vms(R("UR", r, r + 256), BIG)
        vms(R("UR", r + 31, r + 256, 32), -BIG)

    def ghosts_in(w):
        if w == 0:
            arrive("ag", FLY + 1.5)
            vcp(R("FX", VA, VA + GH), R("LG", 0, GH))
            return
        for k in range(NC):
            s, n = slot(w - 1, k), CH[k][1]
            arrive("ag%d%d" % (w - 1, k), FLY - 0.5)
            vcp(IX(R("FX"), R("LG", s, s + n // 16)), R("LG", s + 8, s + 8 + n))

    vts(R("GHS", 0, GH), IX(R("FX", 0, VA), R("BDU")), float(OB + 8), -float(OB), O.max, O.add)
    vts(R("NBX"), R("NB", OFF, EXT), OB, 2559, O.add, O.min)
    for x in START:
        remote(by_sem[x])
    iota(R("INV"), [[1, WE]], WE - 1024)
    iota(R("GK"), [[1, GH]], VA - 1024)
    vcp(IX(R("INV"), R("BDU")), R("GK"))
    vms(R("GHS", slot(0, NC - 1) + 7, slot(RO - 1, 0), 136 * NC), 0)
    for i in range(2):
        arrive("ax%d" % i, FLY + 3.0)
    for i in range(2):
        arrive("an%d" % i, FLY + 3.0)

    def front(w):
        p = str(w % 2)
        AW = R("AW" + p, 0, 15)
        el = R(PF, 0, 40)
        part[0] = "f"
        iota(R("LW", 0, CAP), [[1, CAP]], 1024 + 32)
        if w == 0:
            m = S0 // 16
            mm([(R(PF, 200, 200 + S0), R("BD"), R("MB"), True, True)])
            act(R("LFH", 0, S0), R(PF, 200, 200 + S0), F.Copy)
            act(R("LF", 0, S0), R(PF, 200, 200 + S0), F.Relu, scale=-8000.0, bias=8000.0)
            mm([(R(PF, 0, m), blk("EH", q), R("LFH", q, S0, 16), q == 0, q == 15) for q in range(16)])
            vms(R("EL", m, 40), 1.0)
            vts(R("EL", 0, m), R(PF, 0, m), 0.0, None, O.is_equal)
        else:
            copy("G", R("LFH"), R("LF", 0, VA))
            mm([(el, blk("EH", q), R("LFH", q, VA, 16), q == 0, False) for q in range(16)])
            for i in (1, 0):
                copy(WHO["FH"][i], R("FH%d" % i), R("FL%d" % i, 0, VA))
                mm([(el, blk("EH", q), R("FH%d" % i, q, VA, 16), False, i == 0 and q == 15 and not sum(MV)) for q in range(16)])
            if sum(MV):
                mm([(el, blk("EH", q), R("FL2", q, VA, 16), False, q == 15) for q in range(16)])
            vts(R("EL"), el, 8000.0, None, O.is_ge)
        mm([(R(PF, 40, 120, 2), R("TRIX"), R("EL"), True, True), (R(PF, 41, 120, 2), R("TRIY"), R("EL"), True, True)])
        scan(R("CUM"), R("ONE40"), R(PF, 40, 120), 2046.0, O.mult, O.add)
        vtt(R("POU"), R("CUM", 0, 80, 2), R("DUMPA"), O.min)
        if NFW[w]:
            iota(R("NFW", 0, CAP), [[1, CAP]], 1024)
            vcp(IX(R("NFW"), R("POU")), R("PK"))
            vts(R("NFI"), R("NFW", 0, CAP), 4095, None, O.bitwise_and)
            vcp(R("NFU"), R("NFI"))
            vts(R("XFN" + p), R("NFW", 0, CAP), -1.0 / 4096, R("THR", w, w + 1), O.mult, O.add)
        act(IX(R("LW"), R("POU")), R("IOTAF"), F.Silu)
        act(R("LWH"), R("LW", 0, CAP), F.Copy, bias=-32.0)
        mm([(R(PF, 120, 135), blk("EH", q), R("LWH", q, CAP, 16), q == 0, q == 15) for q in range(16)])
        places(WHO["AW"], AW, R(PF, 120, 135), 0.0)
        if not NFW[w]:
            copy(WHO["NFU"], R("NFU"), IX(R("NBA"), AW))
            act(R("XFN" + p), IX(XA, AW), F.Identity, scale=-1.0, bias=R("THR", w, w + 1))
        for c0, n, e in XRQ:
            for q in range(16):
                copy(e[q % len(e)], R("XR" + p, 16 * c0 + q, 16 * (c0 + n), 16), R("XFN" + p, c0, c0 + n))
        if w < RO - 1:
            mark_tables()
            act(R("GR"), IX(R("INV"), AW), F.Copy)
            mm([(R(PF, 140, 155), blk("EH", q), R("GR", q, CAP, 16), q == 0, q == 15) for q in range(16)])
            for k in range(NC):
                c0, n = CH[k]
                places(WHO["GW"], R("GHS", slot(w, k), slot(w, k) + n // 16), R(PF, 140 + c0 // 16, 140 + (c0 + n) // 16), 1024.0)
            iota(R("CMK"), [[0, 128]], 40 * 4 ** w)

    def pieces(k, t):
        c0, n = CH[k]
        cut = [c0] + [x for x in CUTS[t] if c0 < x < c0 + n] + [c0 + n]
        return [(a, b - a) for a, b in zip(cut, cut[1:])]

    turns = [0]

    def turn(k, z):
        n = CH[k][1]
        mm([(R(PD[k], 128, 256, 1, n), z, R("ID"), True, True)])
        act(blk("IDT", k, n), R(PD[k], 128, 256, 1, n), F.Copy)

    def test(w, k, t):
        p = str(w % 2)
        c0, n = CH[k]
        m, u, r = n // 16, 768 * k, 256 * k
        part[0] = "t%d%d" % (t, k)
        c = R(PC[k], 384, 512, 1, n)
        cut = c0 + n - ALT[w == RO - 1][t][k]
        for a, b in pieces(k, t):
            b = min(a + b, cut)
            if a < b:
                vtt(R("Q", 16 * a, 16 * b), IX(ZB, R("OFS", a, b)), R("XR" + p, 16 * a, 16 * b), O.add)
        for a in range(cut, c0 + n, 32):
            b, i = min(a + 32, c0 + n), turns[0] % 2
            turns[0] += 1
            gb, pa = R("GB", 512 * i, 512 * i + 16 * (b - a)), R(PA[i], 0, 16 * (b - a))
            act(gb, IX(ZB, R("OFS", a, b)), F.Copy)
            mm([(pa, R("ID"), R("XR" + p, 16 * a, 16 * b), True, False), (pa, R("ID"), gb, False, True)])
            act(R("Q", 16 * a, 16 * b), pa, F.Copy)
        cut = [c0] + [x for x in NRC[t] if c0 < x < c0 + n] + [c0 + n]
        for a, b in zip(cut, cut[1:]):
            vts(R("NR", 16 * a, 16 * b), R("Q", 16 * a, 16 * b), R("THR", w, w + 1), 0.84375, O.is_equal, O.subtract)
        mm([(R(PC[k], 384 + q, 512, 16, n), by("NR", k, q), R("SEL"), True, True) for q in range(16)])
        minus = R("UM", u + 2 + t, u + 768, 6, n) if t else R("UR", r, r + 256, 2, n)
        if WHO["U"][NC * t + k] == "A":
            act(minus, c, F.Copy, scale=-1.0)
        else:
            vts(minus, c, -1.0, None, O.mult)
        vtt(R("DM", u + 2 + t, u + 768, 6, n), c, blk("IDT", k, n), O.min)
        if t == 2:
            scan(R("MG", u, u + 768, 1, n), R("UM", u, u + 768, 1, n), R("DM", u, u + 768, 1, n), -BIG)
            mm([(R(PD[k], 256, 256 + n), R("MG", u + 4, u + 768, 6, n), R("ID", 0, n, 1, n), True, True)])
            new, aw = R(PD[k], 256, 256 + n), R("AW" + p, c0 // 16, c0 // 16 + m)
            if w < RO - 1:
                vts(R("GHS", slot(w, k) + 8, slot(w, k) + 8 + n), new, 0.0, 8.0, O.max, O.add)
                remote(by_sem["ag%d%d" % (w, k)])
                act(ch("NI", k), new, F.Relu, bias=float(ZC))
                vcp(IX(FX, aw), ch("NI", k))
            else:
                act(ch("NI", k), new, F.Copy, bias=float(ZC - OFF))
                vts(ch("LFV", k), ch("NI", k), -10.0, 2559.0, O.mult, O.min)
                vtt(IX(R("YO"), aw), ch("NI", k), ch("LFV", k), O.max)
        if t:
            scan(R("S", r, r + 256, 1, n), R("UM", u + t - 1, u + 768, 3, n), R("DM", u + t - 1, u + 768, 3, n), -BIG)
            b = R("S", r + 31, r + 256, 32, n)
        else:
            back = (r - 1) if r else None
            scan(R("S", r + 255, back, -1, n), R("UR", r + 255, back, -1, n), R("DM", u + 767, (u - 1) if u else None, -3, n), -BIG)
            b = R("S", r, r + 256, 32, n)
        if t < 2:
            copy(WHO["B"], R("DM", u + t, u + 768, 96, n), b)
        x = nine(T.ps4[:, 8 * k:8 * k + m, :], k, 9 * m)
        mm([(x, R("GI", 0, 128, 1, 8), R("NEG", 0, 9 * m, 1, 8), True, False)] +
           [(nine(T.ps4[:, 8 * k + i, 0:8], k, 8), blk("CM", i, n), b, False, i == m - 1) for i in range(m)])
        ob = R("OBW", 16 * t + c0 // 16, 16 * t + c0 // 16 + m)
        tk("V", cost(x, None, 1.0), [x], [ob], lambda: V.tensor_reduce(ob["ap"], x["ap"], AxisListType.X, O.max))
        if t < 2:
            places(WHO["OFS"][t + 1], ch("OFS", k), IX(NB, ob), float(OFF))
            if WHO["ZN"][t] == "A":
                act(ch("ZN", k), IX(NB, ob), F.Copy, bias=float(OFF - ZC))
                turn(k, ch("ZN", k))
            else:
                copy("G", ch("ZF", k), ch("OFS", k))
                mm([(R(PD[k], 128, 256, 1, n), ch("ZF", k), R("IDF"), True, True)])
                act(blk("IDT", k, n), R(PD[k], 128, 256, 1, n), F.Copy, bias=-float(ZC))
        if t == 0:
            act(ch("NOH", k), IX(ZB, ob), F.Relu, acc=R("NFAIL", 4 * (w % 2) + k, 4 * (w % 2) + k + 1), bias=-999.0)

    def mark(w, k):
        c0, n = CH[k]
        nb, m, z = (n + 31) // 32, n // 16, 256 + c0
        vts(R("FAIL", 8 * k, 8 * k + m), R("OBW", c0 // 16, c0 // 16 + m), 0.0, 1024.0, O.is_equal, O.mult)
        vtt(R("FT", c0, c0 + 128), IX(R("FAIL", 8 * k, 8 * k + 8), R("REP")), R("FT0", c0, c0 + 128), O.add)
        for q in range(16):
            j = c0 + 2 * nb * q
            if q < MV[k]:
                vcp(IX(R("FL2"), R("FT", j, j + m)), R("CMK", 0, n))
            else:
                act(IX(R("FL%d" % (q % 2 if q < 15 or k < NC - 1 else 0)), R("FT", j, j + m)), R("CMK", 0, n), F.Silu)

    def mark_tables():
        copy(WHO["TT"], R("TT", 0, CAP), R("NFU"))
        tk("V", cost(R("TTT"), None, 0.5), [R("TT")], [R("TTT")], lambda: V.transpose(T.TTT[:], T.TT[:]))
        lst = []
        for c0, n in CH:
            nb = (n + 31) // 32
            for i in range(nb):
                for h in range(2):
                    for e in range(2):
                        j = c0 + 32 * i + 16 * e
                        lst.append((R(PM, c0 + 2 * i + h, c0 + 32 * nb, 2 * nb), blk("HS", 2 * h + e), R("TTT", j, j + 16), e == 0, e == 1))
        mm(lst)
        act(R("FT0"), R(PM, 0, 256), F.Copy)

    def wave(w):
        p = str(w % 2)
        last = w == RO - 1
        AW = R("AW" + p, 0, 15)
        part[0], part[1] = "w", w
        ghosts_in(w)
        if last:
            act(R("Y1"), R("FX", 0, VA), F.Copy, bias=-float(OFF))
            for i in range(2):
                a, b = 320 * i, 320 * i + 320
                act(R(PM, 0, 320), R("FX", a, b), F.Copy, scale=-1000.0, bias=2559.0)
                vtt(R("YO", a, b), R(PM, 0, 320), R("Y1", a, b), O.max)
            act(R("YA", 0, VA), R("XA", 0, VA), F.Copy)
        for c0, n, q in SEEDS:
            out, src = R("ST", 16 * c0, 16 * (c0 + n)), IX(FX, R("NFU", c0, c0 + n))
            if q == "A":
                act(out, src, F.Copy, bias=-float(ZC))
            else:
                vts(out, src, -float(ZC), None, O.add)
        for k in range(NC):
            for c0, n in pieces(k, 0):
                sd = R(PD[k], c0 - CH[k][0], c0 - CH[k][0] + n)
                mm([(sd, blk("EH", q), R("ST", 16 * c0 + q, 16 * (c0 + n), 16), q == 0, q == 15) for q in range(16)])
                places(WHO["OFS"][0], R("OFS", c0, c0 + n), sd, float(ZC))
            act(ch("ZN", k), R(PD[k], 0, CH[k][1]), F.Copy)
            turn(k, ch("ZN", k))
            test(w, k, 0)
            if not last:
                mark(w, k)
        if not last:
            act(R("LFV"), R("NOH"), F.Copy, scale=8000.0 - 35 * 4 ** w)
            if WHO["LF"] == "A":
                act(IX(LF, AW), R("LFV"), F.Silu)
            else:
                vcp(IX(LF, AW), R("LFV"))
            nf = 4 * (w % 2)
            mm([(R(PF, 500, 501), R("O16"), R("NFAIL", nf + k, nf + k + 1), k == 0, k == NC - 1) for k in range(NC)])
            vcp(ICOL["EI"], R(PF, 500, 501))
            vts(ICOL["EJ"], ICOL["EI"], 1, None, O.bitwise_and)
            vts(R("THR", w + 1, w + 2), ICOL["EJ"], -8.0, 1544.0, O.mult, O.add)
        hi, lo = R(PH, 0, CAP), R(PH, CAP, 2 * CAP)
        mm([(hi, R("IN1"), R("XFN" + p), True, False), (hi, R("IN2"), R("NOH"), False, False), (hi, R("ID"), R("C2"), False, True),
            (lo, R("IN1"), R("XFN" + p), True, False), (lo, R("IN1"), R("C2"), False, True)])
        act(R("HL"), R(PH, 0, 2 * CAP), F.Identity, bias=R("THR", w, w + 1))
        for t in (1, 2):
            for k in range(NC):
                test(w, k, t)
        if not last:
            front(w + 1)
            vtt(R("XT"), IX(ZB, R("OBW", 32, 47)), R("HL", 0, CAP), O.min)
            vtt(IX(XA, AW), R("XT"), R("HL", CAP, 2 * CAP), O.max)
            return
        for k in range(NC):
            c0, n = CH[k]
            vtt(ch("XT", k), IX(ZB, R("OBW", 32 + c0 // 16, 32 + (c0 + n) // 16)), R("HL", c0, c0 + n), O.min)
            vtt(ch("XN", k), ch("XT", k), R("HL", CAP + c0, CAP + c0 + n), O.max)
            vcp(IX(R("YA"), R("AW" + p, c0 // 16, (c0 + n) // 16)), ch("XN", k))

    front(0)
    for i in range(2):
        a, b = (0, NB_HALF) if i == 0 else (NB_HALF, OB - 1)
        copy("G", R("NB", EXT + a, EXT + b), R("LN", a, b))
    for w in range(RO):
        wave(w)
    tk("S", 0.1, [R("YO")], [TAG("yf")], lambda: SY.dma_start(T.yf[:], T.YO[:, 0:VA]), sem="oy", val=16)
    tk("A", 0.1, [R("YA")], [TAG("ya")], lambda: A.dma_start(T.ya[:], T.YA[:, 0:VA]), sem="ox", val=16)
    return tasks, sent


LAT = {"V": 0.12, "A": 0.15, "P": 0.15, "G": 0.2, None: 0.0}
EPS = (0.05, 0.1, 0.2, 0.3)
TURNS = 6
CASES = ((1.0, 1.0, 1.0, 0.7, 0.13), (0.9, 0.9, 0.9, 0.9, 0.2), (1.1, 0.8, 1.5, 1.1, 0.13), (1.1, 1.35, 0.6, 1.1, 0.13))
MOVES = 8000
WAW = True


def span(qs, dur, pred, order, wake):
    fin, why, last = [0.0] * len(qs), [-1] * len(qs), {}
    for i in order:
        t, w = 0.0, -1
        for d, gap in pred[i]:
            x = fin[d] + (gap if gap > 1 or gap == 0 else wake)
            if x > t:
                t, w = x, d
        q = qs[i]
        if q is not None:
            if q in last and fin[last[q]] >= t:
                t, w = fin[last[q]], -2 - last[q]
            last[q] = i
        fin[i], why[i] = t + dur[i], w
    return fin, why


def sweep(qs, dur, succ, prio, eps):
    n = len(qs)
    left = [0] * n
    for i in range(n):
        for j, gap in succ[i]:
            left[j] += 1
    est, fin, free, order, ready = [0.0] * n, [0.0] * n, {}, [], {}
    for i in range(n):
        if left[i] == 0:
            ready.setdefault(qs[i], []).append(i)
    while len(order) < n:
        best = None
        for q, lst in ready.items():
            if not lst:
                continue
            f = free.get(q, 0.0) if q is not None else 0.0
            t0 = max(f, min([est[i] for i in lst]))
            if best is None or t0 < best[0]:
                best = (t0, q)
        t0, q = best
        now = [i for i in ready[q] if est[i] <= t0 + eps]
        i = max(now, key=lambda i: prio[i])
        soon = [j for j in ready[q] if t0 + eps < est[j] < t0 + dur[i] and prio[j] > prio[i]]
        if soon and q is not None:
            j = max(soon, key=lambda j: prio[j])
            if max(est[j] + prio[j], est[j] + dur[j] + prio[i]) < max(t0 + prio[i], t0 + dur[i] + prio[j]) - eps:
                fit = [x for x in now if t0 + dur[x] <= est[j] + eps]
                i = max(fit, key=lambda x: prio[x]) if fit else j
        ready[q].remove(i)
        fin[i] = (est[i] if q is None else max(t0, est[i])) + dur[i]
        if q is not None:
            free[q] = fin[i]
        order.append(i)
        for j, gap in succ[i]:
            est[j] = max(est[j], fin[i] + gap)
            left[j] -= 1
            if left[j] == 0:
                ready.setdefault(qs[j], []).append(j)
    return order, fin


PLAN = []


def plan(tasks):
    if PLAN:
        return PLAN[0]
    n = len(tasks)
    qs, dur = [t["q"] for t in tasks], [t["dur"] for t in tasks]
    succ, pred = [[] for _ in range(n)], [[] for _ in range(n)]
    for i, t in enumerate(tasks):
        for d, hard in t["deps"].items():
            u = tasks[d]
            gap = LAT[u["q"]] if u["sem"] is None or u["q"] is None else 0.0 if u["sem"] == "none" else u["lat"]
            if not hard and u["q"] == t["q"] and u["sem"] is None:
                gap = 0.0
            succ[d].append((i, gap))
            pred[i].append((d, gap))
    way = [0.0] * n
    for i in range(n - 1, -1, -1):
        way[i] = dur[i] + max([way[j] + gap for j, gap in succ[i]] + [0.0])
    cases = [([d * x[t["kind"]] for d, t in zip(dur, tasks)], x[4]) for x in CASES]


    def tried(prio, eps):
        order, fin = sweep(qs, dur, succ, prio, eps)
        ends = [max(span(qs, d, pred, order, wake)[0]) for d, wake in cases]
        return order, fin, sum(ends) / len(ends), ends, prio, eps

    best = None
    for eps in EPS:
        prio = way
        for _ in range(TURNS):
            x = tried(prio, eps)
            if best is None or x[2] < best[2]:
                best = x
            prio = sweep(qs, dur, pred, x[1], eps)[1]
    best = (mend(qs, pred, cases, [t["key"] for t in tasks], best[0]),) + best[1:]
    PLAN.append(best)
    return best


def mend(qs, pred, cases, key, order):
    at = {k: i for i, k in enumerate(key)}
    needs = [set(d for d, gap in p) for p in pred]
    rng = np.random.RandomState(0)

    def ends(o):
        r = [span(qs, d, pred, o, wake) for d, wake in cases]
        return sum(max(x[0]) for x in r) / len(r), r

    cur, r = ends(order)
    best = (cur, order)
    for _ in range(MOVES):
        fin, why = r[rng.randint(len(r))]
        i, held = fin.index(max(fin)), []
        while i >= 0:
            if why[i] <= -2:
                held.append((-2 - why[i], i))
            i = -2 - why[i] if why[i] <= -2 else why[i]
        a, b = held[rng.randint(len(held))]
        line = [x for x in order if qs[x] == qs[a]]
        a = line[max(0, line.index(a) - rng.randint(3 if rng.rand() < 0.7 else 20))]
        o, up = list(order), rng.rand() < 0.5
        for s in (range(1 - RO, RO) if rng.rand() < 0.8 else (0,)):
            x, y = at.get((key[a][0] + s, key[a][1])), at.get((key[b][0] + s, key[b][1]))
            if x is None or y is None or o.index(x) > o.index(y):
                continue
            px, py = o.index(x), o.index(y) + 1
            seg = o[px:py]
            if up:
                need, m = set(needs[y]), {y}
                for z in seg[-2::-1]:
                    if z in need:
                        m.add(z)
                        need |= needs[z]
                if x not in m:
                    o[px:py] = [z for z in seg if z in m] + [z for z in seg if z not in m]
            else:
                m = {x}
                for z in seg[1:]:
                    if needs[z] & m:
                        m.add(z)
                if y not in m:
                    o[px:py] = [z for z in seg if z not in m] + [z for z in seg if z in m]
        if o != order:
            v, r2 = ends(o)
            if v < cur + 0.025 * rng.exponential():
                cur, r, order = v, r2, o
                if v < best[0]:
                    best = (v, o)
    return best[1]


def emit(g, T, tasks, order):
    queues = {"V": g.vector, "A": g.scalar, "P": g.tensor, "G": g, "S": g.sync}
    esem = {"V": "sV", "A": "sA", "P": "sP", "G": "sG"}
    cnt = {k: 0 for k in esem}
    known = {k: {} for k in queues}
    done, clock, final = [None] * len(tasks), [None] * len(tasks), {}
    for i in order:
        t = tasks[i]
        q = t["q"]
        if q is None:
            done[i] = (t["sem"], t["val"])
            clock[i] = {t["sem"]: t["val"]}
            final[t["sem"]] = t["val"]
            continue
        kn = known[q]
        need = [d for d, hard in t["deps"].items() if done[d] is not None and (hard or tasks[d]["q"] != q or tasks[d]["sem"] is not None)]
        need.sort(key=lambda d: -done[d][1])
        for d in need:
            s, v = done[d]
            if kn.get(s, 0) < v:
                queues[q].wait_ge(T.sem[s], v)
            for a, b in clock[d].items():
                if kn.get(a, 0) < b:
                    kn[a] = b
        x = t["fn"]()
        if t["sem"] == "none":
            continue
        if t["sem"] is not None:
            x.then_inc(T.sem[t["sem"]], 16)
            done[i] = (t["sem"], 16)
        else:
            cnt[q] += 1
            x.then_inc(T.sem[esem[q]], 1)
            done[i] = (esem[q], cnt[q])
        clock[i] = dict(kn)
        clock[i][done[i][0]] = done[i][1]
        final[done[i][0]] = max(final.get(done[i][0], 0), done[i][1])
    return final


def rank_program(g, core, T, topo):
    msgs = messages(topo, T.cores)
    if T.rank_of(core) is None:
        relay_program(g, core, T, topo, msgs)
        return
    tasks, sent = build(g, core, T, topo, msgs)
    order = plan(tasks)[0]
    final = emit(g, T, tasks, order)
    for s, v in final.items():
        g.wait_ge(T.sem[s], v)
    g.wait_ge(T.sem["ls"], sent[0])
